import numpy as np
import ml_dtypes


def mxq(x, axis, fmt="e4m3"):
    dtype, down = {"e4m3": (ml_dtypes.float8_e4m3fn, 7), "e5m2": (ml_dtypes.float8_e5m2, 14)}[fmt]
    v = np.moveaxis(np.asarray(x, np.float32).astype(ml_dtypes.bfloat16).astype(np.float64), axis, -1)
    blocks = v.reshape(v.shape[:-1] + (-1, 32))
    amax = np.abs(blocks).max(-1, keepdims=True)
    byte = np.maximum(np.where(amax > 0, np.frexp(amax)[1] - 1 + 127, 0) - down, 1)
    scale = np.exp2(byte - 127.0)
    codes = (blocks / scale).astype(np.float32).astype(dtype).astype(np.float64)
    return np.moveaxis((codes * scale).reshape(v.shape), -1, axis)


WIDE = False


def mx_kscale(k):
    if not WIDE:
        return np.ones(k)
    levels = np.array([10, -10, 5, -5, 0])
    if k % 512:
        return np.exp2(np.random.permutation(np.resize(levels, k // 32))).repeat(32)
    a = np.empty((k // 512, 16))
    for p in range(k // 512):
        a[p, :8] = np.random.permutation(np.resize(levels, 8))
        for g in range(8):
            far = levels[np.abs(levels - a[p, g]) >= 10]
            a[p, g + 8] = far[np.random.randint(len(far))]
    return np.exp2(a.ravel()).repeat(32)


def f64(x):
    return np.asarray(x).astype(np.float64)


def striped(idx):
    return np.tile(idx.reshape(-1, 16).T, (8, 1)).astype(np.uint16)


def unstriped(offs):
    return offs[:16].T.reshape(-1).astype(np.int64)


def gelu(v):
    return 0.5 * v * (1.0 + np.tanh(np.sqrt(2.0 / np.pi) * (v + 0.044715 * v**3)))


K, T, H, N = 1024, 128, 512, 256


def setup_inputs():
    n = np.random.standard_normal
    s = mx_kscale(K)[:, None]
    u = mx_kscale(H)
    idx = np.random.permutation(H)
    v = np.empty(H)
    v[idx] = u
    return {
        "xT": (n((K, T)) * s).astype(np.float32),
        "w1": (n((K, H)) / np.sqrt(K) / s * v).astype(np.float32),
        "w2": (n((H, N)) / np.sqrt(H) / u[:, None]).astype(np.float32),
        "offs": striped(idx),
    }


def reference(xT, w1, w2, offs):
    idx = unstriped(offs)
    h = gelu(mxq(f64(w1), 0, "e4m3").T @ mxq(f64(xT), 0, "e4m3"))
    return mxq(f64(w2), 0, "e4m3").T @ mxq(h[idx], 0, "e4m3")

@@ -1,0 +1,185 @@
+from contextlib import ExitStack
+
+import concourse.mybir as mybir
+from concourse.masks import make_identity
+
+K, T, H, N = 1024, 128, 512, 256
+FLOPS = 2 * K * T * H + 2 * H * T * N
+
+F32 = mybir.dt.float32
+BF16 = mybir.dt.bfloat16
+U32 = mybir.dt.uint32
+U16 = mybir.dt.uint16
+U8 = mybir.dt.uint8
+FP8X4 = mybir.dt.float8_e4m3fn_x4
+GELU = mybir.ActivationFunctionType.Gelu_apprx_tanh
+COPY = mybir.ActivationFunctionType.Copy
+
+P = 128
+PACK = 4
+KP = 512
+
+PIECES = ((0, 256), (256, 128), (384, 128))
+
+def tile_picked_shuffle_mlp_gelu_perm_l_kernel(tc, xT, w1, w2, offs, out):
+    nc = tc.nc
+
+    def vcopy(dst, src):
+        nc.vector.tensor_copy(out=dst, in_=src)
+
+    def scopy(dst, src):
+        nc.scalar.copy(dst, src)
+
+    def interleave(copy, dst, raw, c0, c1):
+        copy(
+            dst[:, PACK * c0 : PACK * c1].rearrange("p (c i j) -> p c j i", i=4, j=PACK),
+            raw[:, :, c0:c1].rearrange("p j (c i) -> p c j i", i=4),
+        )
+
+    def quantize(codes, scales, grouped):
+        nc.vector.quantize_mx(out=codes.bitcast(FP8X4), scales=scales, in_=grouped)
+
+    with ExitStack() as ctx:
+        keep = ctx.enter_context(tc.tile_pool(name="keep", bufs=1))
+        psum = ctx.enter_context(tc.psum_pool(name="psum", bufs=1))
+
+        offsets = keep.tile([P, H // 16], U16, name="offsets")
+        x_raw = keep.tile([P, 2, PACK, T], F32, name="x_raw")
+        w1_raw0 = []
+        for c0 in (0, 256):
+            raw = keep.tile([P, PACK, 256], F32, name="w1_raw0_%d" % c0)
+            w1_raw0.append(raw)
+        w1_raw1 = []
+        for c0, width in PIECES:
+            raw = keep.tile([P, PACK, width], F32, name="w1_raw1_%d" % c0, tag="h" if c0 == 384 else "w1_raw1_%d" % c0, align_bytes=64)
+            w1_raw1.append(raw)
+        w2_raw = keep.tile([P, PACK, N], F32, name="w2_raw")
+
+        w1_lo = w1[0:KP, :].rearrange("(p j) c -> p j c", j=PACK)
+        nc.sync.dma_start(out=x_raw[:, 0], in_=xT[0:KP, :].rearrange("(p j) t -> p j t", j=PACK))
+        nc.sync.dma_start(out=w1_raw0[0][:], in_=w1_lo[:, :, 0:256])
+        nc.sync.dma_start(out=w1_raw0[1][:], in_=w1_lo[:, :, 256:512])
+        nc.sync.dma_start(out=x_raw[:, 1], in_=xT[KP:K, :].rearrange("(p j) t -> p j t", j=PACK))
+        w1_hi = w1[KP:K, :].rearrange("(p j) c -> p j c", j=PACK)
+        for raw, (c0, width) in zip(w1_raw1, PIECES):
+            nc.sync.dma_start(out=raw[:], in_=w1_hi[:, :, c0 : c0 + width])
+        nc.sync.dma_start(offsets[:], offs)
+        nc.sync.dma_start(out=w2_raw[:], in_=w2.rearrange("(p j) m -> p j m", j=PACK))
+
+        warm = keep.tile([P, 1], F32, name="warm")
+        warm_out = keep.tile([P, 1], F32, name="warm_out")
+        nc.vector.memset(warm[:], 0.0)
+        nc.scalar.activation(warm_out[:], warm[:], GELU)
+
+        ident = keep.tile([P, P], F32, name="ident")
+        make_identity(nc, ident[:])
+
+        x_bf = keep.tile([P, 2 * T * PACK], BF16, name="x_bf", align_bytes=64)
+        x_codes = keep.tile([P, 2 * T], U32, name="x_codes", align_bytes=64)
+        x_scales = keep.tile([P, 2 * T], U8, name="x_scales", align_bytes=64)
+        w1_bf = keep.tile([P, 2, H * PACK], BF16, name="w1_bf", align_bytes=64)
+        w1_codes = keep.tile([P, 2, H], U32, name="w1_codes", align_bytes=64)
+        w1_scales = keep.tile([P, 2, H], U8, name="w1_scales", align_bytes=64)
+
+        def quantize_x(g):
+            cols = slice(g * T, (g + 1) * T)
+            quantize(x_codes[:, cols], x_scales[:, cols], x_bf[:, PACK * g * T : PACK * (g + 1) * T])
+
+        acc = []
+        for c0, width in PIECES:
+            bank = psum.tile([P, 512], F32, name="acc%d" % c0)
+            acc.append(bank)
+
+        def pass_k(g, index):
+            c0, width = PIECES[index]
+            nc.tensor.matmul_mx(
+                out=acc[index][:, 0:width],
+                lhsT=x_codes[:, g * T : (g + 1) * T].bitcast(FP8X4),
+                lhsT_scale=x_scales[:, g * T : (g + 1) * T],
+                rhs=w1_codes[:, g, c0 : c0 + width].bitcast(FP8X4),
+                rhs_scale=w1_scales[:, g, c0 : c0 + width],
+                start=(g == 0),
+                stop=(g == 1),
+            )
+
+        def gelu(index):
+            c0, width = PIECES[index]
+            cols = slice(c0, c0 + width)
+            nc.scalar.activation(h[:, cols], acc[index][:, 0:width], GELU)
+            if index == 2:
+                nc.scalar.activation(hb[:, cols], acc[index][:, 0:width], GELU)
+            else:
+                vcopy(hb[:, cols], h[:, cols])
+
+        def interleave_x(g, split):
+            dst = x_bf[:, PACK * g * T : PACK * (g + 1) * T]
+            interleave(vcopy, dst, x_raw[:, g], 0, split)
+            interleave(scopy, dst, x_raw[:, g], split, T)
+
+        def interleave_w1(g, c0, width, raw, split):
+            dst = w1_bf[:, g, PACK * c0 : PACK * (c0 + width)]
+            interleave(vcopy, dst, raw, 0, split)
+            interleave(scopy, dst, raw, split, width)
+
+        def quantize_w1(g, c0, width):
+            cols = slice(c0, c0 + width)
+            quantize(w1_codes[:, g, cols], w1_scales[:, g, cols], w1_bf[:, g, PACK * c0 : PACK * (c0 + width)])
+
+        interleave_x(0, 80)
+        quantize_x(0)
+        interleave_w1(0, 0, 256, w1_raw0[0], 176)
+        quantize_w1(0, 0, 256)
+        interleave_w1(0, 256, 256, w1_raw0[1], 176)
+        pass_k(0, 0)
+        quantize_w1(0, 256, 256)
+        interleave_x(1, 80)
+        quantize_x(1)
+        pass_k(0, 1)
+        pass_k(0, 2)
+        for index, split in enumerate((176, 80, 76)):
+            c0, width = PIECES[index]
+            interleave_w1(1, c0, width, w1_raw1[index], split)
+            quantize_w1(1, c0, width)
+            pass_k(1, index)
+        h = keep.tile([P, H], F32, name="h", tag="h", align_bytes=64)
+        hb = keep.tile([P, H], BF16, name="hb", align_bytes=64)
+        for index in range(3):
+            gelu(index)
+
+        g_bf = keep.tile([P, H], BF16, name="g_bf", align_bytes=64)
+        g_view = g_bf[:].rearrange("q (u p e) -> q p u e", u=2, e=2)
+        nc.vector.tensor_copy(out=g_view[:, 0 : 4 * 18], in_=h[:].indirect(offsets[:, 0:18]))
+        nc.scalar.activation(g_view[:, 4 * 18 : P], hb[:].indirect(offsets[:, 18:32]), COPY)
+
+        w2_bf = keep.tile([P, N * PACK], BF16, name="w2_bf", tag="h", align_bytes=64)
+        w2_codes = keep.tile([P, N], U32, name="w2_codes", align_bytes=64)
+        w2_scales = keep.tile([P, N], U8, name="w2_scales", align_bytes=64)
+        interleave(vcopy, w2_bf[:], w2_raw, 0, 192)
+        interleave(scopy, w2_bf[:], w2_raw, 192, N)
+        quantize(w2_codes[:], w2_scales[:], w2_bf[:])
+
+        words = g_bf[:].bitcast(F32)
+        turned = psum.tile([P, 2, P], F32, name="turned")
+        for u in range(2):
+            nc.tensor.transpose(turned[:, u, :], words[:, 128 * u : 128 * (u + 1)], ident[:])
+        h_bf = keep.tile([P, T * PACK], BF16, name="h_bf", align_bytes=64)
+        nc.scalar.copy(h_bf[:].bitcast(F32).rearrange("p (t u) -> p t u", u=2), turned[:].rearrange("p u t -> p t u"))
+        h_codes = keep.tile([P, T], U32, name="h_codes", align_bytes=64)
+        h_scales = keep.tile([P, T], U8, name="h_scales", align_bytes=64)
+        quantize(h_codes[:], h_scales[:], h_bf[:])
+
+        for m, copy, dma in ((0, vcopy, nc.sync), (1, scopy, nc.scalar)):
+            bank = psum.tile([P, 512], F32, name="out_bank%d" % m)
+            cols = slice(P * m, P * (m + 1))
+            nc.tensor.matmul_mx(
+                out=bank[:, 0:T],
+                lhsT=w2_codes[:, cols].bitcast(FP8X4),
+                lhsT_scale=w2_scales[:, cols],
+                rhs=h_codes[:].bitcast(FP8X4),
+                rhs_scale=h_scales[:],
+                start=True,
+                stop=True,
+            )
+            y = keep.tile([P, T], F32, name="y%d" % m)
+            copy(y[:], bank[:, 0:T])
+            dma.dma_start(out=out[cols, :], in_=y[:])

@@ -105,11 +105,7 @@ def tile_picked_shuffle_mlp_gelu_perm_l_kernel(tc, xT, w1, w2, offs, out):
         def gelu(index):
             c0, width = PIECES[index]
             cols = slice(c0, c0 + width)
-            nc.scalar.activation(h[:, cols], acc[index][:, 0:width], GELU)
-            if index == 2:
-                nc.scalar.activation(hb[:, cols], acc[index][:, 0:width], GELU)
-            else:
-                vcopy(hb[:, cols], h[:, cols])
+            nc.scalar.activation(hb[:, cols], acc[index][:, 0:width], GELU)
 
         def interleave_x(g, split):
             dst = x_bf[:, PACK * g * T : PACK * (g + 1) * T]
@@ -141,15 +137,13 @@ def tile_picked_shuffle_mlp_gelu_perm_l_kernel(tc, xT, w1, w2, offs, out):
             interleave_w1(1, c0, width, w1_raw1[index], split)
             quantize_w1(1, c0, width)
             pass_k(1, index)
-        h = keep.tile([P, H], F32, name="h", tag="h", align_bytes=64)
-        hb = keep.tile([P, H], BF16, name="hb", align_bytes=64)
+        hb = keep.tile([P, H], BF16, name="hb", tag="h", align_bytes=64)
         for index in range(3):
             gelu(index)
 
         g_bf = keep.tile([P, H], BF16, name="g_bf", align_bytes=64)
-        g_view = g_bf[:].rearrange("q (u p e) -> q p u e", u=2, e=2)
-        nc.vector.tensor_copy(out=g_view[:, 0 : 4 * 18], in_=h[:].indirect(offsets[:, 0:18]))
-        nc.scalar.activation(g_view[:, 4 * 18 : P], hb[:].indirect(offsets[:, 18:32]), COPY)
+        nc.vector.tensor_copy(out=g_bf[:, 0 : 16 * 18], in_=hb[:].indirect(offsets[:, 0:18]))
+        nc.scalar.activation(g_bf[:, 16 * 18 : H], hb[:].indirect(offsets[:, 18:32]), COPY)
 
         w2_bf = keep.tile([P, N * PACK], BF16, name="w2_bf", tag="h", align_bytes=64)
         w2_codes = keep.tile([P, N], U32, name="w2_codes", align_bytes=64)
@@ -161,7 +155,7 @@ def tile_picked_shuffle_mlp_gelu_perm_l_kernel(tc, xT, w1, w2, offs, out):
         words = g_bf[:].bitcast(F32)
         turned = psum.tile([P, 2, P], F32, name="turned")
         for u in range(2):
-            nc.tensor.transpose(turned[:, u, :], words[:, 128 * u : 128 * (u + 1)], ident[:])
+            nc.tensor.transpose(turned[:, u, :], words[:, u : 2 * P : 2], ident[:])
         h_bf = keep.tile([P, T * PACK], BF16, name="h_bf", align_bytes=64)
         nc.scalar.copy(h_bf[:].bitcast(F32).rearrange("p (t u) -> p t u", u=2), turned[:].rearrange("p u t -> p t u"))
         h_codes = keep.tile([P, T], U32, name="h_codes", align_bytes=64)

@@ -21,6 +21,7 @@ KP = 512
 
 PIECES = ((0, 256), (256, 128), (384, 128))
 
+
 def tile_picked_shuffle_mlp_gelu_perm_l_kernel(tc, xT, w1, w2, offs, out):
     nc = tc.nc
 
@@ -36,6 +37,12 @@ def tile_picked_shuffle_mlp_gelu_perm_l_kernel(tc, xT, w1, w2, offs, out):
             raw[:, :, c0:c1].rearrange("p j (c i) -> p c j i", i=4),
         )
 
+    def shared_interleave(dst, raw, split, width):
+        if split > 0:
+            interleave(vcopy, dst, raw, 0, split)
+        if split < width:
+            interleave(scopy, dst, raw, split, width)
+
     def quantize(codes, scales, grouped):
         nc.vector.quantize_mx(out=codes.bitcast(FP8X4), scales=scales, in_=grouped)
 
@@ -44,27 +51,27 @@ def tile_picked_shuffle_mlp_gelu_perm_l_kernel(tc, xT, w1, w2, offs, out):
         psum = ctx.enter_context(tc.psum_pool(name="psum", bufs=1))
 
         offsets = keep.tile([P, H // 16], U16, name="offsets")
-        x_raw = keep.tile([P, 2, PACK, T], F32, name="x_raw")
-        w1_raw0 = []
-        for c0 in (0, 256):
-            raw = keep.tile([P, PACK, 256], F32, name="w1_raw0_%d" % c0)
-            w1_raw0.append(raw)
-        w1_raw1 = []
-        for c0, width in PIECES:
-            raw = keep.tile([P, PACK, width], F32, name="w1_raw1_%d" % c0, tag="h" if c0 == 384 else "w1_raw1_%d" % c0, align_bytes=64)
-            w1_raw1.append(raw)
-        w2_raw = keep.tile([P, PACK, N], F32, name="w2_raw")
+        x_raw = [keep.tile([P, PACK, T], F32, name="x_raw%d" % g) for g in range(2)]
+        w1_raw0 = [keep.tile([P, PACK, 256], F32, name="w1_raw0_%d" % c0) for c0 in (0, 256)]
+        w1_raw1 = [
+            keep.tile([P, PACK, width], F32, name="w1_raw1_%d" % c0, tag="h" if c0 == 384 else "w1_raw1_%d" % c0, align_bytes=64)
+            for c0, width in PIECES
+        ]
+        w2_raw = [keep.tile([P, PACK, P], F32, name="w2_raw%d" % m) for m in range(2)]
 
         w1_lo = w1[0:KP, :].rearrange("(p j) c -> p j c", j=PACK)
-        nc.sync.dma_start(out=x_raw[:, 0], in_=xT[0:KP, :].rearrange("(p j) t -> p j t", j=PACK))
+        w1_hi = w1[KP:K, :].rearrange("(p j) c -> p j c", j=PACK)
+        w2_rows = w2.rearrange("(p j) m -> p j m", j=PACK)
+        nc.sync.dma_start(out=x_raw[0][:], in_=xT[0:KP, :].rearrange("(p j) t -> p j t", j=PACK))
         nc.sync.dma_start(out=w1_raw0[0][:], in_=w1_lo[:, :, 0:256])
         nc.sync.dma_start(out=w1_raw0[1][:], in_=w1_lo[:, :, 256:512])
-        nc.sync.dma_start(out=x_raw[:, 1], in_=xT[KP:K, :].rearrange("(p j) t -> p j t", j=PACK))
-        w1_hi = w1[KP:K, :].rearrange("(p j) c -> p j c", j=PACK)
-        for raw, (c0, width) in zip(w1_raw1, PIECES):
-            nc.sync.dma_start(out=raw[:], in_=w1_hi[:, :, c0 : c0 + width])
+        nc.sync.dma_start(out=x_raw[1][:], in_=xT[KP:K, :].rearrange("(p j) t -> p j t", j=PACK))
+        nc.sync.dma_start(out=w1_raw1[0][:], in_=w1_hi[:, :, 0:256])
+        nc.sync.dma_start(out=w1_raw1[1][:], in_=w1_hi[:, :, 256:384])
+        nc.sync.dma_start(out=w1_raw1[2][:], in_=w1_hi[:, :, 384:512])
+        nc.sync.dma_start(out=w2_raw[0][:], in_=w2_rows[:, :, 0:P])
         nc.sync.dma_start(offsets[:], offs)
-        nc.sync.dma_start(out=w2_raw[:], in_=w2.rearrange("(p j) m -> p j m", j=PACK))
+        nc.sync.dma_start(out=w2_raw[1][:], in_=w2_rows[:, :, P:N])
 
         warm = keep.tile([P, 1], F32, name="warm")
         warm_out = keep.tile([P, 1], F32, name="warm_out")
@@ -77,18 +84,15 @@ def tile_picked_shuffle_mlp_gelu_perm_l_kernel(tc, xT, w1, w2, offs, out):
         x_bf = keep.tile([P, 2 * T * PACK], BF16, name="x_bf", align_bytes=64)
         x_codes = keep.tile([P, 2 * T], U32, name="x_codes", align_bytes=64)
         x_scales = keep.tile([P, 2 * T], U8, name="x_scales", align_bytes=64)
-        w1_bf = keep.tile([P, 2, H * PACK], BF16, name="w1_bf", align_bytes=64)
+        w1_bf0 = keep.tile([P, H * PACK], BF16, name="w1_bf0", align_bytes=64)
+        w1_bf1 = [
+            keep.tile([P, width * PACK], BF16, name="w1_bf1_%d" % c0, tag="last" if c0 == 384 else "w1_bf1_%d" % c0, align_bytes=64)
+            for c0, width in PIECES
+        ]
         w1_codes = keep.tile([P, 2, H], U32, name="w1_codes", align_bytes=64)
         w1_scales = keep.tile([P, 2, H], U8, name="w1_scales", align_bytes=64)
 
-        def quantize_x(g):
-            cols = slice(g * T, (g + 1) * T)
-            quantize(x_codes[:, cols], x_scales[:, cols], x_bf[:, PACK * g * T : PACK * (g + 1) * T])
-
-        acc = []
-        for c0, width in PIECES:
-            bank = psum.tile([P, 512], F32, name="acc%d" % c0)
-            acc.append(bank)
+        acc = [psum.tile([P, 512], F32, name="acc%d" % c0) for c0, width in PIECES]
 
         def pass_k(g, index):
             c0, width = PIECES[index]
@@ -102,55 +106,61 @@ def tile_picked_shuffle_mlp_gelu_perm_l_kernel(tc, xT, w1, w2, offs, out):
                 stop=(g == 1),
             )
 
-        def gelu(index):
+        def prepare_x(g):
+            cols = slice(g * T, (g + 1) * T)
+            dst = x_bf[:, PACK * g * T : PACK * (g + 1) * T]
+            shared_interleave(dst, x_raw[g], 80, T)
+            quantize(x_codes[:, cols], x_scales[:, cols], dst)
+
+        def prepare_w1_lo(index):
+            cols = slice(256 * index, 256 * (index + 1))
+            dst = w1_bf0[:, PACK * cols.start : PACK * cols.stop]
+            shared_interleave(dst, w1_raw0[index], 176, 256)
+            quantize(w1_codes[:, 0, cols], w1_scales[:, 0, cols], dst)
+
+        def interleave_w1_hi(index, split):
+            shared_interleave(w1_bf1[index][:], w1_raw1[index], split, PIECES[index][1])
+
+        def quantize_w1_hi(index):
             c0, width = PIECES[index]
             cols = slice(c0, c0 + width)
-            nc.scalar.activation(hb[:, cols], acc[index][:, 0:width], GELU)
+            quantize(w1_codes[:, 1, cols], w1_scales[:, 1, cols], w1_bf1[index][:])
+            pass_k(1, index)
 
-        def interleave_x(g, split):
-            dst = x_bf[:, PACK * g * T : PACK * (g + 1) * T]
-            interleave(vcopy, dst, x_raw[:, g], 0, split)
-            interleave(scopy, dst, x_raw[:, g], split, T)
-
-        def interleave_w1(g, c0, width, raw, split):
-            dst = w1_bf[:, g, PACK * c0 : PACK * (c0 + width)]
-            interleave(vcopy, dst, raw, 0, split)
-            interleave(scopy, dst, raw, split, width)
-
-        def quantize_w1(g, c0, width):
-            cols = slice(c0, c0 + width)
-            quantize(w1_codes[:, g, cols], w1_scales[:, g, cols], w1_bf[:, g, PACK * c0 : PACK * (c0 + width)])
-
-        interleave_x(0, 80)
-        quantize_x(0)
-        interleave_w1(0, 0, 256, w1_raw0[0], 176)
-        quantize_w1(0, 0, 256)
-        interleave_w1(0, 256, 256, w1_raw0[1], 176)
+        prepare_x(0)
+        prepare_w1_lo(0)
         pass_k(0, 0)
-        quantize_w1(0, 256, 256)
-        interleave_x(1, 80)
-        quantize_x(1)
+        prepare_w1_lo(1)
+        prepare_x(1)
         pass_k(0, 1)
         pass_k(0, 2)
-        for index, split in enumerate((176, 80, 76)):
-            c0, width = PIECES[index]
-            interleave_w1(1, c0, width, w1_raw1[index], split)
-            quantize_w1(1, c0, width)
-            pass_k(1, index)
+        interleave_w1_hi(0, 160)
+        quantize_w1_hi(0)
+        interleave_w1_hi(1, 0)
+        interleave_w1_hi(2, 80)
+        quantize_w1_hi(1)
+        quantize_w1_hi(2)
+
+        w2_codes = keep.tile([P, N], U32, name="w2_codes", align_bytes=64)
+        w2_scales = keep.tile([P, N], U8, name="w2_scales", align_bytes=64)
+
+        def prepare_w2(m, tag):
+            cols = slice(P * m, P * (m + 1))
+            w2_bf = keep.tile([P, P * PACK], BF16, name="w2_bf%d" % m, tag=tag, align_bytes=64)
+            interleave(vcopy, w2_bf[:], w2_raw[m], 0, P)
+            quantize(w2_codes[:, cols], w2_scales[:, cols], w2_bf[:])
+
+        prepare_w2(0, "last")
+
         hb = keep.tile([P, H], BF16, name="hb", tag="h", align_bytes=64)
-        for index in range(3):
-            gelu(index)
+        for index, (c0, width) in enumerate(PIECES):
+            nc.scalar.activation(hb[:, c0 : c0 + width], acc[index][:, 0:width], GELU)
 
         g_bf = keep.tile([P, H], BF16, name="g_bf", align_bytes=64)
         nc.vector.tensor_copy(out=g_bf[:, 0 : 16 * 18], in_=hb[:].indirect(offsets[:, 0:18]))
         nc.scalar.activation(g_bf[:, 16 * 18 : H], hb[:].indirect(offsets[:, 18:32]), COPY)
 
-        w2_bf = keep.tile([P, N * PACK], BF16, name="w2_bf", tag="h", align_bytes=64)
-        w2_codes = keep.tile([P, N], U32, name="w2_codes", align_bytes=64)
-        w2_scales = keep.tile([P, N], U8, name="w2_scales", align_bytes=64)
-        interleave(vcopy, w2_bf[:], w2_raw, 0, 192)
-        interleave(scopy, w2_bf[:], w2_raw, 192, N)
-        quantize(w2_codes[:], w2_scales[:], w2_bf[:])
+        prepare_w2(1, "h")
 
         words = g_bf[:].bitcast(F32)
         turned = psum.tile([P, 2, P], F32, name="turned")

@@ -57,7 +57,7 @@ def tile_picked_shuffle_mlp_gelu_perm_l_kernel(tc, xT, w1, w2, offs, out):
             keep.tile([P, PACK, width], F32, name="w1_raw1_%d" % c0, tag="h" if c0 == 384 else "w1_raw1_%d" % c0, align_bytes=64)
             for c0, width in PIECES
         ]
-        w2_raw = [keep.tile([P, PACK, P], F32, name="w2_raw%d" % m) for m in range(2)]
+        w2_raw = keep.tile([P, PACK, N], F32, name="w2_raw")
 
         w1_lo = w1[0:KP, :].rearrange("(p j) c -> p j c", j=PACK)
         w1_hi = w1[KP:K, :].rearrange("(p j) c -> p j c", j=PACK)
@@ -69,9 +69,8 @@ def tile_picked_shuffle_mlp_gelu_perm_l_kernel(tc, xT, w1, w2, offs, out):
         nc.sync.dma_start(out=w1_raw1[0][:], in_=w1_hi[:, :, 0:256])
         nc.sync.dma_start(out=w1_raw1[1][:], in_=w1_hi[:, :, 256:384])
         nc.sync.dma_start(out=w1_raw1[2][:], in_=w1_hi[:, :, 384:512])
-        nc.sync.dma_start(out=w2_raw[0][:], in_=w2_rows[:, :, 0:P])
         nc.sync.dma_start(offsets[:], offs)
-        nc.sync.dma_start(out=w2_raw[1][:], in_=w2_rows[:, :, P:N])
+        nc.sync.dma_start(out=w2_raw[:], in_=w2_rows)
 
         warm = keep.tile([P, 1], F32, name="warm")
         warm_out = keep.tile([P, 1], F32, name="warm_out")
@@ -144,14 +143,6 @@ def tile_picked_shuffle_mlp_gelu_perm_l_kernel(tc, xT, w1, w2, offs, out):
         w2_codes = keep.tile([P, N], U32, name="w2_codes", align_bytes=64)
         w2_scales = keep.tile([P, N], U8, name="w2_scales", align_bytes=64)
 
-        def prepare_w2(m, tag):
-            cols = slice(P * m, P * (m + 1))
-            w2_bf = keep.tile([P, P * PACK], BF16, name="w2_bf%d" % m, tag=tag, align_bytes=64)
-            interleave(vcopy, w2_bf[:], w2_raw[m], 0, P)
-            quantize(w2_codes[:, cols], w2_scales[:, cols], w2_bf[:])
-
-        prepare_w2(0, "last")
-
         hb = keep.tile([P, H], BF16, name="hb", tag="h", align_bytes=64)
         for index, (c0, width) in enumerate(PIECES):
             nc.scalar.activation(hb[:, c0 : c0 + width], acc[index][:, 0:width], GELU)
@@ -160,7 +151,9 @@ def tile_picked_shuffle_mlp_gelu_perm_l_kernel(tc, xT, w1, w2, offs, out):
         nc.vector.tensor_copy(out=g_bf[:, 0 : 16 * 18], in_=hb[:].indirect(offsets[:, 0:18]))
         nc.scalar.activation(g_bf[:, 16 * 18 : H], hb[:].indirect(offsets[:, 18:32]), COPY)
 
-        prepare_w2(1, "h")
+        w2_bf = keep.tile([P, N * PACK], BF16, name="w2_bf", tag="h", align_bytes=64)
+        shared_interleave(w2_bf[:], w2_raw, 192, N)
+        quantize(w2_codes[:], w2_scales[:], w2_bf[:])
 
         words = g_bf[:].bitcast(F32)
         turned = psum.tile([P, 2, P], F32, name="turned")

@@ -108,13 +108,13 @@ def tile_picked_shuffle_mlp_gelu_perm_l_kernel(tc, xT, w1, w2, offs, out):
         def prepare_x(g):
             cols = slice(g * T, (g + 1) * T)
             dst = x_bf[:, PACK * g * T : PACK * (g + 1) * T]
-            shared_interleave(dst, x_raw[g], 80, T)
+            shared_interleave(dst, x_raw[g], 64, T)
             quantize(x_codes[:, cols], x_scales[:, cols], dst)
 
         def prepare_w1_lo(index):
             cols = slice(256 * index, 256 * (index + 1))
             dst = w1_bf0[:, PACK * cols.start : PACK * cols.stop]
-            shared_interleave(dst, w1_raw0[index], 176, 256)
+            shared_interleave(dst, w1_raw0[index], 128, 256)
             quantize(w1_codes[:, 0, cols], w1_scales[:, 0, cols], dst)
 
         def interleave_w1_hi(index, split):
@@ -133,10 +133,10 @@ def tile_picked_shuffle_mlp_gelu_perm_l_kernel(tc, xT, w1, w2, offs, out):
         prepare_x(1)
         pass_k(0, 1)
         pass_k(0, 2)
-        interleave_w1_hi(0, 160)
+        interleave_w1_hi(0, 128)
         quantize_w1_hi(0)
         interleave_w1_hi(1, 0)
-        interleave_w1_hi(2, 80)
+        interleave_w1_hi(2, 72)
         quantize_w1_hi(1)
         quantize_w1_hi(2)
 

@@ -51,8 +51,8 @@ def tile_picked_shuffle_mlp_gelu_perm_l_kernel(tc, xT, w1, w2, offs, out):
         psum = ctx.enter_context(tc.psum_pool(name="psum", bufs=1))
 
         offsets = keep.tile([P, H // 16], U16, name="offsets")
-        x_raw = [keep.tile([P, PACK, T], F32, name="x_raw%d" % g) for g in range(2)]
-        w1_raw0 = [keep.tile([P, PACK, 256], F32, name="w1_raw0_%d" % c0) for c0 in (0, 256)]
+        x_raw = keep.tile([P, 2, PACK, T], F32, name="x_raw")
+        w1_raw0 = keep.tile([P, PACK, H], F32, name="w1_raw0")
         w1_raw1 = [
             keep.tile([P, PACK, width], F32, name="w1_raw1_%d" % c0, tag="h" if c0 == 384 else "w1_raw1_%d" % c0, align_bytes=64)
             for c0, width in PIECES
@@ -62,10 +62,8 @@ def tile_picked_shuffle_mlp_gelu_perm_l_kernel(tc, xT, w1, w2, offs, out):
         w1_lo = w1[0:KP, :].rearrange("(p j) c -> p j c", j=PACK)
         w1_hi = w1[KP:K, :].rearrange("(p j) c -> p j c", j=PACK)
         w2_rows = w2.rearrange("(p j) m -> p j m", j=PACK)
-        nc.sync.dma_start(out=x_raw[0][:], in_=xT[0:KP, :].rearrange("(p j) t -> p j t", j=PACK))
-        nc.sync.dma_start(out=w1_raw0[0][:], in_=w1_lo[:, :, 0:256])
-        nc.sync.dma_start(out=w1_raw0[1][:], in_=w1_lo[:, :, 256:512])
-        nc.sync.dma_start(out=x_raw[1][:], in_=xT[KP:K, :].rearrange("(p j) t -> p j t", j=PACK))
+        nc.sync.dma_start(out=w1_raw0[:], in_=w1_lo)
+        nc.sync.dma_start(out=x_raw[:], in_=xT.rearrange("(g p j) t -> p g j t", g=2, j=PACK))
         nc.sync.dma_start(out=w1_raw1[0][:], in_=w1_hi[:, :, 0:256])
         nc.sync.dma_start(out=w1_raw1[1][:], in_=w1_hi[:, :, 256:384])
         nc.sync.dma_start(out=w1_raw1[2][:], in_=w1_hi[:, :, 384:512])
@@ -105,17 +103,16 @@ def tile_picked_shuffle_mlp_gelu_perm_l_kernel(tc, xT, w1, w2, offs, out):
                 stop=(g == 1),
             )
 
-        def prepare_x(g):
-            cols = slice(g * T, (g + 1) * T)
-            dst = x_bf[:, PACK * g * T : PACK * (g + 1) * T]
-            shared_interleave(dst, x_raw[g], 64, T)
-            quantize(x_codes[:, cols], x_scales[:, cols], dst)
+        def interleave_x(g, split):
+            shared_interleave(x_bf[:, PACK * g * T : PACK * (g + 1) * T], x_raw[:, g], split, T)
 
-        def prepare_w1_lo(index):
+        def quantize_x(g):
+            cols = slice(g * T, (g + 1) * T)
+            quantize(x_codes[:, cols], x_scales[:, cols], x_bf[:, PACK * g * T : PACK * (g + 1) * T])
+
+        def quantize_w1_lo(index):
             cols = slice(256 * index, 256 * (index + 1))
-            dst = w1_bf0[:, PACK * cols.start : PACK * cols.stop]
-            shared_interleave(dst, w1_raw0[index], 128, 256)
-            quantize(w1_codes[:, 0, cols], w1_scales[:, 0, cols], dst)
+            quantize(w1_codes[:, 0, cols], w1_scales[:, 0, cols], w1_bf0[:, PACK * cols.start : PACK * cols.stop])
 
         def interleave_w1_hi(index, split):
             shared_interleave(w1_bf1[index][:], w1_raw1[index], split, PIECES[index][1])
@@ -126,13 +123,15 @@ def tile_picked_shuffle_mlp_gelu_perm_l_kernel(tc, xT, w1, w2, offs, out):
             quantize(w1_codes[:, 1, cols], w1_scales[:, 1, cols], w1_bf1[index][:])
             pass_k(1, index)
 
-        prepare_x(0)
-        prepare_w1_lo(0)
-        pass_k(0, 0)
-        prepare_w1_lo(1)
-        prepare_x(1)
-        pass_k(0, 1)
-        pass_k(0, 2)
+        shared_interleave(w1_bf0[:], w1_raw0, 288, H)
+        quantize_w1_lo(0)
+        interleave_x(0, 128)
+        interleave_x(1, 0)
+        quantize_w1_lo(1)
+        quantize_x(0)
+        quantize_x(1)
+        for index in range(3):
+            pass_k(0, index)
         interleave_w1_hi(0, 128)
         quantize_w1_hi(0)
         interleave_w1_hi(1, 0)

@@ -110,9 +110,11 @@ def tile_picked_shuffle_mlp_gelu_perm_l_kernel(tc, xT, w1, w2, offs, out):
             cols = slice(g * T, (g + 1) * T)
             quantize(x_codes[:, cols], x_scales[:, cols], x_bf[:, PACK * g * T : PACK * (g + 1) * T])
 
-        def quantize_w1_lo(index):
-            cols = slice(256 * index, 256 * (index + 1))
-            quantize(w1_codes[:, 0, cols], w1_scales[:, 0, cols], w1_bf0[:, PACK * cols.start : PACK * cols.stop])
+        def quantize_w1_lo(c0, c1):
+            quantize(w1_codes[:, 0, c0:c1], w1_scales[:, 0, c0:c1], w1_bf0[:, PACK * c0 : PACK * c1])
+
+        def quantize_w1_first(c0, c1):
+            quantize(w1_codes[:, 1, c0:c1], w1_scales[:, 1, c0:c1], w1_bf1[0][:, PACK * c0 : PACK * c1])
 
         def interleave_w1_hi(index, split):
             shared_interleave(w1_bf1[index][:], w1_raw1[index], split, PIECES[index][1])
@@ -123,19 +125,23 @@ def tile_picked_shuffle_mlp_gelu_perm_l_kernel(tc, xT, w1, w2, offs, out):
             quantize(w1_codes[:, 1, cols], w1_scales[:, 1, cols], w1_bf1[index][:])
             pass_k(1, index)
 
-        shared_interleave(w1_bf0[:], w1_raw0, 288, H)
-        quantize_w1_lo(0)
-        interleave_x(0, 128)
+        interleave(vcopy, w1_bf0[:], w1_raw0, 0, 256)
+        interleave(vcopy, w1_bf0[:], w1_raw0, 256, 288)
+        interleave(scopy, w1_bf0[:], w1_raw0, 288, H)
+        quantize_w1_lo(0, 256)
+        interleave_x(0, 96)
         interleave_x(1, 0)
-        quantize_w1_lo(1)
+        quantize_w1_lo(256, 512)
         quantize_x(0)
         quantize_x(1)
         for index in range(3):
             pass_k(0, index)
         interleave_w1_hi(0, 128)
-        quantize_w1_hi(0)
+        quantize_w1_first(0, 128)
+        quantize_w1_first(128, 256)
+        pass_k(1, 0)
         interleave_w1_hi(1, 0)
-        interleave_w1_hi(2, 72)
+        interleave_w1_hi(2, 56)
         quantize_w1_hi(1)
         quantize_w1_hi(2)
 

@@ -31,17 +31,11 @@ def tile_picked_shuffle_mlp_gelu_perm_l_kernel(tc, xT, w1, w2, offs, out):
     def scopy(dst, src):
         nc.scalar.copy(dst, src)
 
-    def interleave(copy, dst, raw, c0, c1):
+    def interleave(copy, dst, raw, first, c0, c1):
         copy(
             dst[:, PACK * c0 : PACK * c1].rearrange("p (c i j) -> p c j i", i=4, j=PACK),
-            raw[:, :, c0:c1].rearrange("p j (c i) -> p c j i", i=4),
+            raw[:, :, first + c0 : first + c1].rearrange("p j (c i) -> p c j i", i=4),
         )
-
-    def shared_interleave(dst, raw, split, width):
-        if split > 0:
-            interleave(vcopy, dst, raw, 0, split)
-        if split < width:
-            interleave(scopy, dst, raw, split, width)
 
     def quantize(codes, scales, grouped):
         nc.vector.quantize_mx(out=codes.bitcast(FP8X4), scales=scales, in_=grouped)
@@ -51,22 +45,20 @@ def tile_picked_shuffle_mlp_gelu_perm_l_kernel(tc, xT, w1, w2, offs, out):
         psum = ctx.enter_context(tc.psum_pool(name="psum", bufs=1))
 
         offsets = keep.tile([P, H // 16], U16, name="offsets")
-        x_raw = keep.tile([P, 2, PACK, T], F32, name="x_raw")
-        w1_raw0 = keep.tile([P, PACK, H], F32, name="w1_raw0")
-        w1_raw1 = [
-            keep.tile([P, PACK, width], F32, name="w1_raw1_%d" % c0, tag="h" if c0 == 384 else "w1_raw1_%d" % c0, align_bytes=64)
-            for c0, width in PIECES
-        ]
-        w2_raw = keep.tile([P, PACK, N], F32, name="w2_raw")
-
         w1_lo = w1[0:KP, :].rearrange("(p j) c -> p j c", j=PACK)
         w1_hi = w1[KP:K, :].rearrange("(p j) c -> p j c", j=PACK)
         w2_rows = w2.rearrange("(p j) m -> p j m", j=PACK)
-        nc.sync.dma_start(out=w1_raw0[:], in_=w1_lo)
-        nc.sync.dma_start(out=x_raw[:], in_=xT.rearrange("(g p j) t -> p g j t", g=2, j=PACK))
-        nc.sync.dma_start(out=w1_raw1[0][:], in_=w1_hi[:, :, 0:256])
-        nc.sync.dma_start(out=w1_raw1[1][:], in_=w1_hi[:, :, 256:384])
-        nc.sync.dma_start(out=w1_raw1[2][:], in_=w1_hi[:, :, 384:512])
+        raw_a = keep.tile([P, PACK, H], F32, name="raw_a")
+        raw_x = keep.tile([P, 2, PACK, T], F32, name="raw_x")
+        raw_b0 = keep.tile([P, PACK, 256], F32, name="raw_b0")
+        raw_b1 = keep.tile([P, PACK, 128], F32, name="raw_b1")
+        raw_b2 = keep.tile([P, PACK, 128], F32, name="raw_b2", tag="h", align_bytes=64)
+        w2_raw = keep.tile([P, PACK, N], F32, name="w2_raw")
+        nc.sync.dma_start(out=raw_a[:], in_=w1_lo)
+        nc.sync.dma_start(out=raw_x[:], in_=xT.rearrange("(g p j) t -> p g j t", g=2, j=PACK))
+        nc.sync.dma_start(out=raw_b0[:], in_=w1_hi[:, :, 0:256])
+        nc.sync.dma_start(out=raw_b1[:], in_=w1_hi[:, :, 256:384])
+        nc.sync.dma_start(out=raw_b2[:], in_=w1_hi[:, :, 384:512])
         nc.sync.dma_start(offsets[:], offs)
         nc.sync.dma_start(out=w2_raw[:], in_=w2_rows)
 
@@ -78,86 +70,72 @@ def tile_picked_shuffle_mlp_gelu_perm_l_kernel(tc, xT, w1, w2, offs, out):
         ident = keep.tile([P, P], F32, name="ident")
         make_identity(nc, ident[:])
 
-        x_bf = keep.tile([P, 2 * T * PACK], BF16, name="x_bf", align_bytes=64)
+        bf_a0 = keep.tile([P, 256 * PACK], BF16, name="bf_a0", align_bytes=64)
+        bf_a1 = keep.tile([P, 256 * PACK], BF16, name="bf_a1", align_bytes=64)
+        bf_x0 = keep.tile([P, 128 * PACK], BF16, name="bf_x0", align_bytes=64)
+        bf_x1 = keep.tile([P, 128 * PACK], BF16, name="bf_x1", align_bytes=64)
+        bf_b0 = keep.tile([P, 128 * PACK], BF16, name="bf_b0", align_bytes=64)
+        bf_b0s = keep.tile([P, 128 * PACK], BF16, name="bf_b0s", align_bytes=64)
+        bf_b1 = keep.tile([P, 128 * PACK], BF16, name="bf_b1", align_bytes=64)
+        bf_b2 = keep.tile([P, 128 * PACK], BF16, name="bf_b2", align_bytes=64)
         x_codes = keep.tile([P, 2 * T], U32, name="x_codes", align_bytes=64)
         x_scales = keep.tile([P, 2 * T], U8, name="x_scales", align_bytes=64)
-        w1_bf0 = keep.tile([P, H * PACK], BF16, name="w1_bf0", align_bytes=64)
-        w1_bf1 = [
-            keep.tile([P, width * PACK], BF16, name="w1_bf1_%d" % c0, tag="last" if c0 == 384 else "w1_bf1_%d" % c0, align_bytes=64)
-            for c0, width in PIECES
-        ]
-        w1_codes = keep.tile([P, 2, H], U32, name="w1_codes", align_bytes=64)
-        w1_scales = keep.tile([P, 2, H], U8, name="w1_scales", align_bytes=64)
+        w1_codes = keep.tile([P, 2 * H], U32, name="w1_codes", align_bytes=64)
+        w1_scales = keep.tile([P, 2 * H], U8, name="w1_scales", align_bytes=64)
 
         acc = [psum.tile([P, 512], F32, name="acc%d" % c0) for c0, width in PIECES]
 
         def pass_k(g, index):
             c0, width = PIECES[index]
+            cols = slice(g * H + c0, g * H + c0 + width)
             nc.tensor.matmul_mx(
                 out=acc[index][:, 0:width],
                 lhsT=x_codes[:, g * T : (g + 1) * T].bitcast(FP8X4),
                 lhsT_scale=x_scales[:, g * T : (g + 1) * T],
-                rhs=w1_codes[:, g, c0 : c0 + width].bitcast(FP8X4),
-                rhs_scale=w1_scales[:, g, c0 : c0 + width],
+                rhs=w1_codes[:, cols].bitcast(FP8X4),
+                rhs_scale=w1_scales[:, cols],
                 start=(g == 0),
                 stop=(g == 1),
             )
 
-        def interleave_x(g, split):
-            shared_interleave(x_bf[:, PACK * g * T : PACK * (g + 1) * T], x_raw[:, g], split, T)
-
-        def quantize_x(g):
-            cols = slice(g * T, (g + 1) * T)
-            quantize(x_codes[:, cols], x_scales[:, cols], x_bf[:, PACK * g * T : PACK * (g + 1) * T])
-
-        def quantize_w1_lo(c0, c1):
-            quantize(w1_codes[:, 0, c0:c1], w1_scales[:, 0, c0:c1], w1_bf0[:, PACK * c0 : PACK * c1])
-
-        def quantize_w1_first(c0, c1):
-            quantize(w1_codes[:, 1, c0:c1], w1_scales[:, 1, c0:c1], w1_bf1[0][:, PACK * c0 : PACK * c1])
-
-        def interleave_w1_hi(index, split):
-            shared_interleave(w1_bf1[index][:], w1_raw1[index], split, PIECES[index][1])
-
-        def quantize_w1_hi(index):
-            c0, width = PIECES[index]
-            cols = slice(c0, c0 + width)
-            quantize(w1_codes[:, 1, cols], w1_scales[:, 1, cols], w1_bf1[index][:])
-            pass_k(1, index)
-
-        interleave(vcopy, w1_bf0[:], w1_raw0, 0, 256)
-        interleave(vcopy, w1_bf0[:], w1_raw0, 256, 288)
-        interleave(scopy, w1_bf0[:], w1_raw0, 288, H)
-        quantize_w1_lo(0, 256)
-        interleave_x(0, 96)
-        interleave_x(1, 0)
-        quantize_w1_lo(256, 512)
-        quantize_x(0)
-        quantize_x(1)
-        for index in range(3):
-            pass_k(0, index)
-        interleave_w1_hi(0, 128)
-        quantize_w1_first(0, 128)
-        quantize_w1_first(128, 256)
+        interleave(vcopy, bf_a0[:], raw_a, 0, 0, 256)
+        interleave(vcopy, bf_a1[:], raw_a, 256, 0, 32)
+        interleave(scopy, bf_a1[:], raw_a, 256, 32, 256)
+        quantize(w1_codes[:, 0:256], w1_scales[:, 0:256], bf_a0[:])
+        interleave(vcopy, bf_x0[:], raw_x[:, 0], 0, 0, 128)
+        interleave(scopy, bf_x1[:], raw_x[:, 1], 0, 0, 128)
+        quantize(w1_codes[:, 256:512], w1_scales[:, 256:512], bf_a1[:])
+        quantize(x_codes[:, 0:128], x_scales[:, 0:128], bf_x0[:])
+        pass_k(0, 0)
+        pass_k(0, 1)
+        pass_k(0, 2)
+        quantize(x_codes[:, 128:256], x_scales[:, 128:256], bf_x1[:])
+        interleave(vcopy, bf_b0[:], raw_b0, 0, 0, 128)
+        interleave(scopy, bf_b0s[:], raw_b0, 128, 0, 128)
+        quantize(w1_codes[:, 512:640], w1_scales[:, 512:640], bf_b0[:])
+        quantize(w1_codes[:, 640:768], w1_scales[:, 640:768], bf_b0s[:])
         pass_k(1, 0)
-        interleave_w1_hi(1, 0)
-        interleave_w1_hi(2, 56)
-        quantize_w1_hi(1)
-        quantize_w1_hi(2)
-
-        w2_codes = keep.tile([P, N], U32, name="w2_codes", align_bytes=64)
-        w2_scales = keep.tile([P, N], U8, name="w2_scales", align_bytes=64)
+        interleave(scopy, bf_b1[:], raw_b1, 0, 0, 128)
+        interleave(vcopy, bf_b2[:], raw_b2, 0, 0, 72)
+        interleave(scopy, bf_b2[:], raw_b2, 0, 72, 128)
+        quantize(w1_codes[:, 768:896], w1_scales[:, 768:896], bf_b1[:])
+        pass_k(1, 1)
+        quantize(w1_codes[:, 896:1024], w1_scales[:, 896:1024], bf_b2[:])
+        pass_k(1, 2)
 
         hb = keep.tile([P, H], BF16, name="hb", tag="h", align_bytes=64)
         for index, (c0, width) in enumerate(PIECES):
             nc.scalar.activation(hb[:, c0 : c0 + width], acc[index][:, 0:width], GELU)
 
         g_bf = keep.tile([P, H], BF16, name="g_bf", align_bytes=64)
-        nc.vector.tensor_copy(out=g_bf[:, 0 : 16 * 18], in_=hb[:].indirect(offsets[:, 0:18]))
-        nc.scalar.activation(g_bf[:, 16 * 18 : H], hb[:].indirect(offsets[:, 18:32]), COPY)
+        nc.vector.tensor_copy(out=g_bf[:, 0 : 16 * 16], in_=hb[:].indirect(offsets[:, 0:16]))
+        nc.scalar.activation(g_bf[:, 16 * 16 : H], hb[:].indirect(offsets[:, 16:32]), COPY)
 
+        w2_codes = keep.tile([P, N], U32, name="w2_codes", align_bytes=64)
+        w2_scales = keep.tile([P, N], U8, name="w2_scales", align_bytes=64)
         w2_bf = keep.tile([P, N * PACK], BF16, name="w2_bf", tag="h", align_bytes=64)
-        shared_interleave(w2_bf[:], w2_raw, 192, N)
+        interleave(vcopy, w2_bf[:], w2_raw, 0, 0, 192)
+        interleave(scopy, w2_bf[:], w2_raw, 0, 192, N)
         quantize(w2_codes[:], w2_scales[:], w2_bf[:])
 
         words = g_bf[:].bitcast(F32)

@@ -128,8 +128,8 @@ def tile_picked_shuffle_mlp_gelu_perm_l_kernel(tc, xT, w1, w2, offs, out):
             nc.scalar.activation(hb[:, c0 : c0 + width], acc[index][:, 0:width], GELU)
 
         g_bf = keep.tile([P, H], BF16, name="g_bf", align_bytes=64)
-        nc.vector.tensor_copy(out=g_bf[:, 0 : 16 * 16], in_=hb[:].indirect(offsets[:, 0:16]))
-        nc.scalar.activation(g_bf[:, 16 * 16 : H], hb[:].indirect(offsets[:, 16:32]), COPY)
+        nc.vector.tensor_copy(out=g_bf[:, 0 : 16 * 18], in_=hb[:].indirect(offsets[:, 0:18]))
+        nc.scalar.activation(g_bf[:, 16 * 18 : H], hb[:].indirect(offsets[:, 18:32]), COPY)
 
         w2_codes = keep.tile([P, N], U32, name="w2_codes", align_bytes=64)
         w2_scales = keep.tile([P, N], U8, name="w2_scales", align_bytes=64)

@@ -48,12 +48,12 @@ def tile_picked_shuffle_mlp_gelu_perm_l_kernel(tc, xT, w1, w2, offs, out):
         w1_lo = w1[0:KP, :].rearrange("(p j) c -> p j c", j=PACK)
         w1_hi = w1[KP:K, :].rearrange("(p j) c -> p j c", j=PACK)
         w2_rows = w2.rearrange("(p j) m -> p j m", j=PACK)
-        raw_a = keep.tile([P, PACK, H], F32, name="raw_a")
-        raw_x = keep.tile([P, 2, PACK, T], F32, name="raw_x")
-        raw_b0 = keep.tile([P, PACK, 256], F32, name="raw_b0")
-        raw_b1 = keep.tile([P, PACK, 128], F32, name="raw_b1")
-        raw_b2 = keep.tile([P, PACK, 128], F32, name="raw_b2", tag="h", align_bytes=64)
-        w2_raw = keep.tile([P, PACK, N], F32, name="w2_raw")
+        raw_x = keep.tile([P, 2, PACK, T], F32, name="raw_x", align_bytes=512)
+        raw_a = keep.tile([P, PACK, H], F32, name="raw_a", align_bytes=512)
+        raw_b0 = keep.tile([P, PACK, 256], F32, name="raw_b0", align_bytes=512)
+        raw_b1 = keep.tile([P, PACK, 128], F32, name="raw_b1", align_bytes=512)
+        raw_b2 = keep.tile([P, PACK, 128], F32, name="raw_b2", tag="h", align_bytes=512)
+        w2_raw = keep.tile([P, PACK, N], F32, name="w2_raw", align_bytes=512)
         nc.sync.dma_start(out=raw_a[:], in_=w1_lo)
         nc.sync.dma_start(out=raw_x[:], in_=xT.rearrange("(g p j) t -> p g j t", g=2, j=PACK))
         nc.sync.dma_start(out=raw_b0[:], in_=w1_hi[:, :, 0:256])
@@ -67,21 +67,21 @@ def tile_picked_shuffle_mlp_gelu_perm_l_kernel(tc, xT, w1, w2, offs, out):
         nc.vector.memset(warm[:], 0.0)
         nc.scalar.activation(warm_out[:], warm[:], GELU)
 
-        ident = keep.tile([P, P], F32, name="ident")
+        ident = keep.tile([P, P], F32, name="ident", align_bytes=512)
         make_identity(nc, ident[:])
 
-        bf_a0 = keep.tile([P, 256 * PACK], BF16, name="bf_a0", align_bytes=64)
-        bf_a1 = keep.tile([P, 256 * PACK], BF16, name="bf_a1", align_bytes=64)
-        bf_x0 = keep.tile([P, 128 * PACK], BF16, name="bf_x0", align_bytes=64)
-        bf_x1 = keep.tile([P, 128 * PACK], BF16, name="bf_x1", align_bytes=64)
-        bf_b0 = keep.tile([P, 128 * PACK], BF16, name="bf_b0", align_bytes=64)
-        bf_b0s = keep.tile([P, 128 * PACK], BF16, name="bf_b0s", align_bytes=64)
-        bf_b1 = keep.tile([P, 128 * PACK], BF16, name="bf_b1", align_bytes=64)
-        bf_b2 = keep.tile([P, 128 * PACK], BF16, name="bf_b2", align_bytes=64)
-        x_codes = keep.tile([P, 2 * T], U32, name="x_codes", align_bytes=64)
-        x_scales = keep.tile([P, 2 * T], U8, name="x_scales", align_bytes=64)
-        w1_codes = keep.tile([P, 2 * H], U32, name="w1_codes", align_bytes=64)
-        w1_scales = keep.tile([P, 2 * H], U8, name="w1_scales", align_bytes=64)
+        bf_a0 = keep.tile([P, 256 * PACK], BF16, name="bf_a0", align_bytes=512)
+        bf_a1 = keep.tile([P, 256 * PACK], BF16, name="bf_a1", align_bytes=512)
+        bf_x0 = keep.tile([P, 128 * PACK], BF16, name="bf_x0", align_bytes=512)
+        bf_x1 = keep.tile([P, 128 * PACK], BF16, name="bf_x1", align_bytes=512)
+        bf_b0 = keep.tile([P, 128 * PACK], BF16, name="bf_b0", align_bytes=512)
+        bf_b0s = keep.tile([P, 128 * PACK], BF16, name="bf_b0s", align_bytes=512)
+        bf_b1 = keep.tile([P, 128 * PACK], BF16, name="bf_b1", align_bytes=512)
+        bf_b2 = keep.tile([P, 128 * PACK], BF16, name="bf_b2", align_bytes=512)
+        x_codes = keep.tile([P, 2 * T], U32, name="x_codes", align_bytes=512)
+        x_scales = keep.tile([P, 2 * T], U8, name="x_scales", align_bytes=512)
+        w1_codes = keep.tile([P, 2 * H], U32, name="w1_codes", align_bytes=512)
+        w1_scales = keep.tile([P, 2 * H], U8, name="w1_scales", align_bytes=512)
 
         acc = [psum.tile([P, 512], F32, name="acc%d" % c0) for c0, width in PIECES]
 
@@ -102,38 +102,39 @@ def tile_picked_shuffle_mlp_gelu_perm_l_kernel(tc, xT, w1, w2, offs, out):
         interleave(vcopy, bf_a1[:], raw_a, 256, 0, 32)
         interleave(scopy, bf_a1[:], raw_a, 256, 32, 256)
         quantize(w1_codes[:, 0:256], w1_scales[:, 0:256], bf_a0[:])
-        interleave(vcopy, bf_x0[:], raw_x[:, 0], 0, 0, 128)
+        interleave(vcopy, bf_x0[:], raw_x[:, 0], 0, 0, 96)
+        interleave(scopy, bf_x0[:], raw_x[:, 0], 0, 96, 128)
         interleave(scopy, bf_x1[:], raw_x[:, 1], 0, 0, 128)
         quantize(w1_codes[:, 256:512], w1_scales[:, 256:512], bf_a1[:])
         quantize(x_codes[:, 0:128], x_scales[:, 0:128], bf_x0[:])
+        quantize(x_codes[:, 128:256], x_scales[:, 128:256], bf_x1[:])
         pass_k(0, 0)
         pass_k(0, 1)
         pass_k(0, 2)
-        quantize(x_codes[:, 128:256], x_scales[:, 128:256], bf_x1[:])
         interleave(vcopy, bf_b0[:], raw_b0, 0, 0, 128)
         interleave(scopy, bf_b0s[:], raw_b0, 128, 0, 128)
         quantize(w1_codes[:, 512:640], w1_scales[:, 512:640], bf_b0[:])
         quantize(w1_codes[:, 640:768], w1_scales[:, 640:768], bf_b0s[:])
         pass_k(1, 0)
         interleave(scopy, bf_b1[:], raw_b1, 0, 0, 128)
-        interleave(vcopy, bf_b2[:], raw_b2, 0, 0, 72)
-        interleave(scopy, bf_b2[:], raw_b2, 0, 72, 128)
+        interleave(vcopy, bf_b2[:], raw_b2, 0, 0, 56)
+        interleave(scopy, bf_b2[:], raw_b2, 0, 56, 128)
         quantize(w1_codes[:, 768:896], w1_scales[:, 768:896], bf_b1[:])
         pass_k(1, 1)
         quantize(w1_codes[:, 896:1024], w1_scales[:, 896:1024], bf_b2[:])
         pass_k(1, 2)
 
-        hb = keep.tile([P, H], BF16, name="hb", tag="h", align_bytes=64)
+        w2_codes = keep.tile([P, N], U32, name="w2_codes", align_bytes=512)
+        w2_scales = keep.tile([P, N], U8, name="w2_scales", align_bytes=512)
+        hb = keep.tile([P, H], BF16, name="hb", tag="h", align_bytes=512)
         for index, (c0, width) in enumerate(PIECES):
             nc.scalar.activation(hb[:, c0 : c0 + width], acc[index][:, 0:width], GELU)
 
-        g_bf = keep.tile([P, H], BF16, name="g_bf", align_bytes=64)
+        g_bf = keep.tile([P, H], BF16, name="g_bf", align_bytes=512)
         nc.vector.tensor_copy(out=g_bf[:, 0 : 16 * 18], in_=hb[:].indirect(offsets[:, 0:18]))
         nc.scalar.activation(g_bf[:, 16 * 18 : H], hb[:].indirect(offsets[:, 18:32]), COPY)
 
-        w2_codes = keep.tile([P, N], U32, name="w2_codes", align_bytes=64)
-        w2_scales = keep.tile([P, N], U8, name="w2_scales", align_bytes=64)
-        w2_bf = keep.tile([P, N * PACK], BF16, name="w2_bf", tag="h", align_bytes=64)
+        w2_bf = keep.tile([P, N * PACK], BF16, name="w2_bf", tag="h", align_bytes=512)
         interleave(vcopy, w2_bf[:], w2_raw, 0, 0, 192)
         interleave(scopy, w2_bf[:], w2_raw, 0, 192, N)
         quantize(w2_codes[:], w2_scales[:], w2_bf[:])
@@ -142,10 +143,10 @@ def tile_picked_shuffle_mlp_gelu_perm_l_kernel(tc, xT, w1, w2, offs, out):
         turned = psum.tile([P, 2, P], F32, name="turned")
         for u in range(2):
             nc.tensor.transpose(turned[:, u, :], words[:, u : 2 * P : 2], ident[:])
-        h_bf = keep.tile([P, T * PACK], BF16, name="h_bf", align_bytes=64)
+        h_bf = keep.tile([P, T * PACK], BF16, name="h_bf", align_bytes=512)
         nc.scalar.copy(h_bf[:].bitcast(F32).rearrange("p (t u) -> p t u", u=2), turned[:].rearrange("p u t -> p t u"))
-        h_codes = keep.tile([P, T], U32, name="h_codes", align_bytes=64)
-        h_scales = keep.tile([P, T], U8, name="h_scales", align_bytes=64)
+        h_codes = keep.tile([P, T], U32, name="h_codes", align_bytes=512)
+        h_scales = keep.tile([P, T], U8, name="h_scales", align_bytes=512)
         quantize(h_codes[:], h_scales[:], h_bf[:])
 
         for m, copy, dma in ((0, vcopy, nc.sync), (1, scopy, nc.scalar)):
@@ -160,6 +161,6 @@ def tile_picked_shuffle_mlp_gelu_perm_l_kernel(tc, xT, w1, w2, offs, out):
                 start=True,
                 stop=True,
             )
-            y = keep.tile([P, T], F32, name="y%d" % m)
+            y = keep.tile([P, T], F32, name="y%d" % m, align_bytes=512)
             copy(y[:], bank[:, 0:T])
             dma.dma_start(out=out[cols, :], in_=y[:])

@@ -117,8 +117,7 @@ def tile_picked_shuffle_mlp_gelu_perm_l_kernel(tc, xT, w1, w2, offs, out):
         quantize(w1_codes[:, 640:768], w1_scales[:, 640:768], bf_b0s[:])
         pass_k(1, 0)
         interleave(scopy, bf_b1[:], raw_b1, 0, 0, 128)
-        interleave(vcopy, bf_b2[:], raw_b2, 0, 0, 56)
-        interleave(scopy, bf_b2[:], raw_b2, 0, 56, 128)
+        interleave(vcopy, bf_b2[:], raw_b2, 0, 0, 128)
         quantize(w1_codes[:, 768:896], w1_scales[:, 768:896], bf_b1[:])
         pass_k(1, 1)
         quantize(w1_codes[:, 896:1024], w1_scales[:, 896:1024], bf_b2[:])

@@ -48,14 +48,18 @@ def tile_picked_shuffle_mlp_gelu_perm_l_kernel(tc, xT, w1, w2, offs, out):
         w1_lo = w1[0:KP, :].rearrange("(p j) c -> p j c", j=PACK)
         w1_hi = w1[KP:K, :].rearrange("(p j) c -> p j c", j=PACK)
         w2_rows = w2.rearrange("(p j) m -> p j m", j=PACK)
-        raw_x = keep.tile([P, 2, PACK, T], F32, name="raw_x", align_bytes=512)
-        raw_a = keep.tile([P, PACK, H], F32, name="raw_a", align_bytes=512)
+        raw_x0 = keep.tile([P, PACK, T], F32, name="raw_x0", align_bytes=512)
+        raw_x1 = keep.tile([P, PACK, T], F32, name="raw_x1", align_bytes=512)
+        raw_a0 = keep.tile([P, PACK, 256], F32, name="raw_a0", align_bytes=512)
+        raw_a1 = keep.tile([P, PACK, 256], F32, name="raw_a1", align_bytes=512)
         raw_b0 = keep.tile([P, PACK, 256], F32, name="raw_b0", align_bytes=512)
         raw_b1 = keep.tile([P, PACK, 128], F32, name="raw_b1", align_bytes=512)
         raw_b2 = keep.tile([P, PACK, 128], F32, name="raw_b2", tag="h", align_bytes=512)
         w2_raw = keep.tile([P, PACK, N], F32, name="w2_raw", align_bytes=512)
-        nc.sync.dma_start(out=raw_a[:], in_=w1_lo)
-        nc.sync.dma_start(out=raw_x[:], in_=xT.rearrange("(g p j) t -> p g j t", g=2, j=PACK))
+        nc.sync.dma_start(out=raw_x0[:], in_=xT[0:KP, :].rearrange("(p j) t -> p j t", j=PACK))
+        nc.sync.dma_start(out=raw_a0[:], in_=w1_lo[:, :, 0:256])
+        nc.sync.dma_start(out=raw_a1[:], in_=w1_lo[:, :, 256:512])
+        nc.sync.dma_start(out=raw_x1[:], in_=xT[KP:K, :].rearrange("(p j) t -> p j t", j=PACK))
         nc.sync.dma_start(out=raw_b0[:], in_=w1_hi[:, :, 0:256])
         nc.sync.dma_start(out=raw_b1[:], in_=w1_hi[:, :, 256:384])
         nc.sync.dma_start(out=raw_b2[:], in_=w1_hi[:, :, 384:512])
@@ -98,19 +102,20 @@ def tile_picked_shuffle_mlp_gelu_perm_l_kernel(tc, xT, w1, w2, offs, out):
                 stop=(g == 1),
             )
 
-        interleave(vcopy, bf_a0[:], raw_a, 0, 0, 256)
-        interleave(vcopy, bf_a1[:], raw_a, 256, 0, 32)
-        interleave(scopy, bf_a1[:], raw_a, 256, 32, 256)
-        quantize(w1_codes[:, 0:256], w1_scales[:, 0:256], bf_a0[:])
-        interleave(vcopy, bf_x0[:], raw_x[:, 0], 0, 0, 96)
-        interleave(scopy, bf_x0[:], raw_x[:, 0], 0, 96, 128)
-        interleave(scopy, bf_x1[:], raw_x[:, 1], 0, 0, 128)
-        quantize(w1_codes[:, 256:512], w1_scales[:, 256:512], bf_a1[:])
+        interleave(vcopy, bf_x0[:], raw_x0, 0, 0, 64)
+        interleave(scopy, bf_x0[:], raw_x0, 0, 64, 128)
         quantize(x_codes[:, 0:128], x_scales[:, 0:128], bf_x0[:])
-        quantize(x_codes[:, 128:256], x_scales[:, 128:256], bf_x1[:])
+        interleave(vcopy, bf_a0[:], raw_a0, 0, 0, 128)
+        interleave(scopy, bf_a0[:], raw_a0, 0, 128, 256)
+        quantize(w1_codes[:, 0:256], w1_scales[:, 0:256], bf_a0[:])
         pass_k(0, 0)
+        interleave(vcopy, bf_a1[:], raw_a1, 0, 0, 128)
+        interleave(scopy, bf_a1[:], raw_a1, 0, 128, 256)
+        quantize(w1_codes[:, 256:512], w1_scales[:, 256:512], bf_a1[:])
         pass_k(0, 1)
         pass_k(0, 2)
+        interleave(scopy, bf_x1[:], raw_x1, 0, 0, 128)
+        quantize(x_codes[:, 128:256], x_scales[:, 128:256], bf_x1[:])
         interleave(vcopy, bf_b0[:], raw_b0, 0, 0, 128)
         interleave(scopy, bf_b0s[:], raw_b0, 128, 0, 128)
         quantize(w1_codes[:, 512:640], w1_scales[:, 512:640], bf_b0[:])

@@ -33,8 +33,8 @@ def tile_picked_shuffle_mlp_gelu_perm_l_kernel(tc, xT, w1, w2, offs, out):
 
     def interleave(copy, dst, raw, first, c0, c1):
         copy(
-            dst[:, PACK * c0 : PACK * c1].rearrange("p (c i j) -> p c j i", i=4, j=PACK),
-            raw[:, :, first + c0 : first + c1].rearrange("p j (c i) -> p c j i", i=4),
+            dst[:, PACK * c0 : PACK * c1].rearrange("p (c i j) -> p c j i", i=2, j=PACK),
+            raw[:, :, first + c0 : first + c1].rearrange("p j (c i) -> p c j i", i=2),
         )
 
     def quantize(codes, scales, grouped):
@@ -52,7 +52,8 @@ def tile_picked_shuffle_mlp_gelu_perm_l_kernel(tc, xT, w1, w2, offs, out):
         raw_x1 = keep.tile([P, PACK, T], F32, name="raw_x1", align_bytes=512)
         raw_a0 = keep.tile([P, PACK, 256], F32, name="raw_a0", align_bytes=512)
         raw_a1 = keep.tile([P, PACK, 256], F32, name="raw_a1", align_bytes=512)
-        raw_b0 = keep.tile([P, PACK, 256], F32, name="raw_b0", align_bytes=512)
+        raw_b0 = keep.tile([P, PACK, 128], F32, name="raw_b0", align_bytes=512)
+        raw_b0s = keep.tile([P, PACK, 128], F32, name="raw_b0s", align_bytes=512)
         raw_b1 = keep.tile([P, PACK, 128], F32, name="raw_b1", align_bytes=512)
         raw_b2 = keep.tile([P, PACK, 128], F32, name="raw_b2", tag="h", align_bytes=512)
         w2_raw = keep.tile([P, PACK, N], F32, name="w2_raw", align_bytes=512)
@@ -60,8 +61,10 @@ def tile_picked_shuffle_mlp_gelu_perm_l_kernel(tc, xT, w1, w2, offs, out):
         nc.sync.dma_start(out=raw_a0[:], in_=w1_lo[:, :, 0:256])
         nc.sync.dma_start(out=raw_a1[:], in_=w1_lo[:, :, 256:512])
         nc.sync.dma_start(out=raw_x1[:], in_=xT[KP:K, :].rearrange("(p j) t -> p j t", j=PACK))
-        nc.sync.dma_start(out=raw_b0[:], in_=w1_hi[:, :, 0:256])
-        nc.sync.dma_start(out=raw_b1[:], in_=w1_hi[:, :, 256:384])
+        nc.sync.dma_start(out=raw_b0[:], in_=w1_hi[:, :, 0:128])
+        nc.sync.dma_start(out=raw_b0s[:], in_=w1_hi[:, :, 128:256])
+        nc.sync.dma_start(out=raw_b1[:, 0:2], in_=w1_hi[:, 0:2, 256:384])
+        nc.sync.dma_start(out=raw_b1[:, 2:4], in_=w1_hi[:, 2:4, 256:384])
         nc.sync.dma_start(out=raw_b2[:], in_=w1_hi[:, :, 384:512])
         nc.sync.dma_start(offsets[:], offs)
         nc.sync.dma_start(out=w2_raw[:], in_=w2_rows)
@@ -117,7 +120,7 @@ def tile_picked_shuffle_mlp_gelu_perm_l_kernel(tc, xT, w1, w2, offs, out):
         interleave(scopy, bf_x1[:], raw_x1, 0, 0, 128)
         quantize(x_codes[:, 128:256], x_scales[:, 128:256], bf_x1[:])
         interleave(vcopy, bf_b0[:], raw_b0, 0, 0, 128)
-        interleave(scopy, bf_b0s[:], raw_b0, 128, 0, 128)
+        interleave(scopy, bf_b0s[:], raw_b0s, 0, 0, 128)
         quantize(w1_codes[:, 512:640], w1_scales[:, 512:640], bf_b0[:])
         quantize(w1_codes[:, 640:768], w1_scales[:, 640:768], bf_b0s[:])
         pass_k(1, 0)

@@ -57,14 +57,13 @@ def tile_picked_shuffle_mlp_gelu_perm_l_kernel(tc, xT, w1, w2, offs, out):
         raw_b1 = keep.tile([P, PACK, 128], F32, name="raw_b1", align_bytes=512)
         raw_b2 = keep.tile([P, PACK, 128], F32, name="raw_b2", tag="h", align_bytes=512)
         w2_raw = keep.tile([P, PACK, N], F32, name="w2_raw", align_bytes=512)
-        nc.sync.dma_start(out=raw_x0[:], in_=xT[0:KP, :].rearrange("(p j) t -> p j t", j=PACK))
+        nc.scalar.dma_start(out=raw_x0[:], in_=xT[0:KP, :].rearrange("(p j) t -> p j t", j=PACK))
         nc.sync.dma_start(out=raw_a0[:], in_=w1_lo[:, :, 0:256])
         nc.sync.dma_start(out=raw_a1[:], in_=w1_lo[:, :, 256:512])
         nc.sync.dma_start(out=raw_x1[:], in_=xT[KP:K, :].rearrange("(p j) t -> p j t", j=PACK))
         nc.sync.dma_start(out=raw_b0[:], in_=w1_hi[:, :, 0:128])
         nc.sync.dma_start(out=raw_b0s[:], in_=w1_hi[:, :, 128:256])
-        nc.sync.dma_start(out=raw_b1[:, 0:2], in_=w1_hi[:, 0:2, 256:384])
-        nc.sync.dma_start(out=raw_b1[:, 2:4], in_=w1_hi[:, 2:4, 256:384])
+        nc.sync.dma_start(out=raw_b1[:], in_=w1_hi[:, :, 256:384])
         nc.sync.dma_start(out=raw_b2[:], in_=w1_hi[:, :, 384:512])
         nc.sync.dma_start(offsets[:], offs)
         nc.sync.dma_start(out=w2_raw[:], in_=w2_rows)

@@ -155,7 +155,7 @@ def tile_picked_shuffle_mlp_gelu_perm_l_kernel(tc, xT, w1, w2, offs, out):
         h_scales = keep.tile([P, T], U8, name="h_scales", align_bytes=512)
         quantize(h_codes[:], h_scales[:], h_bf[:])
 
-        for m, copy, dma in ((0, vcopy, nc.sync), (1, scopy, nc.scalar)):
+        for m, copy, dma in ((0, scopy, nc.scalar), (1, vcopy, nc.sync)):
             bank = psum.tile([P, 512], F32, name="out_bank%d" % m)
             cols = slice(P * m, P * (m + 1))
             nc.tensor.matmul_mx(

@@ -52,21 +52,21 @@ def tile_picked_shuffle_mlp_gelu_perm_l_kernel(tc, xT, w1, w2, offs, out):
         raw_x1 = keep.tile([P, PACK, T], F32, name="raw_x1", align_bytes=512)
         raw_a0 = keep.tile([P, PACK, 256], F32, name="raw_a0", align_bytes=512)
         raw_a1 = keep.tile([P, PACK, 256], F32, name="raw_a1", align_bytes=512)
-        raw_b0 = keep.tile([P, PACK, 128], F32, name="raw_b0", align_bytes=512)
-        raw_b0s = keep.tile([P, PACK, 128], F32, name="raw_b0s", align_bytes=512)
+        raw_b0 = keep.tile([P, PACK, 256], F32, name="raw_b0", align_bytes=512)
         raw_b1 = keep.tile([P, PACK, 128], F32, name="raw_b1", align_bytes=512)
         raw_b2 = keep.tile([P, PACK, 128], F32, name="raw_b2", tag="h", align_bytes=512)
-        w2_raw = keep.tile([P, PACK, N], F32, name="w2_raw", align_bytes=512)
+        w2_raw0 = keep.tile([P, PACK, P], F32, name="w2_raw0", align_bytes=512)
+        w2_raw1 = keep.tile([P, PACK, P], F32, name="w2_raw1", align_bytes=512)
         nc.scalar.dma_start(out=raw_x0[:], in_=xT[0:KP, :].rearrange("(p j) t -> p j t", j=PACK))
         nc.sync.dma_start(out=raw_a0[:], in_=w1_lo[:, :, 0:256])
         nc.sync.dma_start(out=raw_a1[:], in_=w1_lo[:, :, 256:512])
         nc.sync.dma_start(out=raw_x1[:], in_=xT[KP:K, :].rearrange("(p j) t -> p j t", j=PACK))
-        nc.sync.dma_start(out=raw_b0[:], in_=w1_hi[:, :, 0:128])
-        nc.sync.dma_start(out=raw_b0s[:], in_=w1_hi[:, :, 128:256])
+        nc.sync.dma_start(out=raw_b0[:], in_=w1_hi[:, :, 0:256])
         nc.sync.dma_start(out=raw_b1[:], in_=w1_hi[:, :, 256:384])
         nc.sync.dma_start(out=raw_b2[:], in_=w1_hi[:, :, 384:512])
         nc.sync.dma_start(offsets[:], offs)
-        nc.sync.dma_start(out=w2_raw[:], in_=w2_rows)
+        nc.sync.dma_start(out=w2_raw0[:], in_=w2_rows[:, :, 0:P])
+        nc.sync.dma_start(out=w2_raw1[:], in_=w2_rows[:, :, P:N])
 
         warm = keep.tile([P, 1], F32, name="warm")
         warm_out = keep.tile([P, 1], F32, name="warm_out")
@@ -83,7 +83,7 @@ def tile_picked_shuffle_mlp_gelu_perm_l_kernel(tc, xT, w1, w2, offs, out):
         bf_b0 = keep.tile([P, 128 * PACK], BF16, name="bf_b0", align_bytes=512)
         bf_b0s = keep.tile([P, 128 * PACK], BF16, name="bf_b0s", align_bytes=512)
         bf_b1 = keep.tile([P, 128 * PACK], BF16, name="bf_b1", align_bytes=512)
-        bf_b2 = keep.tile([P, 128 * PACK], BF16, name="bf_b2", align_bytes=512)
+        bf_b2 = keep.tile([P, 128 * PACK], BF16, name="bf_b2", tag="last", align_bytes=512)
         x_codes = keep.tile([P, 2 * T], U32, name="x_codes", align_bytes=512)
         x_scales = keep.tile([P, 2 * T], U8, name="x_scales", align_bytes=512)
         w1_codes = keep.tile([P, 2 * H], U32, name="w1_codes", align_bytes=512)
@@ -119,7 +119,7 @@ def tile_picked_shuffle_mlp_gelu_perm_l_kernel(tc, xT, w1, w2, offs, out):
         interleave(scopy, bf_x1[:], raw_x1, 0, 0, 128)
         quantize(x_codes[:, 128:256], x_scales[:, 128:256], bf_x1[:])
         interleave(vcopy, bf_b0[:], raw_b0, 0, 0, 128)
-        interleave(scopy, bf_b0s[:], raw_b0s, 0, 0, 128)
+        interleave(scopy, bf_b0s[:], raw_b0, 128, 0, 128)
         quantize(w1_codes[:, 512:640], w1_scales[:, 512:640], bf_b0[:])
         quantize(w1_codes[:, 640:768], w1_scales[:, 640:768], bf_b0s[:])
         pass_k(1, 0)
@@ -132,6 +132,9 @@ def tile_picked_shuffle_mlp_gelu_perm_l_kernel(tc, xT, w1, w2, offs, out):
 
         w2_codes = keep.tile([P, N], U32, name="w2_codes", align_bytes=512)
         w2_scales = keep.tile([P, N], U8, name="w2_scales", align_bytes=512)
+        w2_bf0 = keep.tile([P, P * PACK], BF16, name="w2_bf0", tag="last", align_bytes=512)
+        interleave(vcopy, w2_bf0[:], w2_raw0, 0, 0, P)
+        quantize(w2_codes[:, 0:P], w2_scales[:, 0:P], w2_bf0[:])
         hb = keep.tile([P, H], BF16, name="hb", tag="h", align_bytes=512)
         for index, (c0, width) in enumerate(PIECES):
             nc.scalar.activation(hb[:, c0 : c0 + width], acc[index][:, 0:width], GELU)
@@ -140,10 +143,9 @@ def tile_picked_shuffle_mlp_gelu_perm_l_kernel(tc, xT, w1, w2, offs, out):
         nc.vector.tensor_copy(out=g_bf[:, 0 : 16 * 18], in_=hb[:].indirect(offsets[:, 0:18]))
         nc.scalar.activation(g_bf[:, 16 * 18 : H], hb[:].indirect(offsets[:, 18:32]), COPY)
 
-        w2_bf = keep.tile([P, N * PACK], BF16, name="w2_bf", tag="h", align_bytes=512)
-        interleave(vcopy, w2_bf[:], w2_raw, 0, 0, 192)
-        interleave(scopy, w2_bf[:], w2_raw, 0, 192, N)
-        quantize(w2_codes[:], w2_scales[:], w2_bf[:])
+        w2_bf1 = keep.tile([P, P * PACK], BF16, name="w2_bf1", tag="h", align_bytes=512)
+        interleave(vcopy, w2_bf1[:], w2_raw1, 0, 0, P)
+        quantize(w2_codes[:, P:N], w2_scales[:, P:N], w2_bf1[:])
 
         words = g_bf[:].bitcast(F32)
         turned = psum.tile([P, 2, P], F32, name="turned")

@@ -151,11 +151,13 @@ def tile_picked_shuffle_mlp_gelu_perm_l_kernel(tc, xT, w1, w2, offs, out):
         turned = psum.tile([P, 2, P], F32, name="turned")
         for u in range(2):
             nc.tensor.transpose(turned[:, u, :], words[:, u : 2 * P : 2], ident[:])
-        h_bf = keep.tile([P, T * PACK], BF16, name="h_bf", align_bytes=512)
-        nc.scalar.copy(h_bf[:].bitcast(F32).rearrange("p (t u) -> p t u", u=2), turned[:].rearrange("p u t -> p t u"))
         h_codes = keep.tile([P, T], U32, name="h_codes", align_bytes=512)
         h_scales = keep.tile([P, T], U8, name="h_scales", align_bytes=512)
-        quantize(h_codes[:], h_scales[:], h_bf[:])
+        for half in range(2):
+            tokens = slice(half * T // 2, (half + 1) * T // 2)
+            h_bf = keep.tile([P, T // 2 * PACK], BF16, name="h_bf%d" % half, align_bytes=512)
+            nc.scalar.copy(h_bf[:].bitcast(F32).rearrange("p (t u) -> p t u", u=2), turned[:, :, tokens].rearrange("p u t -> p t u"))
+            quantize(h_codes[:, tokens], h_scales[:, tokens], h_bf[:])
 
         for m, copy, dma in ((0, scopy, nc.scalar), (1, vcopy, nc.sync)):
             bank = psum.tile([P, 512], F32, name="out_bank%d" % m)

@@ -52,7 +52,8 @@ def tile_picked_shuffle_mlp_gelu_perm_l_kernel(tc, xT, w1, w2, offs, out):
         raw_x1 = keep.tile([P, PACK, T], F32, name="raw_x1", align_bytes=512)
         raw_a0 = keep.tile([P, PACK, 256], F32, name="raw_a0", align_bytes=512)
         raw_a1 = keep.tile([P, PACK, 256], F32, name="raw_a1", align_bytes=512)
-        raw_b0 = keep.tile([P, PACK, 256], F32, name="raw_b0", align_bytes=512)
+        raw_b0 = keep.tile([P, PACK, 128], F32, name="raw_b0", align_bytes=512)
+        raw_b0s = keep.tile([P, PACK, 128], F32, name="raw_b0s", align_bytes=512)
         raw_b1 = keep.tile([P, PACK, 128], F32, name="raw_b1", align_bytes=512)
         raw_b2 = keep.tile([P, PACK, 128], F32, name="raw_b2", tag="h", align_bytes=512)
         w2_raw0 = keep.tile([P, PACK, P], F32, name="w2_raw0", align_bytes=512)
@@ -61,8 +62,10 @@ def tile_picked_shuffle_mlp_gelu_perm_l_kernel(tc, xT, w1, w2, offs, out):
         nc.sync.dma_start(out=raw_a0[:], in_=w1_lo[:, :, 0:256])
         nc.sync.dma_start(out=raw_a1[:], in_=w1_lo[:, :, 256:512])
         nc.sync.dma_start(out=raw_x1[:], in_=xT[KP:K, :].rearrange("(p j) t -> p j t", j=PACK))
-        nc.sync.dma_start(out=raw_b0[:], in_=w1_hi[:, :, 0:256])
-        nc.sync.dma_start(out=raw_b1[:], in_=w1_hi[:, :, 256:384])
+        nc.sync.dma_start(out=raw_b0[:], in_=w1_hi[:, :, 0:128])
+        nc.sync.dma_start(out=raw_b0s[:], in_=w1_hi[:, :, 128:256])
+        nc.sync.dma_start(out=raw_b1[:, 0:2], in_=w1_hi[:, 0:2, 256:384])
+        nc.sync.dma_start(out=raw_b1[:, 2:4], in_=w1_hi[:, 2:4, 256:384])
         nc.sync.dma_start(out=raw_b2[:], in_=w1_hi[:, :, 384:512])
         nc.sync.dma_start(offsets[:], offs)
         nc.sync.dma_start(out=w2_raw0[:], in_=w2_rows[:, :, 0:P])
@@ -119,7 +122,7 @@ def tile_picked_shuffle_mlp_gelu_perm_l_kernel(tc, xT, w1, w2, offs, out):
         interleave(scopy, bf_x1[:], raw_x1, 0, 0, 128)
         quantize(x_codes[:, 128:256], x_scales[:, 128:256], bf_x1[:])
         interleave(vcopy, bf_b0[:], raw_b0, 0, 0, 128)
-        interleave(scopy, bf_b0s[:], raw_b0, 128, 0, 128)
+        interleave(scopy, bf_b0s[:], raw_b0s, 0, 0, 128)
         quantize(w1_codes[:, 512:640], w1_scales[:, 512:640], bf_b0[:])
         quantize(w1_codes[:, 640:768], w1_scales[:, 640:768], bf_b0s[:])
         pass_k(1, 0)

@@ -116,13 +116,13 @@ def tile_picked_shuffle_mlp_gelu_perm_l_kernel(tc, xT, w1, w2, offs, out):
         pass_k(0, 0)
         interleave(vcopy, bf_a1[:], raw_a1, 0, 0, 128)
         interleave(scopy, bf_a1[:], raw_a1, 0, 128, 256)
+        interleave(vcopy, bf_x1[:], raw_x1, 0, 0, 128)
         quantize(w1_codes[:, 256:512], w1_scales[:, 256:512], bf_a1[:])
         pass_k(0, 1)
         pass_k(0, 2)
-        interleave(scopy, bf_x1[:], raw_x1, 0, 0, 128)
         quantize(x_codes[:, 128:256], x_scales[:, 128:256], bf_x1[:])
-        interleave(vcopy, bf_b0[:], raw_b0, 0, 0, 128)
-        interleave(scopy, bf_b0s[:], raw_b0s, 0, 0, 128)
+        interleave(scopy, bf_b0[:], raw_b0, 0, 0, 128)
+        interleave(vcopy, bf_b0s[:], raw_b0s, 0, 0, 128)
         quantize(w1_codes[:, 512:640], w1_scales[:, 512:640], bf_b0[:])
         quantize(w1_codes[:, 640:768], w1_scales[:, 640:768], bf_b0s[:])
         pass_k(1, 0)

@@ -17,163 +17,154 @@ COPY = mybir.ActivationFunctionType.Copy
 
 P = 128
 PACK = 4
-KP = 512
-
-PIECES = ((0, 256), (256, 128), (384, 128))
+KP = P * PACK
+W = 128
+ALIGN = 512
+GROUPS = ((0, 256), (256, 128), (384, 128))
+VECTOR_LIST_COLUMNS = 18
 
 
 def tile_picked_shuffle_mlp_gelu_perm_l_kernel(tc, xT, w1, w2, offs, out):
     nc = tc.nc
 
-    def vcopy(dst, src):
+    def vector_copy(dst, src):
         nc.vector.tensor_copy(out=dst, in_=src)
 
-    def scopy(dst, src):
+    def scalar_copy(dst, src):
         nc.scalar.copy(dst, src)
 
-    def interleave(copy, dst, raw, first, c0, c1):
+    def cast(copy, grouped, raw):
         copy(
-            dst[:, PACK * c0 : PACK * c1].rearrange("p (c i j) -> p c j i", i=2, j=PACK),
-            raw[:, :, first + c0 : first + c1].rearrange("p j (c i) -> p c j i", i=2),
+            grouped.rearrange("p (c i j) -> p c j i", i=2, j=PACK),
+            raw.rearrange("p j (c i) -> p c j i", i=2),
         )
 
     def quantize(codes, scales, grouped):
         nc.vector.quantize_mx(out=codes.bitcast(FP8X4), scales=scales, in_=grouped)
 
+    def product(acc, lhs_codes, lhs_scales, rhs_codes, rhs_scales, start, stop):
+        nc.tensor.matmul_mx(
+            out=acc,
+            lhsT=lhs_codes.bitcast(FP8X4),
+            lhsT_scale=lhs_scales,
+            rhs=rhs_codes.bitcast(FP8X4),
+            rhs_scale=rhs_scales,
+            start=start,
+            stop=stop,
+        )
+
     with ExitStack() as ctx:
         keep = ctx.enter_context(tc.tile_pool(name="keep", bufs=1))
         psum = ctx.enter_context(tc.psum_pool(name="psum", bufs=1))
 
+        def load(queue, name, rows, tag=None):
+            raw = keep.tile([P, PACK, rows.shape[1]], F32, name=name, tag=tag or name, align_bytes=ALIGN)
+            queue.dma_start(out=raw[:], in_=rows.rearrange("(p j) c -> p j c", j=PACK))
+            return raw
+
         offsets = keep.tile([P, H // 16], U16, name="offsets")
-        w1_lo = w1[0:KP, :].rearrange("(p j) c -> p j c", j=PACK)
-        w1_hi = w1[KP:K, :].rearrange("(p j) c -> p j c", j=PACK)
-        w2_rows = w2.rearrange("(p j) m -> p j m", j=PACK)
-        raw_x0 = keep.tile([P, PACK, T], F32, name="raw_x0", align_bytes=512)
-        raw_x1 = keep.tile([P, PACK, T], F32, name="raw_x1", align_bytes=512)
-        raw_a0 = keep.tile([P, PACK, 256], F32, name="raw_a0", align_bytes=512)
-        raw_a1 = keep.tile([P, PACK, 256], F32, name="raw_a1", align_bytes=512)
-        raw_b0 = keep.tile([P, PACK, 128], F32, name="raw_b0", align_bytes=512)
-        raw_b0s = keep.tile([P, PACK, 128], F32, name="raw_b0s", align_bytes=512)
-        raw_b1 = keep.tile([P, PACK, 128], F32, name="raw_b1", align_bytes=512)
-        raw_b2 = keep.tile([P, PACK, 128], F32, name="raw_b2", tag="h", align_bytes=512)
-        w2_raw0 = keep.tile([P, PACK, P], F32, name="w2_raw0", align_bytes=512)
-        w2_raw1 = keep.tile([P, PACK, P], F32, name="w2_raw1", align_bytes=512)
-        nc.scalar.dma_start(out=raw_x0[:], in_=xT[0:KP, :].rearrange("(p j) t -> p j t", j=PACK))
-        nc.sync.dma_start(out=raw_a0[:], in_=w1_lo[:, :, 0:256])
-        nc.sync.dma_start(out=raw_a1[:], in_=w1_lo[:, :, 256:512])
-        nc.sync.dma_start(out=raw_x1[:], in_=xT[KP:K, :].rearrange("(p j) t -> p j t", j=PACK))
-        nc.sync.dma_start(out=raw_b0[:], in_=w1_hi[:, :, 0:128])
-        nc.sync.dma_start(out=raw_b0s[:], in_=w1_hi[:, :, 128:256])
-        nc.sync.dma_start(out=raw_b1[:, 0:2], in_=w1_hi[:, 0:2, 256:384])
-        nc.sync.dma_start(out=raw_b1[:, 2:4], in_=w1_hi[:, 2:4, 256:384])
-        nc.sync.dma_start(out=raw_b2[:], in_=w1_hi[:, :, 384:512])
+        x_raw = [load(nc.scalar, "x_raw0", xT[0:KP, :])]
+        w1_wide = load(nc.sync, "w1_raw_wide", w1[0:KP, 0 : 2 * W])
+        w1_raw = {(0, 0): w1_wide[:, :, 0:W], (0, W): w1_wide[:, :, W : 2 * W]}
+        for c0 in range(2 * W, H, W):
+            w1_raw[0, c0] = load(nc.sync, "w1_raw0_%d" % c0, w1[0:KP, c0 : c0 + W])[:]
+        x_raw.append(load(nc.sync, "x_raw1", xT[KP:K, :]))
+        for c0 in range(0, H, W):
+            tag = "h" if c0 == H - W else None
+            w1_raw[1, c0] = load(nc.sync, "w1_raw1_%d" % c0, w1[KP:K, c0 : c0 + W], tag)[:]
         nc.sync.dma_start(offsets[:], offs)
-        nc.sync.dma_start(out=w2_raw0[:], in_=w2_rows[:, :, 0:P])
-        nc.sync.dma_start(out=w2_raw1[:], in_=w2_rows[:, :, P:N])
+        w2_raw = [load(nc.sync, "w2_raw%d" % m, w2[:, P * m : P * (m + 1)]) for m in range(2)]
 
         warm = keep.tile([P, 1], F32, name="warm")
         warm_out = keep.tile([P, 1], F32, name="warm_out")
         nc.vector.memset(warm[:], 0.0)
         nc.scalar.activation(warm_out[:], warm[:], GELU)
 
-        ident = keep.tile([P, P], F32, name="ident", align_bytes=512)
+        ident = keep.tile([P, P], F32, name="ident", align_bytes=ALIGN)
         make_identity(nc, ident[:])
 
-        bf_a0 = keep.tile([P, 256 * PACK], BF16, name="bf_a0", align_bytes=512)
-        bf_a1 = keep.tile([P, 256 * PACK], BF16, name="bf_a1", align_bytes=512)
-        bf_x0 = keep.tile([P, 128 * PACK], BF16, name="bf_x0", align_bytes=512)
-        bf_x1 = keep.tile([P, 128 * PACK], BF16, name="bf_x1", align_bytes=512)
-        bf_b0 = keep.tile([P, 128 * PACK], BF16, name="bf_b0", align_bytes=512)
-        bf_b0s = keep.tile([P, 128 * PACK], BF16, name="bf_b0s", align_bytes=512)
-        bf_b1 = keep.tile([P, 128 * PACK], BF16, name="bf_b1", align_bytes=512)
-        bf_b2 = keep.tile([P, 128 * PACK], BF16, name="bf_b2", tag="last", align_bytes=512)
-        x_codes = keep.tile([P, 2 * T], U32, name="x_codes", align_bytes=512)
-        x_scales = keep.tile([P, 2 * T], U8, name="x_scales", align_bytes=512)
-        w1_codes = keep.tile([P, 2 * H], U32, name="w1_codes", align_bytes=512)
-        w1_scales = keep.tile([P, 2 * H], U8, name="w1_scales", align_bytes=512)
+        x_codes = keep.tile([P, 2 * T], U32, name="x_codes", align_bytes=ALIGN)
+        x_scales = keep.tile([P, 2 * T], U8, name="x_scales", align_bytes=ALIGN)
+        w1_codes = keep.tile([P, 2 * H], U32, name="w1_codes", align_bytes=ALIGN)
+        w1_scales = keep.tile([P, 2 * H], U8, name="w1_scales", align_bytes=ALIGN)
+        acc = [psum.tile([P, 512], F32, name="acc%d" % c0) for c0, width in GROUPS]
 
-        acc = [psum.tile([P, 512], F32, name="acc%d" % c0) for c0, width in PIECES]
+        pieces = [(x_raw[0][:], x_codes, x_scales, 0)]
+        pieces += [(w1_raw[0, c0], w1_codes, w1_scales, c0) for c0 in range(0, H, W)]
+        pieces += [(x_raw[1][:], x_codes, x_scales, T)]
+        pieces += [(w1_raw[1, c0], w1_codes, w1_scales, H + c0) for c0 in range(0, H, W)]
+        passes_after = {}
+        for g in range(2):
+            for index, (c0, width) in enumerate(GROUPS):
+                last_piece = g * (len(pieces) // 2) + (c0 + width) // W
+                passes_after.setdefault(last_piece, []).append((g, index))
 
-        def pass_k(g, index):
-            c0, width = PIECES[index]
-            cols = slice(g * H + c0, g * H + c0 + width)
-            nc.tensor.matmul_mx(
-                out=acc[index][:, 0:width],
-                lhsT=x_codes[:, g * T : (g + 1) * T].bitcast(FP8X4),
-                lhsT_scale=x_scales[:, g * T : (g + 1) * T],
-                rhs=w1_codes[:, cols].bitcast(FP8X4),
-                rhs_scale=w1_scales[:, cols],
-                start=(g == 0),
-                stop=(g == 1),
-            )
+        for first in range(0, len(pieces), 2):
+            grouped = []
+            for number, copy in ((first, scalar_copy), (first + 1, vector_copy)):
+                tag = "last" if number == len(pieces) - 1 else "grouped%d" % number
+                tile = keep.tile([P, W * PACK], BF16, name="grouped%d" % number, tag=tag, align_bytes=ALIGN)
+                cast(copy, tile[:], pieces[number][0])
+                grouped.append((number, tile))
+            for number, tile in grouped:
+                raw, codes, scales, c0 = pieces[number]
+                quantize(codes[:, c0 : c0 + W], scales[:, c0 : c0 + W], tile[:])
+                for g, index in passes_after.get(number, []):
+                    h0, width = GROUPS[index]
+                    tokens = slice(g * T, (g + 1) * T)
+                    channels = slice(g * H + h0, g * H + h0 + width)
+                    product(
+                        acc[index][:, 0:width],
+                        x_codes[:, tokens],
+                        x_scales[:, tokens],
+                        w1_codes[:, channels],
+                        w1_scales[:, channels],
+                        start=(g == 0),
+                        stop=(g == 1),
+                    )
 
-        interleave(vcopy, bf_x0[:], raw_x0, 0, 0, 64)
-        interleave(scopy, bf_x0[:], raw_x0, 0, 64, 128)
-        quantize(x_codes[:, 0:128], x_scales[:, 0:128], bf_x0[:])
-        interleave(vcopy, bf_a0[:], raw_a0, 0, 0, 128)
-        interleave(scopy, bf_a0[:], raw_a0, 0, 128, 256)
-        quantize(w1_codes[:, 0:256], w1_scales[:, 0:256], bf_a0[:])
-        pass_k(0, 0)
-        interleave(vcopy, bf_a1[:], raw_a1, 0, 0, 128)
-        interleave(scopy, bf_a1[:], raw_a1, 0, 128, 256)
-        interleave(vcopy, bf_x1[:], raw_x1, 0, 0, 128)
-        quantize(w1_codes[:, 256:512], w1_scales[:, 256:512], bf_a1[:])
-        pass_k(0, 1)
-        pass_k(0, 2)
-        quantize(x_codes[:, 128:256], x_scales[:, 128:256], bf_x1[:])
-        interleave(scopy, bf_b0[:], raw_b0, 0, 0, 128)
-        interleave(vcopy, bf_b0s[:], raw_b0s, 0, 0, 128)
-        quantize(w1_codes[:, 512:640], w1_scales[:, 512:640], bf_b0[:])
-        quantize(w1_codes[:, 640:768], w1_scales[:, 640:768], bf_b0s[:])
-        pass_k(1, 0)
-        interleave(scopy, bf_b1[:], raw_b1, 0, 0, 128)
-        interleave(vcopy, bf_b2[:], raw_b2, 0, 0, 128)
-        quantize(w1_codes[:, 768:896], w1_scales[:, 768:896], bf_b1[:])
-        pass_k(1, 1)
-        quantize(w1_codes[:, 896:1024], w1_scales[:, 896:1024], bf_b2[:])
-        pass_k(1, 2)
+        w2_codes = keep.tile([P, N], U32, name="w2_codes", align_bytes=ALIGN)
+        w2_scales = keep.tile([P, N], U8, name="w2_scales", align_bytes=ALIGN)
 
-        w2_codes = keep.tile([P, N], U32, name="w2_codes", align_bytes=512)
-        w2_scales = keep.tile([P, N], U8, name="w2_scales", align_bytes=512)
-        w2_bf0 = keep.tile([P, P * PACK], BF16, name="w2_bf0", tag="last", align_bytes=512)
-        interleave(vcopy, w2_bf0[:], w2_raw0, 0, 0, P)
-        quantize(w2_codes[:, 0:P], w2_scales[:, 0:P], w2_bf0[:])
-        hb = keep.tile([P, H], BF16, name="hb", tag="h", align_bytes=512)
-        for index, (c0, width) in enumerate(PIECES):
-            nc.scalar.activation(hb[:, c0 : c0 + width], acc[index][:, 0:width], GELU)
+        def prepare_w2(m, tag):
+            grouped = keep.tile([P, P * PACK], BF16, name="w2_grouped%d" % m, tag=tag, align_bytes=ALIGN)
+            cast(vector_copy, grouped[:], w2_raw[m][:])
+            outputs = slice(P * m, P * (m + 1))
+            quantize(w2_codes[:, outputs], w2_scales[:, outputs], grouped[:])
 
-        g_bf = keep.tile([P, H], BF16, name="g_bf", align_bytes=512)
-        nc.vector.tensor_copy(out=g_bf[:, 0 : 16 * 18], in_=hb[:].indirect(offsets[:, 0:18]))
-        nc.scalar.activation(g_bf[:, 16 * 18 : H], hb[:].indirect(offsets[:, 18:32]), COPY)
+        prepare_w2(0, "last")
 
-        w2_bf1 = keep.tile([P, P * PACK], BF16, name="w2_bf1", tag="h", align_bytes=512)
-        interleave(vcopy, w2_bf1[:], w2_raw1, 0, 0, P)
-        quantize(w2_codes[:, P:N], w2_scales[:, P:N], w2_bf1[:])
+        h = keep.tile([P, H], BF16, name="h", tag="h", align_bytes=ALIGN)
+        for index, (c0, width) in enumerate(GROUPS):
+            nc.scalar.activation(h[:, c0 : c0 + width], acc[index][:, 0:width], GELU)
 
-        words = g_bf[:].bitcast(F32)
+        gathered = keep.tile([P, H], BF16, name="gathered", align_bytes=ALIGN)
+        split = VECTOR_LIST_COLUMNS
+        nc.vector.tensor_copy(out=gathered[:, 0 : 16 * split], in_=h[:].indirect(offsets[:, 0:split]))
+        nc.scalar.activation(gathered[:, 16 * split : H], h[:].indirect(offsets[:, split : H // 16]), COPY)
+
+        prepare_w2(1, "h")
+
+        words = gathered[:].bitcast(F32)
         turned = psum.tile([P, 2, P], F32, name="turned")
         for u in range(2):
             nc.tensor.transpose(turned[:, u, :], words[:, u : 2 * P : 2], ident[:])
-        h_codes = keep.tile([P, T], U32, name="h_codes", align_bytes=512)
-        h_scales = keep.tile([P, T], U8, name="h_scales", align_bytes=512)
+
+        h_codes = keep.tile([P, T], U32, name="h_codes", align_bytes=ALIGN)
+        h_scales = keep.tile([P, T], U8, name="h_scales", align_bytes=ALIGN)
         for half in range(2):
             tokens = slice(half * T // 2, (half + 1) * T // 2)
-            h_bf = keep.tile([P, T // 2 * PACK], BF16, name="h_bf%d" % half, align_bytes=512)
-            nc.scalar.copy(h_bf[:].bitcast(F32).rearrange("p (t u) -> p t u", u=2), turned[:, :, tokens].rearrange("p u t -> p t u"))
-            quantize(h_codes[:, tokens], h_scales[:, tokens], h_bf[:])
-
-        for m, copy, dma in ((0, scopy, nc.scalar), (1, vcopy, nc.sync)):
-            bank = psum.tile([P, 512], F32, name="out_bank%d" % m)
-            cols = slice(P * m, P * (m + 1))
-            nc.tensor.matmul_mx(
-                out=bank[:, 0:T],
-                lhsT=w2_codes[:, cols].bitcast(FP8X4),
-                lhsT_scale=w2_scales[:, cols],
-                rhs=h_codes[:].bitcast(FP8X4),
-                rhs_scale=h_scales[:],
-                start=True,
-                stop=True,
+            grouped = keep.tile([P, T // 2 * PACK], BF16, name="h_grouped%d" % half, align_bytes=ALIGN)
+            scalar_copy(
+                grouped[:].bitcast(F32).rearrange("p (t u) -> p t u", u=2),
+                turned[:, :, tokens].rearrange("p u t -> p t u"),
             )
-            y = keep.tile([P, T], F32, name="y%d" % m, align_bytes=512)
+            quantize(h_codes[:, tokens], h_scales[:, tokens], grouped[:])
+
+        for m, copy, queue in ((0, scalar_copy, nc.scalar), (1, vector_copy, nc.sync)):
+            outputs = slice(P * m, P * (m + 1))
+            bank = psum.tile([P, 512], F32, name="out_bank%d" % m)
+            product(bank[:, 0:T], w2_codes[:, outputs], w2_scales[:, outputs], h_codes[:], h_scales[:], True, True)
+            y = keep.tile([P, T], F32, name="y%d" % m, align_bytes=ALIGN)
             copy(y[:], bank[:, 0:T])
-            dma.dma_start(out=out[cols, :], in_=y[:])
+            queue.dma_start(out=out[outputs, :], in_=y[:])

@@ -57,21 +57,24 @@ def tile_picked_shuffle_mlp_gelu_perm_l_kernel(tc, xT, w1, w2, offs, out):
         keep = ctx.enter_context(tc.tile_pool(name="keep", bufs=1))
         psum = ctx.enter_context(tc.psum_pool(name="psum", bufs=1))
 
-        def load(queue, name, rows, tag=None):
+        def load(queue, name, rows, tag=None, parts=1):
             raw = keep.tile([P, PACK, rows.shape[1]], F32, name=name, tag=tag or name, align_bytes=ALIGN)
-            queue.dma_start(out=raw[:], in_=rows.rearrange("(p j) c -> p j c", j=PACK))
+            dealt = rows.rearrange("(p j) c -> p j c", j=PACK)
+            for j in range(0, PACK, PACK // parts):
+                queue.dma_start(out=raw[:, j : j + PACK // parts], in_=dealt[:, j : j + PACK // parts])
             return raw
 
         offsets = keep.tile([P, H // 16], U16, name="offsets")
         x_raw = [load(nc.scalar, "x_raw0", xT[0:KP, :])]
-        w1_wide = load(nc.sync, "w1_raw_wide", w1[0:KP, 0 : 2 * W])
-        w1_raw = {(0, 0): w1_wide[:, :, 0:W], (0, W): w1_wide[:, :, W : 2 * W]}
-        for c0 in range(2 * W, H, W):
-            w1_raw[0, c0] = load(nc.sync, "w1_raw0_%d" % c0, w1[0:KP, c0 : c0 + W])[:]
+        w1_raw = {}
+        for c0 in range(0, H, 2 * W):
+            wide = load(nc.sync, "w1_raw0_%d" % c0, w1[0:KP, c0 : c0 + 2 * W])
+            w1_raw[0, c0], w1_raw[0, c0 + W] = wide[:, :, 0:W], wide[:, :, W : 2 * W]
         x_raw.append(load(nc.sync, "x_raw1", xT[KP:K, :]))
         for c0 in range(0, H, W):
             tag = "h" if c0 == H - W else None
-            w1_raw[1, c0] = load(nc.sync, "w1_raw1_%d" % c0, w1[KP:K, c0 : c0 + W], tag)[:]
+            parts = 2 if c0 == H - 2 * W else 1
+            w1_raw[1, c0] = load(nc.sync, "w1_raw1_%d" % c0, w1[KP:K, c0 : c0 + W], tag, parts)[:]
         nc.sync.dma_start(offsets[:], offs)
         w2_raw = [load(nc.sync, "w2_raw%d" % m, w2[:, P * m : P * (m + 1)]) for m in range(2)]
 

@@ -1,7 +1,6 @@
 from contextlib import ExitStack
 
 import concourse.mybir as mybir
-from concourse.masks import make_identity
 
 K, T, H, N = 1024, 128, 512, 256
 FLOPS = 2 * K * T * H + 2 * H * T * N
@@ -84,7 +83,17 @@ def tile_picked_shuffle_mlp_gelu_perm_l_kernel(tc, xT, w1, w2, offs, out):
         nc.scalar.activation(warm_out[:], warm[:], GELU)
 
         ident = keep.tile([P, P], F32, name="ident", align_bytes=ALIGN)
-        make_identity(nc, ident[:])
+        ones = keep.tile([P, 32], F32, name="ones", align_bytes=64)
+        column = keep.tile([P, 32], F32, name="column", align_bytes=64)
+        row = keep.tile([P, 32], F32, name="row", align_bytes=64)
+        nc.vector.memset(ones[:], 1.0)
+        nc.vector.memset(ident[:], 0.0)
+        nc.vector.tensor_tensor_scan(column[:], ones[:], ones[:], 0.0, mybir.AluOpType.mult, mybir.AluOpType.add)
+        nc.vector.transpose(row[:], column[:])
+        for q in range(0, P, 32):
+            nc.vector.tensor_tensor(
+                ident[q : q + 32, q : q + 32], column[q : q + 32, :], row[q : q + 32, :], mybir.AluOpType.is_equal
+            )
 
         x_codes = keep.tile([P, 2 * T], U32, name="x_codes", align_bytes=ALIGN)
         x_scales = keep.tile([P, 2 * T], U8, name="x_scales", align_bytes=ALIGN)

@@ -66,14 +66,13 @@ def tile_picked_shuffle_mlp_gelu_perm_l_kernel(tc, xT, w1, w2, offs, out):
         offsets = keep.tile([P, H // 16], U16, name="offsets")
         x_raw = [load(nc.scalar, "x_raw0", xT[0:KP, :])]
         w1_raw = {}
-        for c0 in range(0, H, 2 * W):
-            wide = load(nc.sync, "w1_raw0_%d" % c0, w1[0:KP, c0 : c0 + 2 * W])
-            w1_raw[0, c0], w1_raw[0, c0 + W] = wide[:, :, 0:W], wide[:, :, W : 2 * W]
+        for g, c0 in ((0, 0), (0, 2 * W), (1, 0)):
+            wide = load(nc.sync, "w1_raw%d_%d" % (g, c0), w1[g * KP : (g + 1) * KP, c0 : c0 + 2 * W], parts=2)
+            w1_raw[g, c0], w1_raw[g, c0 + W] = wide[:, :, 0:W], wide[:, :, W : 2 * W]
         x_raw.append(load(nc.sync, "x_raw1", xT[KP:K, :]))
-        for c0 in range(0, H, W):
+        for c0 in range(2 * W, H, W):
             tag = "h" if c0 == H - W else None
-            parts = 2 if c0 == H - 2 * W else 1
-            w1_raw[1, c0] = load(nc.sync, "w1_raw1_%d" % c0, w1[KP:K, c0 : c0 + W], tag, parts)[:]
+            w1_raw[1, c0] = load(nc.sync, "w1_raw1_%d" % c0, w1[KP:K, c0 : c0 + W], tag)[:]
         nc.sync.dma_start(offsets[:], offs)
         w2_raw = [load(nc.sync, "w2_raw%d" % m, w2[:, P * m : P * (m + 1)]) for m in range(2)]
 
@@ -103,8 +102,9 @@ def tile_picked_shuffle_mlp_gelu_perm_l_kernel(tc, xT, w1, w2, offs, out):
 
         pieces = [(x_raw[0][:], x_codes, x_scales, 0)]
         pieces += [(w1_raw[0, c0], w1_codes, w1_scales, c0) for c0 in range(0, H, W)]
+        pieces += [(w1_raw[1, c0], w1_codes, w1_scales, H + c0) for c0 in range(0, 2 * W, W)]
         pieces += [(x_raw[1][:], x_codes, x_scales, T)]
-        pieces += [(w1_raw[1, c0], w1_codes, w1_scales, H + c0) for c0 in range(0, H, W)]
+        pieces += [(w1_raw[1, c0], w1_codes, w1_scales, H + c0) for c0 in range(2 * W, H, W)]
         passes_after = {}
         for g in range(2):
             for index, (c0, width) in enumerate(GROUPS):
@@ -173,10 +173,24 @@ def tile_picked_shuffle_mlp_gelu_perm_l_kernel(tc, xT, w1, w2, offs, out):
             )
             quantize(h_codes[:, tokens], h_scales[:, tokens], grouped[:])
 
-        for m, copy, queue in ((0, scalar_copy, nc.scalar), (1, vector_copy, nc.sync)):
+        parts = (
+            (0, slice(0, T // 2), scalar_copy, nc.sync),
+            (1, slice(0, T), vector_copy, nc.sync),
+            (0, slice(T // 2, T), scalar_copy, nc.scalar),
+        )
+        for number, (m, tokens, copy, queue) in enumerate(parts):
             outputs = slice(P * m, P * (m + 1))
-            bank = psum.tile([P, 512], F32, name="out_bank%d" % m)
-            product(bank[:, 0:T], w2_codes[:, outputs], w2_scales[:, outputs], h_codes[:], h_scales[:], True, True)
-            y = keep.tile([P, T], F32, name="y%d" % m, align_bytes=ALIGN)
-            copy(y[:], bank[:, 0:T])
-            queue.dma_start(out=out[outputs, :], in_=y[:])
+            width = tokens.stop - tokens.start
+            bank = psum.tile([P, 512], F32, name="out_bank%d" % number)
+            product(
+                bank[:, 0:width],
+                w2_codes[:, outputs],
+                w2_scales[:, outputs],
+                h_codes[:, tokens],
+                h_scales[:, tokens],
+                True,
+                True,
+            )
+            y = keep.tile([P, width], F32, name="y%d" % number, align_bytes=ALIGN)
+            copy(y[:], bank[:, 0:width])
+            queue.dma_start(out=out[outputs, tokens], in_=y[:])

@@ -1,6 +1,7 @@
 from contextlib import ExitStack
 
 import concourse.mybir as mybir
+from concourse.masks import make_identity
 
 K, T, H, N = 1024, 128, 512, 256
 FLOPS = 2 * K * T * H + 2 * H * T * N
@@ -82,17 +83,7 @@ def tile_picked_shuffle_mlp_gelu_perm_l_kernel(tc, xT, w1, w2, offs, out):
         nc.scalar.activation(warm_out[:], warm[:], GELU)
 
         ident = keep.tile([P, P], F32, name="ident", align_bytes=ALIGN)
-        ones = keep.tile([P, 32], F32, name="ones", align_bytes=64)
-        column = keep.tile([P, 32], F32, name="column", align_bytes=64)
-        row = keep.tile([P, 32], F32, name="row", align_bytes=64)
-        nc.vector.memset(ones[:], 1.0)
-        nc.vector.memset(ident[:], 0.0)
-        nc.vector.tensor_tensor_scan(column[:], ones[:], ones[:], 0.0, mybir.AluOpType.mult, mybir.AluOpType.add)
-        nc.vector.transpose(row[:], column[:])
-        for q in range(0, P, 32):
-            nc.vector.tensor_tensor(
-                ident[q : q + 32, q : q + 32], column[q : q + 32, :], row[q : q + 32, :], mybir.AluOpType.is_equal
-            )
+        make_identity(nc, ident[:])
 
         x_codes = keep.tile([P, 2 * T], U32, name="x_codes", align_bytes=ALIGN)
         x_scales = keep.tile([P, 2 * T], U8, name="x_scales", align_bytes=ALIGN)

@@ -90,6 +90,15 @@ def tile_picked_shuffle_mlp_gelu_perm_l_kernel(tc, xT, w1, w2, offs, out):
         w1_codes = keep.tile([P, 2 * H], U32, name="w1_codes", align_bytes=ALIGN)
         w1_scales = keep.tile([P, 2 * H], U8, name="w1_scales", align_bytes=ALIGN)
         acc = [psum.tile([P, 512], F32, name="acc%d" % c0) for c0, width in GROUPS]
+        spare = psum.tile([P, 512], F32, name="spare")
+        turned = psum.tile([P, 4, P], F32, name="turned")
+        out_banks = [psum.tile([P, 512], F32, name="out_bank%d" % number) for number in range(3)]
+        ident16 = keep.tile([P, P], BF16, name="ident16", align_bytes=ALIGN)
+        make_identity(nc, ident16[:])
+
+        def fill(count, bank, source):
+            for i in range(count):
+                nc.tensor.transpose(bank.bitcast(BF16)[:, 256 * (i % 4) : 256 * (i % 4) + P], source, ident16[:])
 
         pieces = [(x_raw[0][:], x_codes, x_scales, 0)]
         pieces += [(w1_raw[0, c0], w1_codes, w1_scales, c0) for c0 in range(0, H, W)]
@@ -99,7 +108,7 @@ def tile_picked_shuffle_mlp_gelu_perm_l_kernel(tc, xT, w1, w2, offs, out):
         passes_after = {}
         for g in range(2):
             for index, (c0, width) in enumerate(GROUPS):
-                last_piece = g * (len(pieces) // 2) + (c0 + width) // W
+                last_piece = g * (len(pieces) // 2) + ((c0 + width) // W if g else H // W)
                 passes_after.setdefault(last_piece, []).append((g, index))
 
         for first in range(0, len(pieces), 2):
@@ -109,6 +118,9 @@ def tile_picked_shuffle_mlp_gelu_perm_l_kernel(tc, xT, w1, w2, offs, out):
                 tile = keep.tile([P, W * PACK], BF16, name="grouped%d" % number, tag=tag, align_bytes=ALIGN)
                 cast(copy, tile[:], pieces[number][0])
                 grouped.append((number, tile))
+                if number == 3:
+                    for bank, count in zip(acc + [spare], (8, 1, 1, 1)):
+                        fill(count, bank[:], tile[:, 0:P])
             for number, tile in grouped:
                 raw, codes, scales, c0 = pieces[number]
                 quantize(codes[:, c0 : c0 + W], scales[:, c0 : c0 + W], tile[:])
@@ -125,6 +137,10 @@ def tile_picked_shuffle_mlp_gelu_perm_l_kernel(tc, xT, w1, w2, offs, out):
                         start=(g == 0),
                         stop=(g == 1),
                     )
+                if number == 4:
+                    product(spare[:, 0:P], x_codes[:, 0:T], x_scales[:, 0:T], codes[:, c0 : c0 + W], scales[:, c0 : c0 + W], True, True)
+                if number == 9:
+                    fill(11, turned[:].rearrange("p a b -> p (a b)"), codes[:, c0 : c0 + W].bitcast(BF16)[:, 0:P])
 
         w2_codes = keep.tile([P, N], U32, name="w2_codes", align_bytes=ALIGN)
         w2_scales = keep.tile([P, N], U8, name="w2_scales", align_bytes=ALIGN)
@@ -149,9 +165,10 @@ def tile_picked_shuffle_mlp_gelu_perm_l_kernel(tc, xT, w1, w2, offs, out):
         prepare_w2(1, "h")
 
         words = gathered[:].bitcast(F32)
-        turned = psum.tile([P, 2, P], F32, name="turned")
         for u in range(2):
             nc.tensor.transpose(turned[:, u, :], words[:, u : 2 * P : 2], ident[:])
+        for bank, count in zip(out_banks, (3, 1, 1)):
+            fill(count, bank[:], gathered[:, 0:P])
 
         h_codes = keep.tile([P, T], U32, name="h_codes", align_bytes=ALIGN)
         h_scales = keep.tile([P, T], U8, name="h_scales", align_bytes=ALIGN)
@@ -160,7 +177,7 @@ def tile_picked_shuffle_mlp_gelu_perm_l_kernel(tc, xT, w1, w2, offs, out):
             grouped = keep.tile([P, T // 2 * PACK], BF16, name="h_grouped%d" % half, align_bytes=ALIGN)
             scalar_copy(
                 grouped[:].bitcast(F32).rearrange("p (t u) -> p t u", u=2),
-                turned[:, :, tokens].rearrange("p u t -> p t u"),
+                turned[:, 0:2, tokens].rearrange("p u t -> p t u"),
             )
             quantize(h_codes[:, tokens], h_scales[:, tokens], grouped[:])
 
@@ -172,7 +189,7 @@ def tile_picked_shuffle_mlp_gelu_perm_l_kernel(tc, xT, w1, w2, offs, out):
         for number, (m, tokens, copy, queue) in enumerate(parts):
             outputs = slice(P * m, P * (m + 1))
             width = tokens.stop - tokens.start
-            bank = psum.tile([P, 512], F32, name="out_bank%d" % number)
+            bank = out_banks[number]
             product(
                 bank[:, 0:width],
                 w2_codes[:, outputs],

@@ -105,11 +105,7 @@ def tile_picked_shuffle_mlp_gelu_perm_l_kernel(tc, xT, w1, w2, offs, out):
         pieces += [(w1_raw[1, c0], w1_codes, w1_scales, H + c0) for c0 in range(0, 2 * W, W)]
         pieces += [(x_raw[1][:], x_codes, x_scales, T)]
         pieces += [(w1_raw[1, c0], w1_codes, w1_scales, H + c0) for c0 in range(2 * W, H, W)]
-        passes_after = {}
-        for g in range(2):
-            for index, (c0, width) in enumerate(GROUPS):
-                last_piece = g * (len(pieces) // 2) + ((c0 + width) // W if g else H // W)
-                passes_after.setdefault(last_piece, []).append((g, index))
+        passes_after = {7: [(0, 0), (1, 0), (0, 1), (0, 2)], 8: [(1, 1)], 9: [(1, 2)]}
 
         for first in range(0, len(pieces), 2):
             grouped = []
@@ -137,10 +133,10 @@ def tile_picked_shuffle_mlp_gelu_perm_l_kernel(tc, xT, w1, w2, offs, out):
                         start=(g == 0),
                         stop=(g == 1),
                     )
-                if number == 4:
-                    product(spare[:, 0:P], x_codes[:, 0:T], x_scales[:, 0:T], codes[:, c0 : c0 + W], scales[:, c0 : c0 + W], True, True)
+                if number == 7:
+                    product(spare[:, 0:P], x_codes[:, 0:T], x_scales[:, 0:T], w1_codes[:, 0:W], w1_scales[:, 0:W], True, True)
                 if number == 9:
-                    fill(11, turned[:].rearrange("p a b -> p (a b)"), codes[:, c0 : c0 + W].bitcast(BF16)[:, 0:P])
+                    fill(10, turned[:].rearrange("p a b -> p (a b)"), codes[:, c0 : c0 + W].bitcast(BF16)[:, 0:P])
 
         w2_codes = keep.tile([P, N], U32, name="w2_codes", align_bytes=ALIGN)
         w2_scales = keep.tile([P, N], U8, name="w2_scales", align_bytes=ALIGN)

@@ -105,7 +105,7 @@ def tile_picked_shuffle_mlp_gelu_perm_l_kernel(tc, xT, w1, w2, offs, out):
         pieces += [(w1_raw[1, c0], w1_codes, w1_scales, H + c0) for c0 in range(0, 2 * W, W)]
         pieces += [(x_raw[1][:], x_codes, x_scales, T)]
         pieces += [(w1_raw[1, c0], w1_codes, w1_scales, H + c0) for c0 in range(2 * W, H, W)]
-        passes_after = {7: [(0, 0), (1, 0), (0, 1), (0, 2)], 8: [(1, 1)], 9: [(1, 2)]}
+        passes_after = {7: [(0, 0), (0, 1), (1, 0), (0, 2)], 8: [(1, 1)], 9: [(1, 2)]}
 
         for first in range(0, len(pieces), 2):
             grouped = []
@@ -136,7 +136,7 @@ def tile_picked_shuffle_mlp_gelu_perm_l_kernel(tc, xT, w1, w2, offs, out):
                 if number == 7:
                     product(spare[:, 0:P], x_codes[:, 0:T], x_scales[:, 0:T], w1_codes[:, 0:W], w1_scales[:, 0:W], True, True)
                 if number == 9:
-                    fill(10, turned[:].rearrange("p a b -> p (a b)"), codes[:, c0 : c0 + W].bitcast(BF16)[:, 0:P])
+                    fill(18, turned[:].rearrange("p a b -> p (a b)"), codes[:, c0 : c0 + W].bitcast(BF16)[:, 0:P])
 
         w2_codes = keep.tile([P, N], U32, name="w2_codes", align_bytes=ALIGN)
         w2_scales = keep.tile([P, N], U8, name="w2_scales", align_bytes=ALIGN)
@@ -163,7 +163,7 @@ def tile_picked_shuffle_mlp_gelu_perm_l_kernel(tc, xT, w1, w2, offs, out):
         words = gathered[:].bitcast(F32)
         for u in range(2):
             nc.tensor.transpose(turned[:, u, :], words[:, u : 2 * P : 2], ident[:])
-        for bank, count in zip(out_banks, (3, 1, 1)):
+        for bank, count in zip(out_banks, (6, 1, 1)):
             fill(count, bank[:], gathered[:, 0:P])
 
         h_codes = keep.tile([P, T], U32, name="h_codes", align_bytes=ALIGN)

@@ -105,7 +105,7 @@ def tile_picked_shuffle_mlp_gelu_perm_l_kernel(tc, xT, w1, w2, offs, out):
         pieces += [(w1_raw[1, c0], w1_codes, w1_scales, H + c0) for c0 in range(0, 2 * W, W)]
         pieces += [(x_raw[1][:], x_codes, x_scales, T)]
         pieces += [(w1_raw[1, c0], w1_codes, w1_scales, H + c0) for c0 in range(2 * W, H, W)]
-        passes_after = {7: [(0, 0), (0, 1), (1, 0), (0, 2)], 8: [(1, 1)], 9: [(1, 2)]}
+        passes_after = {7: [(0, 0), (0, 1), (0, 2), (1, 0)], 8: [(1, 1)], 9: [(1, 2)]}
 
         for first in range(0, len(pieces), 2):
             grouped = []

@@ -96,9 +96,10 @@ def tile_picked_shuffle_mlp_gelu_perm_l_kernel(tc, xT, w1, w2, offs, out):
         ident16 = keep.tile([P, P], BF16, name="ident16", align_bytes=ALIGN)
         make_identity(nc, ident16[:])
 
-        def fill(count, bank, source):
+        def fill(count, banks, source):
             for i in range(count):
-                nc.tensor.transpose(bank.bitcast(BF16)[:, 256 * (i % 4) : 256 * (i % 4) + P], source, ident16[:])
+                bank = banks[(i - count) % len(banks)]
+                nc.tensor.transpose(bank.bitcast(BF16)[:, 0:P], source[:, 64 : 64 + P], ident16[:])
 
         pieces = [(x_raw[0][:], x_codes, x_scales, 0)]
         pieces += [(w1_raw[0, c0], w1_codes, w1_scales, c0) for c0 in range(0, H, W)]
@@ -115,8 +116,7 @@ def tile_picked_shuffle_mlp_gelu_perm_l_kernel(tc, xT, w1, w2, offs, out):
                 cast(copy, tile[:], pieces[number][0])
                 grouped.append((number, tile))
                 if number == 3:
-                    for bank, count in zip(acc + [spare], (8, 1, 1, 1)):
-                        fill(count, bank[:], tile[:, 0:P])
+                    fill(11, [bank[:] for bank in acc + [spare]], tile[:])
             for number, tile in grouped:
                 raw, codes, scales, c0 = pieces[number]
                 quantize(codes[:, c0 : c0 + W], scales[:, c0 : c0 + W], tile[:])
@@ -136,7 +136,7 @@ def tile_picked_shuffle_mlp_gelu_perm_l_kernel(tc, xT, w1, w2, offs, out):
                 if number == 7:
                     product(spare[:, 0:P], x_codes[:, 0:T], x_scales[:, 0:T], w1_codes[:, 0:W], w1_scales[:, 0:W], True, True)
                 if number == 9:
-                    fill(18, turned[:].rearrange("p a b -> p (a b)"), codes[:, c0 : c0 + W].bitcast(BF16)[:, 0:P])
+                    fill(21, [spare[:], turned[:].rearrange("p a b -> p (a b)")], codes[:, c0 : c0 + W].bitcast(BF16))
 
         w2_codes = keep.tile([P, N], U32, name="w2_codes", align_bytes=ALIGN)
         w2_scales = keep.tile([P, N], U8, name="w2_scales", align_bytes=ALIGN)
@@ -163,8 +163,7 @@ def tile_picked_shuffle_mlp_gelu_perm_l_kernel(tc, xT, w1, w2, offs, out):
         words = gathered[:].bitcast(F32)
         for u in range(2):
             nc.tensor.transpose(turned[:, u, :], words[:, u : 2 * P : 2], ident[:])
-        for bank, count in zip(out_banks, (6, 1, 1)):
-            fill(count, bank[:], gathered[:, 0:P])
+        fill(9, [bank[:] for bank in out_banks], gathered[:])
 
         h_codes = keep.tile([P, T], U32, name="h_codes", align_bytes=ALIGN)
         h_scales = keep.tile([P, T], U8, name="h_scales", align_bytes=ALIGN)

@@ -116,7 +116,7 @@ def tile_picked_shuffle_mlp_gelu_perm_l_kernel(tc, xT, w1, w2, offs, out):
                 cast(copy, tile[:], pieces[number][0])
                 grouped.append((number, tile))
                 if number == 3:
-                    fill(11, [bank[:] for bank in acc + [spare]], tile[:])
+                    fill(15, [bank[:] for bank in acc + [spare]], tile[:])
             for number, tile in grouped:
                 raw, codes, scales, c0 = pieces[number]
                 quantize(codes[:, c0 : c0 + W], scales[:, c0 : c0 + W], tile[:])

@@ -163,7 +163,7 @@ def tile_picked_shuffle_mlp_gelu_perm_l_kernel(tc, xT, w1, w2, offs, out):
         words = gathered[:].bitcast(F32)
         for u in range(2):
             nc.tensor.transpose(turned[:, u, :], words[:, u : 2 * P : 2], ident[:])
-        fill(9, [bank[:] for bank in out_banks], gathered[:])
+        fill(12, [bank[:] for bank in out_banks], gathered[:])
 
         h_codes = keep.tile([P, T], U32, name="h_codes", align_bytes=ALIGN)
         h_scales = keep.tile([P, T], U8, name="h_scales", align_bytes=ALIGN)

@@ -116,7 +116,7 @@ def tile_picked_shuffle_mlp_gelu_perm_l_kernel(tc, xT, w1, w2, offs, out):
                 cast(copy, tile[:], pieces[number][0])
                 grouped.append((number, tile))
                 if number == 3:
-                    fill(15, [bank[:] for bank in acc + [spare]], tile[:])
+                    fill(14, [bank[:] for bank in acc + [spare]], tile[:])
             for number, tile in grouped:
                 raw, codes, scales, c0 = pieces[number]
                 quantize(codes[:, c0 : c0 + W], scales[:, c0 : c0 + W], tile[:])

@@ -136,7 +136,7 @@ def tile_picked_shuffle_mlp_gelu_perm_l_kernel(tc, xT, w1, w2, offs, out):
                 if number == 7:
                     product(spare[:, 0:P], x_codes[:, 0:T], x_scales[:, 0:T], w1_codes[:, 0:W], w1_scales[:, 0:W], True, True)
                 if number == 9:
-                    fill(21, [spare[:], turned[:].rearrange("p a b -> p (a b)")], codes[:, c0 : c0 + W].bitcast(BF16))
+                    fill(20, [spare[:], turned[:].rearrange("p a b -> p (a b)")], codes[:, c0 : c0 + W].bitcast(BF16))
 
         w2_codes = keep.tile([P, N], U32, name="w2_codes", align_bytes=ALIGN)
         w2_scales = keep.tile([P, N], U8, name="w2_scales", align_bytes=ALIGN)
@@ -161,6 +161,7 @@ def tile_picked_shuffle_mlp_gelu_perm_l_kernel(tc, xT, w1, w2, offs, out):
         prepare_w2(1, "h")
 
         words = gathered[:].bitcast(F32)
+        fill(1, [spare[:]], gathered[:, H - 192 : H])
         for u in range(2):
             nc.tensor.transpose(turned[:, u, :], words[:, u : 2 * P : 2], ident[:])
         fill(12, [bank[:] for bank in out_banks], gathered[:])

@@ -164,6 +164,7 @@ def tile_picked_shuffle_mlp_gelu_perm_l_kernel(tc, xT, w1, w2, offs, out):
         fill(1, [spare[:]], gathered[:, H - 192 : H])
         for u in range(2):
             nc.tensor.transpose(turned[:, u, :], words[:, u : 2 * P : 2], ident[:])
+        out_banks.append(acc[0])
         fill(12, [bank[:] for bank in out_banks], gathered[:])
 
         h_codes = keep.tile([P, T], U32, name="h_codes", align_bytes=ALIGN)
@@ -177,24 +178,21 @@ def tile_picked_shuffle_mlp_gelu_perm_l_kernel(tc, xT, w1, w2, offs, out):
             )
             quantize(h_codes[:, tokens], h_scales[:, tokens], grouped[:])
 
-        parts = (
-            (0, slice(0, T // 2), scalar_copy, nc.sync),
-            (1, slice(0, T), vector_copy, nc.sync),
-            (0, slice(T // 2, T), scalar_copy, nc.scalar),
-        )
-        for number, (m, tokens, copy, queue) in enumerate(parts):
-            outputs = slice(P * m, P * (m + 1))
-            width = tokens.stop - tokens.start
-            bank = out_banks[number]
-            product(
-                bank[:, 0:width],
-                w2_codes[:, outputs],
-                w2_scales[:, outputs],
-                h_codes[:, tokens],
-                h_scales[:, tokens],
-                True,
-                True,
-            )
-            y = keep.tile([P, width], F32, name="y%d" % number, align_bytes=ALIGN)
-            copy(y[:], bank[:, 0:width])
-            queue.dma_start(out=out[outputs, tokens], in_=y[:])
+        rows = out.rearrange("(m p) t -> p m t", p=P)
+        for half in range(2):
+            tokens = slice(half * T // 2, (half + 1) * T // 2)
+            y = keep.tile([P, 2, T // 2], F32, name="y%d" % half, align_bytes=ALIGN)
+            for m, copy in ((0, scalar_copy), (1, vector_copy)):
+                outputs = slice(P * m, P * (m + 1))
+                bank = out_banks[2 * half + m]
+                product(
+                    bank[:, 0 : T // 2],
+                    w2_codes[:, outputs],
+                    w2_scales[:, outputs],
+                    h_codes[:, tokens],
+                    h_scales[:, tokens],
+                    True,
+                    True,
+                )
+                copy(y[:, m, :], bank[:, 0 : T // 2])
+            nc.sync.dma_start(out=rows[:, :, tokens], in_=y[:])

@@ -178,10 +178,9 @@ def tile_picked_shuffle_mlp_gelu_perm_l_kernel(tc, xT, w1, w2, offs, out):
             )
             quantize(h_codes[:, tokens], h_scales[:, tokens], grouped[:])
 
-        rows = out.rearrange("(m p) t -> p m t", p=P)
+        y = [keep.tile([P, T], F32, name="y%d" % m, align_bytes=ALIGN) for m in range(2)]
         for half in range(2):
             tokens = slice(half * T // 2, (half + 1) * T // 2)
-            y = keep.tile([P, 2, T // 2], F32, name="y%d" % half, align_bytes=ALIGN)
             for m, copy in ((0, scalar_copy), (1, vector_copy)):
                 outputs = slice(P * m, P * (m + 1))
                 bank = out_banks[2 * half + m]
@@ -194,5 +193,8 @@ def tile_picked_shuffle_mlp_gelu_perm_l_kernel(tc, xT, w1, w2, offs, out):
                     True,
                     True,
                 )
-                copy(y[:, m, :], bank[:, 0 : T // 2])
-            nc.sync.dma_start(out=rows[:, :, tokens], in_=y[:])
+                copy(y[m][:, tokens], bank[:, 0 : T // 2])
+                if m == 0:
+                    queue = nc.scalar if half else nc.sync
+                    queue.dma_start(out=out[outputs, tokens], in_=y[m][:, tokens])
+        nc.sync.dma_start(out=out[P:N, :], in_=y[1][:])

@@ -18,10 +18,12 @@ COPY = mybir.ActivationFunctionType.Copy
 P = 128
 PACK = 4
 KP = P * PACK
-W = 128
 ALIGN = 512
 GROUPS = ((0, 256), (256, 128), (384, 128))
 VECTOR_LIST_COLUMNS = 18
+FIRST_ON_VECTOR = 320
+WIDE_ON_VECTOR = 64
+WARM_BEFORE, WARM_GATHER, WARM_COPY = 18, 20, 12
 
 
 def tile_picked_shuffle_mlp_gelu_perm_l_kernel(tc, xT, w1, w2, offs, out):
@@ -33,22 +35,25 @@ def tile_picked_shuffle_mlp_gelu_perm_l_kernel(tc, xT, w1, w2, offs, out):
     def scalar_copy(dst, src):
         nc.scalar.copy(dst, src)
 
-    def cast(copy, grouped, raw):
+    def cast(copy, grouped, raw, c0, c1):
         copy(
-            grouped.rearrange("p (c i j) -> p c j i", i=2, j=PACK),
-            raw.rearrange("p j (c i) -> p c j i", i=2),
+            grouped[:, PACK * c0 : PACK * c1].rearrange("p (c i j) -> p c j i", i=2, j=PACK),
+            raw[:, :, c0:c1].rearrange("p j (c i) -> p c j i", i=2),
         )
 
-    def quantize(codes, scales, grouped):
-        nc.vector.quantize_mx(out=codes.bitcast(FP8X4), scales=scales, in_=grouped)
+    def quantize(codes, scales, first, grouped, c0, c1):
+        columns = slice(first + c0, first + c1)
+        nc.vector.quantize_mx(
+            out=codes[:, columns].bitcast(FP8X4), scales=scales[:, columns], in_=grouped[:, PACK * c0 : PACK * c1]
+        )
 
-    def product(acc, lhs_codes, lhs_scales, rhs_codes, rhs_scales, start, stop):
+    def product(acc, lhs, lhs_columns, rhs, rhs_columns, start, stop):
         nc.tensor.matmul_mx(
             out=acc,
-            lhsT=lhs_codes.bitcast(FP8X4),
-            lhsT_scale=lhs_scales,
-            rhs=rhs_codes.bitcast(FP8X4),
-            rhs_scale=rhs_scales,
+            lhsT=lhs[0][:, lhs_columns].bitcast(FP8X4),
+            lhsT_scale=lhs[1][:, lhs_columns],
+            rhs=rhs[0][:, rhs_columns].bitcast(FP8X4),
+            rhs_scale=rhs[1][:, rhs_columns],
             start=start,
             stop=stop,
         )
@@ -64,16 +69,21 @@ def tile_picked_shuffle_mlp_gelu_perm_l_kernel(tc, xT, w1, w2, offs, out):
                 queue.dma_start(out=raw[:, j : j + PACK // parts], in_=dealt[:, j : j + PACK // parts])
             return raw
 
+        def staged(name, columns, tag=None):
+            return keep.tile([P, columns * PACK], BF16, name=name, tag=tag or name, align_bytes=ALIGN)
+
+        def operand(name, columns):
+            codes = keep.tile([P, columns], U32, name=name + "_codes", align_bytes=ALIGN)
+            scales = keep.tile([P, columns], U8, name=name + "_scales", align_bytes=ALIGN)
+            return codes, scales
+
         offsets = keep.tile([P, H // 16], U16, name="offsets")
-        x_raw = [load(nc.scalar, "x_raw0", xT[0:KP, :])]
-        w1_raw = {}
-        for g, c0 in ((0, 0), (0, 2 * W), (1, 0)):
-            wide = load(nc.sync, "w1_raw%d_%d" % (g, c0), w1[g * KP : (g + 1) * KP, c0 : c0 + 2 * W], parts=2)
-            w1_raw[g, c0], w1_raw[g, c0 + W] = wide[:, :, 0:W], wide[:, :, W : 2 * W]
-        x_raw.append(load(nc.sync, "x_raw1", xT[KP:K, :]))
-        for c0 in range(2 * W, H, W):
-            tag = "h" if c0 == H - W else None
-            w1_raw[1, c0] = load(nc.sync, "w1_raw1_%d" % c0, w1[KP:K, c0 : c0 + W], tag)[:]
+        x0_raw = load(nc.scalar, "x0_raw", xT[0:KP, :])
+        first_raw = load(nc.sync, "first_raw", w1[0:KP, :], parts=4)
+        wide_raw = load(nc.sync, "wide_raw", w1[KP:K, 0:256], parts=2)
+        x1_raw = load(nc.sync, "x1_raw", xT[KP:K, :])
+        third_raw = load(nc.sync, "third_raw", w1[KP:K, 256:384])
+        last_raw = load(nc.sync, "last_raw", w1[KP:K, 384:512], tag="h")
         nc.sync.dma_start(offsets[:], offs)
         w2_raw = [load(nc.sync, "w2_raw%d" % m, w2[:, P * m : P * (m + 1)]) for m in range(2)]
 
@@ -84,68 +94,65 @@ def tile_picked_shuffle_mlp_gelu_perm_l_kernel(tc, xT, w1, w2, offs, out):
 
         ident = keep.tile([P, P], F32, name="ident", align_bytes=ALIGN)
         make_identity(nc, ident[:])
-
-        x_codes = keep.tile([P, 2 * T], U32, name="x_codes", align_bytes=ALIGN)
-        x_scales = keep.tile([P, 2 * T], U8, name="x_scales", align_bytes=ALIGN)
-        w1_codes = keep.tile([P, 2 * H], U32, name="w1_codes", align_bytes=ALIGN)
-        w1_scales = keep.tile([P, 2 * H], U8, name="w1_scales", align_bytes=ALIGN)
-        acc = [psum.tile([P, 512], F32, name="acc%d" % c0) for c0, width in GROUPS]
-        spare = psum.tile([P, 512], F32, name="spare")
-        turned = psum.tile([P, 4, P], F32, name="turned")
-        out_banks = [psum.tile([P, 512], F32, name="out_bank%d" % number) for number in range(3)]
         ident16 = keep.tile([P, P], BF16, name="ident16", align_bytes=ALIGN)
         make_identity(nc, ident16[:])
 
-        def fill(count, banks, source):
+        banks = [psum.tile([P, 512], F32, name="bank%d" % b) for b in range(8)]
+        acc, spare, turned, out_banks = banks[0:3], banks[3], banks[4], banks[5:8] + banks[0:1]
+
+        def keep_busy(count, targets, source):
             for i in range(count):
-                bank = banks[(i - count) % len(banks)]
-                nc.tensor.transpose(bank.bitcast(BF16)[:, 0:P], source[:, 64 : 64 + P], ident16[:])
+                bank = targets[(i - count) % len(targets)]
+                nc.tensor.transpose(bank[:].bitcast(BF16)[:, 0:P], source[:, 64 : 64 + P], ident16[:])
 
-        pieces = [(x_raw[0][:], x_codes, x_scales, 0)]
-        pieces += [(w1_raw[0, c0], w1_codes, w1_scales, c0) for c0 in range(0, H, W)]
-        pieces += [(w1_raw[1, c0], w1_codes, w1_scales, H + c0) for c0 in range(0, 2 * W, W)]
-        pieces += [(x_raw[1][:], x_codes, x_scales, T)]
-        pieces += [(w1_raw[1, c0], w1_codes, w1_scales, H + c0) for c0 in range(2 * W, H, W)]
-        passes_after = {7: [(0, 0), (0, 1), (0, 2), (1, 0)], 8: [(1, 1)], 9: [(1, 2)]}
+        x = operand("x", 2 * T)
+        w1q = operand("w1", 2 * H)
 
-        for first in range(0, len(pieces), 2):
-            grouped = []
-            for number, copy in ((first, scalar_copy), (first + 1, vector_copy)):
-                tag = "last" if number == len(pieces) - 1 else "grouped%d" % number
-                tile = keep.tile([P, W * PACK], BF16, name="grouped%d" % number, tag=tag, align_bytes=ALIGN)
-                cast(copy, tile[:], pieces[number][0])
-                grouped.append((number, tile))
-                if number == 3:
-                    fill(14, [bank[:] for bank in acc + [spare]], tile[:])
-            for number, tile in grouped:
-                raw, codes, scales, c0 = pieces[number]
-                quantize(codes[:, c0 : c0 + W], scales[:, c0 : c0 + W], tile[:])
-                for g, index in passes_after.get(number, []):
-                    h0, width = GROUPS[index]
-                    tokens = slice(g * T, (g + 1) * T)
-                    channels = slice(g * H + h0, g * H + h0 + width)
-                    product(
-                        acc[index][:, 0:width],
-                        x_codes[:, tokens],
-                        x_scales[:, tokens],
-                        w1_codes[:, channels],
-                        w1_scales[:, channels],
-                        start=(g == 0),
-                        stop=(g == 1),
-                    )
-                if number == 7:
-                    product(spare[:, 0:P], x_codes[:, 0:T], x_scales[:, 0:T], w1_codes[:, 0:W], w1_scales[:, 0:W], True, True)
-                if number == 9:
-                    fill(20, [spare[:], turned[:].rearrange("p a b -> p (a b)")], codes[:, c0 : c0 + W].bitcast(BF16))
+        x0, x1 = staged("x0", T), staged("x1", T)
+        cast(scalar_copy, x0, x0_raw, 0, T)
+        quantize(*x, 0, x0, 0, T)
 
-        w2_codes = keep.tile([P, N], U32, name="w2_codes", align_bytes=ALIGN)
-        w2_scales = keep.tile([P, N], U8, name="w2_scales", align_bytes=ALIGN)
+        nc.tensor.transpose(spare[:, 0:P], first_raw[:, PACK - 1, 0:P], ident[:])
+        keep_busy(WARM_BEFORE - 1, [spare] + acc, x0)
+
+        first = staged("first", H)
+        cast(vector_copy, first, first_raw, 0, FIRST_ON_VECTOR)
+        cast(scalar_copy, first, first_raw, FIRST_ON_VECTOR, H)
+        quantize(*w1q, 0, first, 0, 256)
+        quantize(*w1q, 0, first, 256, H)
+
+        wide = staged("wide", 256)
+        cast(vector_copy, wide, wide_raw, 0, WIDE_ON_VECTOR)
+        cast(scalar_copy, wide, wide_raw, WIDE_ON_VECTOR, 256)
+        cast(vector_copy, x1, x1_raw, 0, T)
+        quantize(*w1q, H, wide, 0, 256)
+        quantize(*x, T, x1, 0, T)
+
+        def layer1(g, index):
+            c0, width = GROUPS[index]
+            tokens = slice(g * T, (g + 1) * T)
+            product(acc[index][:, 0:width], x, tokens, w1q, slice(g * H + c0, g * H + c0 + width), g == 0, g == 1)
+
+        for index in range(3):
+            layer1(0, index)
+        layer1(1, 0)
+        product(spare[:, 0:P], x, slice(0, T), w1q, slice(0, P), True, True)
+
+        third, last = staged("third", P), staged("last", P)
+        cast(scalar_copy, third, third_raw, 0, P)
+        cast(vector_copy, last, last_raw, 0, P)
+        quantize(*w1q, H + 256, third, 0, P)
+        layer1(1, 1)
+        quantize(*w1q, H + 384, last, 0, P)
+        layer1(1, 2)
+        keep_busy(WARM_GATHER, [spare, turned], third)
+
+        w2q = operand("w2", N)
 
         def prepare_w2(m, tag):
-            grouped = keep.tile([P, P * PACK], BF16, name="w2_grouped%d" % m, tag=tag, align_bytes=ALIGN)
-            cast(vector_copy, grouped[:], w2_raw[m][:])
-            outputs = slice(P * m, P * (m + 1))
-            quantize(w2_codes[:, outputs], w2_scales[:, outputs], grouped[:])
+            grouped = staged("w2_grouped%d" % m, P, tag)
+            cast(vector_copy, grouped, w2_raw[m], 0, P)
+            quantize(*w2q, P * m, grouped, 0, P)
 
         prepare_w2(0, "last")
 
@@ -160,41 +167,26 @@ def tile_picked_shuffle_mlp_gelu_perm_l_kernel(tc, xT, w1, w2, offs, out):
 
         prepare_w2(1, "h")
 
+        keep_busy(1, [spare], gathered[:, H - 192 : H])
         words = gathered[:].bitcast(F32)
-        fill(1, [spare[:]], gathered[:, H - 192 : H])
         for u in range(2):
-            nc.tensor.transpose(turned[:, u, :], words[:, u : 2 * P : 2], ident[:])
-        out_banks.append(acc[0])
-        fill(12, [bank[:] for bank in out_banks], gathered[:])
+            nc.tensor.transpose(turned[:, u * P : (u + 1) * P], words[:, u : 2 * P : 2], ident[:])
+        keep_busy(WARM_COPY, out_banks, gathered)
 
-        h_codes = keep.tile([P, T], U32, name="h_codes", align_bytes=ALIGN)
-        h_scales = keep.tile([P, T], U8, name="h_scales", align_bytes=ALIGN)
-        for half in range(2):
-            tokens = slice(half * T // 2, (half + 1) * T // 2)
-            grouped = keep.tile([P, T // 2 * PACK], BF16, name="h_grouped%d" % half, align_bytes=ALIGN)
-            scalar_copy(
-                grouped[:].bitcast(F32).rearrange("p (t u) -> p t u", u=2),
-                turned[:, 0:2, tokens].rearrange("p u t -> p t u"),
-            )
-            quantize(h_codes[:, tokens], h_scales[:, tokens], grouped[:])
+        hq = operand("h", T)
+        turned_words = turned[:, 0 : 2 * P].rearrange("p (u t) -> p t u", u=2)
+        halves = [slice(0, T // 2), slice(T // 2, T)]
+        for half, tokens in enumerate(halves):
+            grouped = staged("h_grouped%d" % half, T // 2)
+            scalar_copy(grouped[:].bitcast(F32).rearrange("p (t u) -> p t u", u=2), turned_words[:, tokens])
+            quantize(*hq, tokens.start, grouped, 0, T // 2)
 
         y = [keep.tile([P, T], F32, name="y%d" % m, align_bytes=ALIGN) for m in range(2)]
-        for half in range(2):
-            tokens = slice(half * T // 2, (half + 1) * T // 2)
+        for half, tokens in enumerate(halves):
             for m, copy in ((0, scalar_copy), (1, vector_copy)):
-                outputs = slice(P * m, P * (m + 1))
                 bank = out_banks[2 * half + m]
-                product(
-                    bank[:, 0 : T // 2],
-                    w2_codes[:, outputs],
-                    w2_scales[:, outputs],
-                    h_codes[:, tokens],
-                    h_scales[:, tokens],
-                    True,
-                    True,
-                )
+                product(bank[:, 0 : T // 2], w2q, slice(P * m, P * (m + 1)), hq, tokens, True, True)
                 copy(y[m][:, tokens], bank[:, 0 : T // 2])
-                if m == 0:
-                    queue = nc.scalar if half else nc.sync
-                    queue.dma_start(out=out[outputs, tokens], in_=y[m][:, tokens])
+            queue = nc.scalar if half else nc.sync
+            queue.dma_start(out=out[0:P, tokens], in_=y[0][:, tokens])
         nc.sync.dma_start(out=out[P:N, :], in_=y[1][:])

@@ -23,7 +23,7 @@ GROUPS = ((0, 256), (256, 128), (384, 128))
 VECTOR_LIST_COLUMNS = 18
 FIRST_ON_VECTOR = 320
 WIDE_ON_VECTOR = 64
-WARM_BEFORE, WARM_GATHER, WARM_COPY = 18, 20, 12
+WARM_BEFORE, WARM_GATHER, WARM_COPY = 19, 20, 12
 
 
 def tile_picked_shuffle_mlp_gelu_perm_l_kernel(tc, xT, w1, w2, offs, out):

@@ -21,8 +21,8 @@ KP = P * PACK
 ALIGN = 512
 GROUPS = ((0, 256), (256, 128), (384, 128))
 VECTOR_LIST_COLUMNS = 18
-FIRST_ON_VECTOR = 320
-WIDE_ON_VECTOR = 64
+FIRST_ON_VECTOR = 256
+WIDE_ON_VECTOR = 128
 WARM_BEFORE, WARM_GATHER, WARM_COPY = 19, 20, 12
 
 
@@ -135,8 +135,8 @@ def tile_picked_shuffle_mlp_gelu_perm_l_kernel(tc, xT, w1, w2, offs, out):
 
         for index in range(3):
             layer1(0, index)
-        layer1(1, 0)
         product(spare[:, 0:P], x, slice(0, T), w1q, slice(0, P), True, True)
+        layer1(1, 0)
 
         third, last = staged("third", P), staged("last", P)
         cast(scalar_copy, third, third_raw, 0, P)

@@ -23,7 +23,7 @@ GROUPS = ((0, 256), (256, 128), (384, 128))
 VECTOR_LIST_COLUMNS = 18
 FIRST_ON_VECTOR = 256
 WIDE_ON_VECTOR = 128
-WARM_BEFORE, WARM_GATHER, WARM_COPY = 19, 20, 12
+WARM_BEFORE, WARM_GATHER, WARM_COPY = 20, 20, 12
 
 
 def tile_picked_shuffle_mlp_gelu_perm_l_kernel(tc, xT, w1, w2, offs, out):

@@ -18,12 +18,12 @@ COPY = mybir.ActivationFunctionType.Copy
 P = 128
 PACK = 4
 KP = P * PACK
+BANK = 512
+LIST_ROWS = 16
 ALIGN = 512
 GROUPS = ((0, 256), (256, 128), (384, 128))
 VECTOR_LIST_COLUMNS = 18
-FIRST_ON_VECTOR = 256
-WIDE_ON_VECTOR = 128
-WARM_BEFORE, WARM_GATHER, WARM_COPY = 20, 20, 12
+WARM_BEFORE, WARM_GATHER, WARM_COPY = 14, 20, 12
 
 
 def tile_picked_shuffle_mlp_gelu_perm_l_kernel(tc, xT, w1, w2, offs, out):
@@ -41,19 +41,18 @@ def tile_picked_shuffle_mlp_gelu_perm_l_kernel(tc, xT, w1, w2, offs, out):
             raw[:, :, c0:c1].rearrange("p j (c i) -> p c j i", i=2),
         )
 
-    def quantize(codes, scales, first, grouped, c0, c1):
-        columns = slice(first + c0, first + c1)
-        nc.vector.quantize_mx(
-            out=codes[:, columns].bitcast(FP8X4), scales=scales[:, columns], in_=grouped[:, PACK * c0 : PACK * c1]
-        )
+    def quantize(operand, first, grouped):
+        codes, scales = operand
+        columns = slice(first, first + grouped.shape[1] // PACK)
+        nc.vector.quantize_mx(out=codes[:, columns].bitcast(FP8X4), scales=scales[:, columns], in_=grouped)
 
-    def product(acc, lhs, lhs_columns, rhs, rhs_columns, start, stop):
+    def product(acc, stationary, stationary_columns, moving, moving_columns, start, stop):
         nc.tensor.matmul_mx(
             out=acc,
-            lhsT=lhs[0][:, lhs_columns].bitcast(FP8X4),
-            lhsT_scale=lhs[1][:, lhs_columns],
-            rhs=rhs[0][:, rhs_columns].bitcast(FP8X4),
-            rhs_scale=rhs[1][:, rhs_columns],
+            lhsT=stationary[0][:, stationary_columns].bitcast(FP8X4),
+            lhsT_scale=stationary[1][:, stationary_columns],
+            rhs=moving[0][:, moving_columns].bitcast(FP8X4),
+            rhs_scale=moving[1][:, moving_columns],
             start=start,
             stop=stop,
         )
@@ -72,12 +71,12 @@ def tile_picked_shuffle_mlp_gelu_perm_l_kernel(tc, xT, w1, w2, offs, out):
         def staged(name, columns, tag=None):
             return keep.tile([P, columns * PACK], BF16, name=name, tag=tag or name, align_bytes=ALIGN)
 
-        def operand(name, columns):
+        def quantised(name, columns):
             codes = keep.tile([P, columns], U32, name=name + "_codes", align_bytes=ALIGN)
             scales = keep.tile([P, columns], U8, name=name + "_scales", align_bytes=ALIGN)
             return codes, scales
 
-        offsets = keep.tile([P, H // 16], U16, name="offsets")
+        offsets = keep.tile([P, H // LIST_ROWS], U16, name="offsets")
         x0_raw = load(nc.scalar, "x0_raw", xT[0:KP, :])
         first_raw = load(nc.sync, "first_raw", w1[0:KP, :], parts=4)
         wide_raw = load(nc.sync, "wide_raw", w1[KP:K, 0:256], parts=2)
@@ -85,74 +84,71 @@ def tile_picked_shuffle_mlp_gelu_perm_l_kernel(tc, xT, w1, w2, offs, out):
         third_raw = load(nc.sync, "third_raw", w1[KP:K, 256:384])
         last_raw = load(nc.sync, "last_raw", w1[KP:K, 384:512], tag="h")
         nc.sync.dma_start(offsets[:], offs)
-        w2_raw = [load(nc.sync, "w2_raw%d" % m, w2[:, P * m : P * (m + 1)]) for m in range(2)]
+        w2_raw = [load(nc.sync, "w2_raw%d" % m, w2[:, P * m : P * (m + 1)]) for m in range(N // P)]
 
-        warm = keep.tile([P, 1], F32, name="warm")
-        warm_out = keep.tile([P, 1], F32, name="warm_out")
-        nc.vector.memset(warm[:], 0.0)
-        nc.scalar.activation(warm_out[:], warm[:], GELU)
+        preload = keep.tile([P, 1], F32, name="preload")
+        preload_out = keep.tile([P, 1], F32, name="preload_out")
+        nc.vector.memset(preload[:], 0.0)
+        nc.scalar.activation(preload_out[:], preload[:], GELU)
 
-        ident = keep.tile([P, P], F32, name="ident", align_bytes=ALIGN)
-        make_identity(nc, ident[:])
-        ident16 = keep.tile([P, P], BF16, name="ident16", align_bytes=ALIGN)
-        make_identity(nc, ident16[:])
+        identity = keep.tile([P, P], F32, name="identity", align_bytes=ALIGN)
+        make_identity(nc, identity[:])
+        warm_identity = keep.tile([P, P], BF16, name="warm_identity", align_bytes=ALIGN)
+        make_identity(nc, warm_identity[:])
 
-        banks = [psum.tile([P, 512], F32, name="bank%d" % b) for b in range(8)]
-        acc, spare, turned, out_banks = banks[0:3], banks[3], banks[4], banks[5:8] + banks[0:1]
+        banks = [psum.tile([P, BANK], F32, name="bank%d" % b) for b in range(8)]
+        acc, warm_bank, turned, out_banks = banks[0:3], banks[3], banks[4], banks[5:8] + banks[0:1]
 
-        def keep_busy(count, targets, source):
+        def warm_up(count, targets, source):
             for i in range(count):
-                bank = targets[(i - count) % len(targets)]
-                nc.tensor.transpose(bank[:].bitcast(BF16)[:, 0:P], source[:, 64 : 64 + P], ident16[:])
+                nc.tensor.transpose(targets[i % len(targets)][:].bitcast(BF16)[:, 0:P], source[:, 0:P], warm_identity[:])
 
-        x = operand("x", 2 * T)
-        w1q = operand("w1", 2 * H)
+        x_q = quantised("x", 2 * T)
+        w1_q = quantised("w1", 2 * H)
 
         x0, x1 = staged("x0", T), staged("x1", T)
         cast(scalar_copy, x0, x0_raw, 0, T)
-        quantize(*x, 0, x0, 0, T)
-
-        nc.tensor.transpose(spare[:, 0:P], first_raw[:, PACK - 1, 0:P], ident[:])
-        keep_busy(WARM_BEFORE - 1, [spare] + acc, x0)
+        quantize(x_q, 0, x0[:])
 
         first = staged("first", H)
-        cast(vector_copy, first, first_raw, 0, FIRST_ON_VECTOR)
-        cast(scalar_copy, first, first_raw, FIRST_ON_VECTOR, H)
-        quantize(*w1q, 0, first, 0, 256)
-        quantize(*w1q, 0, first, 256, H)
+        cast(vector_copy, first, first_raw, 0, H // 2)
+        cast(scalar_copy, first, first_raw, H // 2, H)
+        warm_up(WARM_BEFORE, acc + [warm_bank], first)
+        quantize(w1_q, 0, first[:, 0 : PACK * H // 2])
+        quantize(w1_q, H // 2, first[:, PACK * H // 2 : PACK * H])
 
-        wide = staged("wide", 256)
-        cast(vector_copy, wide, wide_raw, 0, WIDE_ON_VECTOR)
-        cast(scalar_copy, wide, wide_raw, WIDE_ON_VECTOR, 256)
+        wide = staged("wide", 2 * P)
+        cast(vector_copy, wide, wide_raw, 0, P)
+        cast(scalar_copy, wide, wide_raw, P, 2 * P)
         cast(vector_copy, x1, x1_raw, 0, T)
-        quantize(*w1q, H, wide, 0, 256)
-        quantize(*x, T, x1, 0, T)
+        quantize(w1_q, H, wide[:])
+        quantize(x_q, T, x1[:])
 
-        def layer1(g, index):
+        def first_layer(g, index):
             c0, width = GROUPS[index]
-            tokens = slice(g * T, (g + 1) * T)
-            product(acc[index][:, 0:width], x, tokens, w1q, slice(g * H + c0, g * H + c0 + width), g == 0, g == 1)
+            channels = slice(g * H + c0, g * H + c0 + width)
+            product(acc[index][:, 0:width], x_q, slice(g * T, (g + 1) * T), w1_q, channels, g == 0, g == 1)
 
-        for index in range(3):
-            layer1(0, index)
-        product(spare[:, 0:P], x, slice(0, T), w1q, slice(0, P), True, True)
-        layer1(1, 0)
+        for index in range(len(GROUPS)):
+            first_layer(0, index)
+        product(warm_bank[:, 0:P], x_q, slice(0, T), w1_q, slice(0, P), True, True)
+        first_layer(1, 0)
 
         third, last = staged("third", P), staged("last", P)
         cast(scalar_copy, third, third_raw, 0, P)
         cast(vector_copy, last, last_raw, 0, P)
-        quantize(*w1q, H + 256, third, 0, P)
-        layer1(1, 1)
-        quantize(*w1q, H + 384, last, 0, P)
-        layer1(1, 2)
-        keep_busy(WARM_GATHER, [spare, turned], third)
+        quantize(w1_q, H + GROUPS[1][0], third[:])
+        first_layer(1, 1)
+        quantize(w1_q, H + GROUPS[2][0], last[:])
+        first_layer(1, 2)
+        warm_up(WARM_GATHER, [warm_bank, turned], w1_q[0][:, H + GROUPS[2][0] : 2 * H].bitcast(BF16))
 
-        w2q = operand("w2", N)
+        w2_q = quantised("w2", N)
 
         def prepare_w2(m, tag):
             grouped = staged("w2_grouped%d" % m, P, tag)
             cast(vector_copy, grouped, w2_raw[m], 0, P)
-            quantize(*w2q, P * m, grouped, 0, P)
+            quantize(w2_q, P * m, grouped[:])
 
         prepare_w2(0, "last")
 
@@ -161,32 +157,33 @@ def tile_picked_shuffle_mlp_gelu_perm_l_kernel(tc, xT, w1, w2, offs, out):
             nc.scalar.activation(h[:, c0 : c0 + width], acc[index][:, 0:width], GELU)
 
         gathered = keep.tile([P, H], BF16, name="gathered", align_bytes=ALIGN)
-        split = VECTOR_LIST_COLUMNS
-        nc.vector.tensor_copy(out=gathered[:, 0 : 16 * split], in_=h[:].indirect(offsets[:, 0:split]))
-        nc.scalar.activation(gathered[:, 16 * split : H], h[:].indirect(offsets[:, split : H // 16]), COPY)
+        split = LIST_ROWS * VECTOR_LIST_COLUMNS
+        nc.vector.tensor_copy(out=gathered[:, 0:split], in_=h[:].indirect(offsets[:, 0:VECTOR_LIST_COLUMNS]))
+        nc.scalar.activation(
+            gathered[:, split:H], h[:].indirect(offsets[:, VECTOR_LIST_COLUMNS : H // LIST_ROWS]), COPY
+        )
 
         prepare_w2(1, "h")
 
-        keep_busy(1, [spare], gathered[:, H - 192 : H])
+        warm_up(1, [warm_bank], gathered[:, split:H])
         words = gathered[:].bitcast(F32)
         for u in range(2):
-            nc.tensor.transpose(turned[:, u * P : (u + 1) * P], words[:, u : 2 * P : 2], ident[:])
-        keep_busy(WARM_COPY, out_banks, gathered)
+            nc.tensor.transpose(turned[:, u * P : (u + 1) * P], words[:, u : 2 * P : 2], identity[:])
+        warm_up(WARM_COPY, out_banks, gathered)
 
-        hq = operand("h", T)
+        h_q = quantised("h", T)
         turned_words = turned[:, 0 : 2 * P].rearrange("p (u t) -> p t u", u=2)
-        halves = [slice(0, T // 2), slice(T // 2, T)]
+        halves = (slice(0, T // 2), slice(T // 2, T))
         for half, tokens in enumerate(halves):
             grouped = staged("h_grouped%d" % half, T // 2)
             scalar_copy(grouped[:].bitcast(F32).rearrange("p (t u) -> p t u", u=2), turned_words[:, tokens])
-            quantize(*hq, tokens.start, grouped, 0, T // 2)
+            quantize(h_q, tokens.start, grouped[:])
 
-        y = [keep.tile([P, T], F32, name="y%d" % m, align_bytes=ALIGN) for m in range(2)]
-        for half, tokens in enumerate(halves):
-            for m, copy in ((0, scalar_copy), (1, vector_copy)):
+        y = [keep.tile([P, T], F32, name="y%d" % m, align_bytes=ALIGN) for m in range(N // P)]
+        for half, (tokens, queue) in enumerate(zip(halves, (nc.sync, nc.scalar))):
+            for m, copy in enumerate((scalar_copy, vector_copy)):
                 bank = out_banks[2 * half + m]
-                product(bank[:, 0 : T // 2], w2q, slice(P * m, P * (m + 1)), hq, tokens, True, True)
+                product(bank[:, 0 : T // 2], w2_q, slice(P * m, P * (m + 1)), h_q, tokens, True, True)
                 copy(y[m][:, tokens], bank[:, 0 : T // 2])
-            queue = nc.scalar if half else nc.sync
             queue.dma_start(out=out[0:P, tokens], in_=y[0][:, tokens])
         nc.sync.dma_start(out=out[P:N, :], in_=y[1][:])

@@ -23,7 +23,7 @@ LIST_ROWS = 16
 ALIGN = 512
 GROUPS = ((0, 256), (256, 128), (384, 128))
 VECTOR_LIST_COLUMNS = 18
-WARM_BEFORE, WARM_GATHER, WARM_COPY = 14, 20, 12
+WARM_BEFORE, WARM_GATHER, WARM_COPY = 13, 20, 12
 
 
 def tile_picked_shuffle_mlp_gelu_perm_l_kernel(tc, xT, w1, w2, offs, out):

@@ -141,7 +141,7 @@ def tile_picked_shuffle_mlp_gelu_perm_l_kernel(tc, xT, w1, w2, offs, out):
         first_layer(1, 1)
         quantize(w1_q, H + GROUPS[2][0], last[:])
         first_layer(1, 2)
-        warm_up(WARM_GATHER, [warm_bank, turned], w1_q[0][:, H + GROUPS[2][0] : 2 * H].bitcast(BF16))
+        warm_up(WARM_GATHER, [warm_bank, turned], third)
 
         w2_q = quantised("w2", N)
 

@@ -23,7 +23,7 @@ LIST_ROWS = 16
 ALIGN = 512
 GROUPS = ((0, 256), (256, 128), (384, 128))
 VECTOR_LIST_COLUMNS = 18
-WARM_BEFORE, WARM_GATHER, WARM_COPY = 13, 20, 12
+WARM_BEFORE, WARM_GATHER, WARM_COPY = 14, 20, 12
 
 
 def tile_picked_shuffle_mlp_gelu_perm_l_kernel(tc, xT, w1, w2, offs, out):

@@ -61,8 +61,8 @@ def tile_picked_shuffle_mlp_gelu_perm_l_kernel(tc, xT, w1, w2, offs, out):
         keep = ctx.enter_context(tc.tile_pool(name="keep", bufs=1))
         psum = ctx.enter_context(tc.psum_pool(name="psum", bufs=1))
 
-        def load(queue, name, rows, tag=None, parts=1):
-            raw = keep.tile([P, PACK, rows.shape[1]], F32, name=name, tag=tag or name, align_bytes=ALIGN)
+        def load(queue, name, rows, parts=1):
+            raw = keep.tile([P, PACK, rows.shape[1]], F32, name=name, align_bytes=ALIGN)
             dealt = rows.rearrange("(p j) c -> p j c", j=PACK)
             for j in range(0, PACK, PACK // parts):
                 queue.dma_start(out=raw[:, j : j + PACK // parts], in_=dealt[:, j : j + PACK // parts])
@@ -82,7 +82,7 @@ def tile_picked_shuffle_mlp_gelu_perm_l_kernel(tc, xT, w1, w2, offs, out):
         wide_raw = load(nc.sync, "wide_raw", w1[KP:K, 0:256], parts=2)
         x1_raw = load(nc.sync, "x1_raw", xT[KP:K, :])
         third_raw = load(nc.sync, "third_raw", w1[KP:K, 256:384])
-        last_raw = load(nc.sync, "last_raw", w1[KP:K, 384:512], tag="h")
+        last_raw = load(nc.sync, "last_raw", w1[KP:K, 384:512])
         nc.sync.dma_start(offsets[:], offs)
         w2_raw = [load(nc.sync, "w2_raw%d" % m, w2[:, P * m : P * (m + 1)]) for m in range(N // P)]
 
@@ -145,12 +145,12 @@ def tile_picked_shuffle_mlp_gelu_perm_l_kernel(tc, xT, w1, w2, offs, out):
 
         w2_q = quantised("w2", N)
 
-        def prepare_w2(m, tag):
+        def prepare_w2(m, tag=None):
             grouped = staged("w2_grouped%d" % m, P, tag)
             cast(vector_copy, grouped, w2_raw[m], 0, P)
             quantize(w2_q, P * m, grouped[:])
 
-        prepare_w2(0, "last")
+        prepare_w2(0)
 
         h = keep.tile([P, H], BF16, name="h", tag="h", align_bytes=ALIGN)
         for index, (c0, width) in enumerate(GROUPS):

@@ -22,7 +22,7 @@ BANK = 512
 LIST_ROWS = 16
 ALIGN = 512
 GROUPS = ((0, 256), (256, 128), (384, 128))
-VECTOR_LIST_COLUMNS = 18
+VECTOR_LIST_COLUMNS = 16
 WARM_BEFORE, WARM_GATHER, WARM_COPY = 14, 20, 12
 
 
@@ -165,7 +165,7 @@ def tile_picked_shuffle_mlp_gelu_perm_l_kernel(tc, xT, w1, w2, offs, out):
 
         prepare_w2(1, "h")
 
-        warm_up(1, [warm_bank], gathered[:, split:H])
+        warm_up(1, [warm_bank], gathered[:, 0:split])
         words = gathered[:].bitcast(F32)
         for u in range(2):
             nc.tensor.transpose(turned[:, u * P : (u + 1) * P], words[:, u : 2 * P : 2], identity[:])

@@ -136,10 +136,12 @@ def tile_picked_shuffle_mlp_gelu_perm_l_kernel(tc, xT, w1, w2, offs, out):
 
         third, last = staged("third", P), staged("last", P)
         cast(scalar_copy, third, third_raw, 0, P)
-        cast(vector_copy, last, last_raw, 0, P)
+        cast(vector_copy, last, last_raw, 0, 96)
+        cast(scalar_copy, last, last_raw, 96, P)
         quantize(w1_q, H + GROUPS[1][0], third[:])
         first_layer(1, 1)
-        quantize(w1_q, H + GROUPS[2][0], last[:])
+        quantize(w1_q, H + GROUPS[2][0], last[:, 0 : PACK * 64])
+        quantize(w1_q, H + GROUPS[2][0] + 64, last[:, PACK * 64 : PACK * P])
         first_layer(1, 2)
         warm_up(WARM_GATHER, [warm_bank, turned], third)
 

@@ -136,8 +136,8 @@ def tile_picked_shuffle_mlp_gelu_perm_l_kernel(tc, xT, w1, w2, offs, out):
 
         third, last = staged("third", P), staged("last", P)
         cast(scalar_copy, third, third_raw, 0, P)
-        cast(vector_copy, last, last_raw, 0, 96)
-        cast(scalar_copy, last, last_raw, 96, P)
+        cast(vector_copy, last, last_raw, 0, 80)
+        cast(scalar_copy, last, last_raw, 80, P)
         quantize(w1_q, H + GROUPS[1][0], third[:])
         first_layer(1, 1)
         quantize(w1_q, H + GROUPS[2][0], last[:, 0 : PACK * 64])

@@ -23,7 +23,7 @@ LIST_ROWS = 16
 ALIGN = 512
 GROUPS = ((0, 256), (256, 128), (384, 128))
 VECTOR_LIST_COLUMNS = 16
-WARM_BEFORE, WARM_GATHER, WARM_COPY = 14, 20, 12
+WARM_BEFORE, WARM_GATHER, WARM_COPY = 13, 20, 12
 
 
 def tile_picked_shuffle_mlp_gelu_perm_l_kernel(tc, xT, w1, w2, offs, out):

@@ -83,8 +83,9 @@ def tile_picked_shuffle_mlp_gelu_perm_l_kernel(tc, xT, w1, w2, offs, out):
         x1_raw = load(nc.sync, "x1_raw", xT[KP:K, :])
         third_raw = load(nc.sync, "third_raw", w1[KP:K, 256:384])
         last_raw = load(nc.sync, "last_raw", w1[KP:K, 384:512])
+        w2_raw = [load(nc.sync, "w2_raw0", w2[:, 0:P])]
         nc.sync.dma_start(offsets[:], offs)
-        w2_raw = [load(nc.sync, "w2_raw%d" % m, w2[:, P * m : P * (m + 1)]) for m in range(N // P)]
+        w2_raw.append(load(nc.sync, "w2_raw1", w2[:, P:N]))
 
         preload = keep.tile([P, 1], F32, name="preload")
         preload_out = keep.tile([P, 1], F32, name="preload_out")
@@ -135,10 +136,12 @@ def tile_picked_shuffle_mlp_gelu_perm_l_kernel(tc, xT, w1, w2, offs, out):
         first_layer(1, 0)
 
         third, last = staged("third", P), staged("last", P)
-        cast(scalar_copy, third, third_raw, 0, P)
-        cast(vector_copy, last, last_raw, 0, 80)
-        cast(scalar_copy, last, last_raw, 80, P)
-        quantize(w1_q, H + GROUPS[1][0], third[:])
+        cast(scalar_copy, third, third_raw, 0, 96)
+        cast(vector_copy, third, third_raw, 96, P)
+        cast(vector_copy, last, last_raw, 0, 76)
+        cast(scalar_copy, last, last_raw, 76, P)
+        quantize(w1_q, H + GROUPS[1][0], third[:, 0 : PACK * 64])
+        quantize(w1_q, H + GROUPS[1][0] + 64, third[:, PACK * 64 : PACK * P])
         first_layer(1, 1)
         quantize(w1_q, H + GROUPS[2][0], last[:, 0 : PACK * 64])
         quantize(w1_q, H + GROUPS[2][0] + 64, last[:, PACK * 64 : PACK * P])

@@ -78,14 +78,14 @@ def tile_picked_shuffle_mlp_gelu_perm_l_kernel(tc, xT, w1, w2, offs, out):
 
         offsets = keep.tile([P, H // LIST_ROWS], U16, name="offsets")
         x0_raw = load(nc.scalar, "x0_raw", xT[0:KP, :])
-        first_raw = load(nc.sync, "first_raw", w1[0:KP, :], parts=4)
-        wide_raw = load(nc.sync, "wide_raw", w1[KP:K, 0:256], parts=2)
+        first_raw = load(nc.sync, "first_raw", w1[0:KP, :], parts=2)
+        wide_raw = load(nc.sync, "wide_raw", w1[KP:K, 0:256])
         x1_raw = load(nc.sync, "x1_raw", xT[KP:K, :])
         third_raw = load(nc.sync, "third_raw", w1[KP:K, 256:384])
         last_raw = load(nc.sync, "last_raw", w1[KP:K, 384:512])
         w2_raw = [load(nc.sync, "w2_raw0", w2[:, 0:P])]
         nc.sync.dma_start(offsets[:], offs)
-        w2_raw.append(load(nc.sync, "w2_raw1", w2[:, P:N]))
+        w2_raw.append(load(nc.sync, "w2_raw1", w2[:, P:N], parts=4))
 
         preload = keep.tile([P, 1], F32, name="preload")
         preload_out = keep.tile([P, 1], F32, name="preload_out")

@@ -138,8 +138,8 @@ def tile_picked_shuffle_mlp_gelu_perm_l_kernel(tc, xT, w1, w2, offs, out):
         third, last = staged("third", P), staged("last", P)
         cast(scalar_copy, third, third_raw, 0, 96)
         cast(vector_copy, third, third_raw, 96, P)
-        cast(vector_copy, last, last_raw, 0, 76)
-        cast(scalar_copy, last, last_raw, 76, P)
+        cast(vector_copy, last, last_raw, 0, 64)
+        cast(scalar_copy, last, last_raw, 64, P)
         quantize(w1_q, H + GROUPS[1][0], third[:, 0 : PACK * 64])
         quantize(w1_q, H + GROUPS[1][0] + 64, third[:, PACK * 64 : PACK * P])
         first_layer(1, 1)

@@ -136,12 +136,10 @@ def tile_picked_shuffle_mlp_gelu_perm_l_kernel(tc, xT, w1, w2, offs, out):
         first_layer(1, 0)
 
         third, last = staged("third", P), staged("last", P)
-        cast(scalar_copy, third, third_raw, 0, 96)
-        cast(vector_copy, third, third_raw, 96, P)
+        cast(scalar_copy, third, third_raw, 0, P)
         cast(vector_copy, last, last_raw, 0, 64)
         cast(scalar_copy, last, last_raw, 64, P)
-        quantize(w1_q, H + GROUPS[1][0], third[:, 0 : PACK * 64])
-        quantize(w1_q, H + GROUPS[1][0] + 64, third[:, PACK * 64 : PACK * P])
+        quantize(w1_q, H + GROUPS[1][0], third[:])
         first_layer(1, 1)
         quantize(w1_q, H + GROUPS[2][0], last[:, 0 : PACK * 64])
         quantize(w1_q, H + GROUPS[2][0] + 64, last[:, PACK * 64 : PACK * P])

@@ -184,7 +184,7 @@ def tile_picked_shuffle_mlp_gelu_perm_l_kernel(tc, xT, w1, w2, offs, out):
 
         y = [keep.tile([P, T], F32, name="y%d" % m, align_bytes=ALIGN) for m in range(N // P)]
         for half, (tokens, queue) in enumerate(zip(halves, (nc.sync, nc.scalar))):
-            for m, copy in enumerate((scalar_copy, vector_copy)):
+            for m, copy in enumerate((vector_copy, scalar_copy)):
                 bank = out_banks[2 * half + m]
                 product(bank[:, 0 : T // 2], w2_q, slice(P * m, P * (m + 1)), h_q, tokens, True, True)
                 copy(y[m][:, tokens], bank[:, 0 : T // 2])

@@ -161,14 +161,14 @@ def tile_picked_shuffle_mlp_gelu_perm_l_kernel(tc, xT, w1, w2, offs, out):
 
         gathered = keep.tile([P, H], BF16, name="gathered", align_bytes=ALIGN)
         split = LIST_ROWS * VECTOR_LIST_COLUMNS
-        nc.vector.tensor_copy(out=gathered[:, 0:split], in_=h[:].indirect(offsets[:, 0:VECTOR_LIST_COLUMNS]))
-        nc.scalar.activation(
-            gathered[:, split:H], h[:].indirect(offsets[:, VECTOR_LIST_COLUMNS : H // LIST_ROWS]), COPY
+        nc.vector.tensor_copy(
+            out=gathered[:, split:H], in_=h[:].indirect(offsets[:, VECTOR_LIST_COLUMNS : H // LIST_ROWS])
         )
+        nc.scalar.activation(gathered[:, 0:split], h[:].indirect(offsets[:, 0:VECTOR_LIST_COLUMNS]), COPY)
 
         prepare_w2(1, "h")
 
-        warm_up(1, [warm_bank], gathered[:, 0:split])
+        warm_up(1, [warm_bank], gathered[:, split:H])
         words = gathered[:].bitcast(F32)
         for u in range(2):
             nc.tensor.transpose(turned[:, u * P : (u + 1) * P], words[:, u : 2 * P : 2], identity[:])

@@ -23,7 +23,7 @@ LIST_ROWS = 16
 ALIGN = 512
 GROUPS = ((0, 256), (256, 128), (384, 128))
 VECTOR_LIST_COLUMNS = 16
-WARM_BEFORE, WARM_GATHER, WARM_COPY = 13, 20, 12
+WARM_BEFORE, WARM_GATHER, WARM_COPY = 17, 20, 12
 
 
 def tile_picked_shuffle_mlp_gelu_perm_l_kernel(tc, xT, w1, w2, offs, out):
@@ -77,8 +77,10 @@ def tile_picked_shuffle_mlp_gelu_perm_l_kernel(tc, xT, w1, w2, offs, out):
             return codes, scales
 
         offsets = keep.tile([P, H // LIST_ROWS], U16, name="offsets")
-        x0_raw = load(nc.scalar, "x0_raw", xT[0:KP, :])
-        first_raw = load(nc.sync, "first_raw", w1[0:KP, :], parts=2)
+        first_raw = keep.tile([P, PACK, H], F32, name="first_raw", align_bytes=ALIGN)
+        for j0, queue in ((0, nc.sync), (2, nc.scalar)):
+            queue.dma_start(out=first_raw[:, j0 : j0 + 2], in_=w1[0:KP, :].rearrange("(p j) c -> p j c", j=PACK)[:, j0 : j0 + 2])
+        x0_raw = load(nc.sync, "x0_raw", xT[0:KP, :])
         wide_raw = load(nc.sync, "wide_raw", w1[KP:K, 0:256])
         x1_raw = load(nc.sync, "x1_raw", xT[KP:K, :])
         third_raw = load(nc.sync, "third_raw", w1[KP:K, 256:384])
@@ -108,19 +110,20 @@ def tile_picked_shuffle_mlp_gelu_perm_l_kernel(tc, xT, w1, w2, offs, out):
         w1_q = quantised("w1", 2 * H)
 
         x0, x1 = staged("x0", T), staged("x1", T)
-        cast(scalar_copy, x0, x0_raw, 0, T)
-        quantize(x_q, 0, x0[:])
 
         first = staged("first", H)
-        cast(vector_copy, first, first_raw, 0, H // 2)
-        cast(scalar_copy, first, first_raw, H // 2, H)
+        cast(vector_copy, first, first_raw, 0, 320)
+        cast(scalar_copy, first, first_raw, 320, H)
         warm_up(WARM_BEFORE, acc + [warm_bank], first)
         quantize(w1_q, 0, first[:, 0 : PACK * H // 2])
         quantize(w1_q, H // 2, first[:, PACK * H // 2 : PACK * H])
 
+        cast(scalar_copy, x0, x0_raw, 0, T)
+        quantize(x_q, 0, x0[:])
+
         wide = staged("wide", 2 * P)
-        cast(vector_copy, wide, wide_raw, 0, P)
-        cast(scalar_copy, wide, wide_raw, P, 2 * P)
+        cast(vector_copy, wide, wide_raw, 0, 160)
+        cast(scalar_copy, wide, wide_raw, 160, 2 * P)
         cast(vector_copy, x1, x1_raw, 0, T)
         quantize(w1_q, H, wide[:])
         quantize(x_q, T, x1[:])

@@ -139,10 +139,12 @@ def tile_picked_shuffle_mlp_gelu_perm_l_kernel(tc, xT, w1, w2, offs, out):
         first_layer(1, 0)
 
         third, last = staged("third", P), staged("last", P)
-        cast(scalar_copy, third, third_raw, 0, P)
+        cast(scalar_copy, third, third_raw, 0, 96)
+        cast(vector_copy, third, third_raw, 96, P)
         cast(vector_copy, last, last_raw, 0, 64)
         cast(scalar_copy, last, last_raw, 64, P)
-        quantize(w1_q, H + GROUPS[1][0], third[:])
+        quantize(w1_q, H + GROUPS[1][0], third[:, 0 : PACK * 64])
+        quantize(w1_q, H + GROUPS[1][0] + 64, third[:, PACK * 64 : PACK * P])
         first_layer(1, 1)
         quantize(w1_q, H + GROUPS[2][0], last[:, 0 : PACK * 64])
         quantize(w1_q, H + GROUPS[2][0] + 64, last[:, PACK * 64 : PACK * P])

@@ -86,8 +86,8 @@ def tile_picked_shuffle_mlp_gelu_perm_l_kernel(tc, xT, w1, w2, offs, out):
         third_raw = load(nc.sync, "third_raw", w1[KP:K, 256:384])
         last_raw = load(nc.sync, "last_raw", w1[KP:K, 384:512])
         w2_raw = [load(nc.sync, "w2_raw0", w2[:, 0:P])]
-        nc.sync.dma_start(offsets[:], offs)
         w2_raw.append(load(nc.sync, "w2_raw1", w2[:, P:N], parts=4))
+        nc.sync.dma_start(offsets[:], offs)
 
         preload = keep.tile([P, 1], F32, name="preload")
         preload_out = keep.tile([P, 1], F32, name="preload_out")

@@ -22,8 +22,7 @@ BANK = 512
 LIST_ROWS = 16
 ALIGN = 512
 GROUPS = ((0, 256), (256, 128), (384, 128))
-VECTOR_LIST_COLUMNS = 16
-WARM_BEFORE, WARM_GATHER, WARM_COPY = 17, 20, 12
+SCALAR_LIST_COLUMNS = 14
 
 
 def tile_picked_shuffle_mlp_gelu_perm_l_kernel(tc, xT, w1, w2, offs, out):
@@ -41,10 +40,12 @@ def tile_picked_shuffle_mlp_gelu_perm_l_kernel(tc, xT, w1, w2, offs, out):
             raw[:, :, c0:c1].rearrange("p j (c i) -> p c j i", i=2),
         )
 
-    def quantize(operand, first, grouped):
+    def quantize(operand, first, grouped, c0, c1):
         codes, scales = operand
-        columns = slice(first, first + grouped.shape[1] // PACK)
-        nc.vector.quantize_mx(out=codes[:, columns].bitcast(FP8X4), scales=scales[:, columns], in_=grouped)
+        columns = slice(first + c0, first + c1)
+        nc.vector.quantize_mx(
+            out=codes[:, columns].bitcast(FP8X4), scales=scales[:, columns], in_=grouped[:, PACK * c0 : PACK * c1]
+        )
 
     def product(acc, stationary, stationary_columns, moving, moving_columns, start, stop):
         nc.tensor.matmul_mx(
@@ -61,11 +62,11 @@ def tile_picked_shuffle_mlp_gelu_perm_l_kernel(tc, xT, w1, w2, offs, out):
         keep = ctx.enter_context(tc.tile_pool(name="keep", bufs=1))
         psum = ctx.enter_context(tc.psum_pool(name="psum", bufs=1))
 
-        def load(queue, name, rows, parts=1):
-            raw = keep.tile([P, PACK, rows.shape[1]], F32, name=name, align_bytes=ALIGN)
+        def load(name, rows, parts=((nc.sync, 0, PACK),), tag=None):
+            raw = keep.tile([P, PACK, rows.shape[1]], F32, name=name, tag=tag or name, align_bytes=ALIGN)
             dealt = rows.rearrange("(p j) c -> p j c", j=PACK)
-            for j in range(0, PACK, PACK // parts):
-                queue.dma_start(out=raw[:, j : j + PACK // parts], in_=dealt[:, j : j + PACK // parts])
+            for queue, j0, j1 in parts:
+                queue.dma_start(out=raw[:, j0:j1], in_=dealt[:, j0:j1])
             return raw
 
         def staged(name, columns, tag=None):
@@ -77,16 +78,14 @@ def tile_picked_shuffle_mlp_gelu_perm_l_kernel(tc, xT, w1, w2, offs, out):
             return codes, scales
 
         offsets = keep.tile([P, H // LIST_ROWS], U16, name="offsets")
-        first_raw = keep.tile([P, PACK, H], F32, name="first_raw", align_bytes=ALIGN)
-        for j0, queue in ((0, nc.sync), (2, nc.scalar)):
-            queue.dma_start(out=first_raw[:, j0 : j0 + 2], in_=w1[0:KP, :].rearrange("(p j) c -> p j c", j=PACK)[:, j0 : j0 + 2])
-        x0_raw = load(nc.sync, "x0_raw", xT[0:KP, :])
-        wide_raw = load(nc.sync, "wide_raw", w1[KP:K, 0:256])
-        x1_raw = load(nc.sync, "x1_raw", xT[KP:K, :])
-        third_raw = load(nc.sync, "third_raw", w1[KP:K, 256:384])
-        last_raw = load(nc.sync, "last_raw", w1[KP:K, 384:512])
-        w2_raw = [load(nc.sync, "w2_raw0", w2[:, 0:P])]
-        w2_raw.append(load(nc.sync, "w2_raw1", w2[:, P:N], parts=4))
+        first_raw = load("first_raw", w1[0:KP, :], ((nc.sync, 0, 2), (nc.scalar, 2, 4)))
+        x0_raw = load("x0_raw", xT[0:KP, :])
+        wide_raw = load("wide_raw", w1[KP:K, 0:256])
+        x1_raw = load("x1_raw", xT[KP:K, :])
+        third_raw = load("third_raw", w1[KP:K, 256:384])
+        last_raw = load("last_raw", w1[KP:K, 384:512], tag="h")
+        w2_raw = [load("w2_raw0", w2[:, 0:P])]
+        w2_raw.append(load("w2_raw1", w2[:, P:N], [(nc.sync, j, j + 1) for j in range(PACK)]))
         nc.sync.dma_start(offsets[:], offs)
 
         preload = keep.tile([P, 1], F32, name="preload")
@@ -96,37 +95,29 @@ def tile_picked_shuffle_mlp_gelu_perm_l_kernel(tc, xT, w1, w2, offs, out):
 
         identity = keep.tile([P, P], F32, name="identity", align_bytes=ALIGN)
         make_identity(nc, identity[:])
-        warm_identity = keep.tile([P, P], BF16, name="warm_identity", align_bytes=ALIGN)
-        make_identity(nc, warm_identity[:])
 
-        banks = [psum.tile([P, BANK], F32, name="bank%d" % b) for b in range(8)]
-        acc, warm_bank, turned, out_banks = banks[0:3], banks[3], banks[4], banks[5:8] + banks[0:1]
-
-        def warm_up(count, targets, source):
-            for i in range(count):
-                nc.tensor.transpose(targets[i % len(targets)][:].bitcast(BF16)[:, 0:P], source[:, 0:P], warm_identity[:])
+        banks = [psum.tile([P, BANK], F32, name="bank%d" % b) for b in range(7)]
+        acc, turned, out_banks = banks[0:3], banks[3], banks[4:7]
 
         x_q = quantised("x", 2 * T)
         w1_q = quantised("w1", 2 * H)
 
-        x0, x1 = staged("x0", T), staged("x1", T)
-
         first = staged("first", H)
         cast(vector_copy, first, first_raw, 0, 320)
         cast(scalar_copy, first, first_raw, 320, H)
-        warm_up(WARM_BEFORE, acc + [warm_bank], first)
-        quantize(w1_q, 0, first[:, 0 : PACK * H // 2])
-        quantize(w1_q, H // 2, first[:, PACK * H // 2 : PACK * H])
+        quantize(w1_q, 0, first, 0, H // 2)
+        quantize(w1_q, 0, first, H // 2, H)
 
+        x0, x1 = staged("x0", T), staged("x1", T)
         cast(scalar_copy, x0, x0_raw, 0, T)
-        quantize(x_q, 0, x0[:])
+        quantize(x_q, 0, x0, 0, T)
 
         wide = staged("wide", 2 * P)
         cast(vector_copy, wide, wide_raw, 0, 160)
         cast(scalar_copy, wide, wide_raw, 160, 2 * P)
         cast(vector_copy, x1, x1_raw, 0, T)
-        quantize(w1_q, H, wide[:])
-        quantize(x_q, T, x1[:])
+        quantize(w1_q, H, wide, 0, 2 * P)
+        quantize(x_q, T, x1, 0, T)
 
         def first_layer(g, index):
             c0, width = GROUPS[index]
@@ -135,7 +126,6 @@ def tile_picked_shuffle_mlp_gelu_perm_l_kernel(tc, xT, w1, w2, offs, out):
 
         for index in range(len(GROUPS)):
             first_layer(0, index)
-        product(warm_bank[:, 0:P], x_q, slice(0, T), w1_q, slice(0, P), True, True)
         first_layer(1, 0)
 
         third, last = staged("third", P), staged("last", P)
@@ -143,20 +133,19 @@ def tile_picked_shuffle_mlp_gelu_perm_l_kernel(tc, xT, w1, w2, offs, out):
         cast(vector_copy, third, third_raw, 96, P)
         cast(vector_copy, last, last_raw, 0, 64)
         cast(scalar_copy, last, last_raw, 64, P)
-        quantize(w1_q, H + GROUPS[1][0], third[:, 0 : PACK * 64])
-        quantize(w1_q, H + GROUPS[1][0] + 64, third[:, PACK * 64 : PACK * P])
+        quantize(w1_q, H + 256, third, 0, 64)
+        quantize(w1_q, H + 256, third, 64, P)
         first_layer(1, 1)
-        quantize(w1_q, H + GROUPS[2][0], last[:, 0 : PACK * 64])
-        quantize(w1_q, H + GROUPS[2][0] + 64, last[:, PACK * 64 : PACK * P])
+        quantize(w1_q, H + 384, last, 0, 64)
+        quantize(w1_q, H + 384, last, 64, P)
         first_layer(1, 2)
-        warm_up(WARM_GATHER, [warm_bank, turned], third)
 
         w2_q = quantised("w2", N)
 
         def prepare_w2(m, tag=None):
             grouped = staged("w2_grouped%d" % m, P, tag)
             cast(vector_copy, grouped, w2_raw[m], 0, P)
-            quantize(w2_q, P * m, grouped[:])
+            quantize(w2_q, P * m, grouped, 0, P)
 
         prepare_w2(0)
 
@@ -165,19 +154,17 @@ def tile_picked_shuffle_mlp_gelu_perm_l_kernel(tc, xT, w1, w2, offs, out):
             nc.scalar.activation(h[:, c0 : c0 + width], acc[index][:, 0:width], GELU)
 
         gathered = keep.tile([P, H], BF16, name="gathered", align_bytes=ALIGN)
-        split = LIST_ROWS * VECTOR_LIST_COLUMNS
+        split = LIST_ROWS * SCALAR_LIST_COLUMNS
         nc.vector.tensor_copy(
-            out=gathered[:, split:H], in_=h[:].indirect(offsets[:, VECTOR_LIST_COLUMNS : H // LIST_ROWS])
+            out=gathered[:, split:H], in_=h[:].indirect(offsets[:, SCALAR_LIST_COLUMNS : H // LIST_ROWS])
         )
-        nc.scalar.activation(gathered[:, 0:split], h[:].indirect(offsets[:, 0:VECTOR_LIST_COLUMNS]), COPY)
+        nc.scalar.activation(gathered[:, 0:split], h[:].indirect(offsets[:, 0:SCALAR_LIST_COLUMNS]), COPY)
 
         prepare_w2(1, "h")
 
-        warm_up(1, [warm_bank], gathered[:, split:H])
         words = gathered[:].bitcast(F32)
         for u in range(2):
             nc.tensor.transpose(turned[:, u * P : (u + 1) * P], words[:, u : 2 * P : 2], identity[:])
-        warm_up(WARM_COPY, out_banks, gathered)
 
         h_q = quantised("h", T)
         turned_words = turned[:, 0 : 2 * P].rearrange("p (u t) -> p t u", u=2)
@@ -185,13 +172,16 @@ def tile_picked_shuffle_mlp_gelu_perm_l_kernel(tc, xT, w1, w2, offs, out):
         for half, tokens in enumerate(halves):
             grouped = staged("h_grouped%d" % half, T // 2)
             scalar_copy(grouped[:].bitcast(F32).rearrange("p (t u) -> p t u", u=2), turned_words[:, tokens])
-            quantize(h_q, tokens.start, grouped[:])
+            quantize(h_q, tokens.start, grouped, 0, T // 2)
 
         y = [keep.tile([P, T], F32, name="y%d" % m, align_bytes=ALIGN) for m in range(N // P)]
-        for half, (tokens, queue) in enumerate(zip(halves, (nc.sync, nc.scalar))):
-            for m, copy in enumerate((vector_copy, scalar_copy)):
-                bank = out_banks[2 * half + m]
-                product(bank[:, 0 : T // 2], w2_q, slice(P * m, P * (m + 1)), h_q, tokens, True, True)
-                copy(y[m][:, tokens], bank[:, 0 : T // 2])
-            queue.dma_start(out=out[0:P, tokens], in_=y[0][:, tokens])
-        nc.sync.dma_start(out=out[P:N, :], in_=y[1][:])
+        steps = (
+            (0, halves[0], vector_copy, nc.sync),
+            (1, slice(0, T), scalar_copy, nc.sync),
+            (0, halves[1], vector_copy, nc.scalar),
+        )
+        for bank, (m, tokens, copy, queue) in zip(out_banks, steps):
+            width = tokens.stop - tokens.start
+            product(bank[:, 0:width], w2_q, slice(P * m, P * (m + 1)), h_q, tokens, True, True)
+            copy(y[m][:, tokens], bank[:, 0:width])
+            queue.dma_start(out=out[P * m : P * (m + 1), tokens], in_=y[m][:, tokens])

@@ -131,13 +131,15 @@ def tile_picked_shuffle_mlp_gelu_perm_l_kernel(tc, xT, w1, w2, offs, out):
         third, last = staged("third", P), staged("last", P)
         cast(scalar_copy, third, third_raw, 0, 96)
         cast(vector_copy, third, third_raw, 96, P)
-        cast(vector_copy, last, last_raw, 0, 64)
-        cast(scalar_copy, last, last_raw, 64, P)
+        cast(vector_copy, last, last_raw, 0, 32)
+        cast(scalar_copy, last, last_raw, 64, 96)
+        cast(vector_copy, last, last_raw, 32, 64)
+        cast(scalar_copy, last, last_raw, 96, P)
         quantize(w1_q, H + 256, third, 0, 64)
         quantize(w1_q, H + 256, third, 64, P)
         first_layer(1, 1)
-        quantize(w1_q, H + 384, last, 0, 64)
-        quantize(w1_q, H + 384, last, 64, P)
+        for c0 in (64, 0, 32, 96):
+            quantize(w1_q, H + 384, last, c0, c0 + 32)
         first_layer(1, 2)
 
         w2_q = quantised("w2", N)

@@ -22,7 +22,7 @@ BANK = 512
 LIST_ROWS = 16
 ALIGN = 512
 GROUPS = ((0, 256), (256, 128), (384, 128))
-SCALAR_LIST_COLUMNS = 14
+SCALAR_LIST_COLUMNS = 16
 
 
 def tile_picked_shuffle_mlp_gelu_perm_l_kernel(tc, xT, w1, w2, offs, out):
@@ -96,7 +96,7 @@ def tile_picked_shuffle_mlp_gelu_perm_l_kernel(tc, xT, w1, w2, offs, out):
         identity = keep.tile([P, P], F32, name="identity", align_bytes=ALIGN)
         make_identity(nc, identity[:])
 
-        banks = [psum.tile([P, BANK], F32, name="bank%d" % b) for b in range(7)]
+        banks = [psum.tile([P, BANK], F32, name="bank%d" % b) for b in range(8)]
         acc, turned, out_banks = banks[0:3], banks[3], banks[4:7]
 
         x_q = quantised("x", 2 * T)
@@ -141,6 +141,8 @@ def tile_picked_shuffle_mlp_gelu_perm_l_kernel(tc, xT, w1, w2, offs, out):
         for c0 in (64, 0, 32, 96):
             quantize(w1_q, H + 384, last, c0, c0 + 32)
         first_layer(1, 2)
+
+        nc.tensor.transpose(banks[7][:, 0:P], identity[:], identity[:])
 
         w2_q = quantised("w2", N)
 

@@ -84,8 +84,8 @@ def tile_picked_shuffle_mlp_gelu_perm_l_kernel(tc, xT, w1, w2, offs, out):
         x1_raw = load("x1_raw", xT[KP:K, :])
         third_raw = load("third_raw", w1[KP:K, 256:384])
         last_raw = load("last_raw", w1[KP:K, 384:512], tag="h")
-        w2_raw = [load("w2_raw0", w2[:, 0:P])]
-        w2_raw.append(load("w2_raw1", w2[:, P:N], [(nc.sync, j, j + 1) for j in range(PACK)]))
+        w2_raw = [load("w2_raw0", w2[:, 0:P], [(nc.sync, j, j + 1) for j in range(PACK)])]
+        w2_raw.append(load("w2_raw1", w2[:, P:N]))
         nc.sync.dma_start(offsets[:], offs)
 
         preload = keep.tile([P, 1], F32, name="preload")
@@ -146,12 +146,9 @@ def tile_picked_shuffle_mlp_gelu_perm_l_kernel(tc, xT, w1, w2, offs, out):
 
         w2_q = quantised("w2", N)
 
-        def prepare_w2(m, tag=None):
-            grouped = staged("w2_grouped%d" % m, P, tag)
-            cast(vector_copy, grouped, w2_raw[m], 0, P)
-            quantize(w2_q, P * m, grouped, 0, P)
-
-        prepare_w2(0)
+        w2_early = staged("w2_early", P)
+        cast(vector_copy, w2_early, w2_raw[0], 0, P)
+        quantize(w2_q, 0, w2_early, 0, P)
 
         h = keep.tile([P, H], BF16, name="h", tag="h", align_bytes=ALIGN)
         for index, (c0, width) in enumerate(GROUPS):
@@ -164,7 +161,11 @@ def tile_picked_shuffle_mlp_gelu_perm_l_kernel(tc, xT, w1, w2, offs, out):
         )
         nc.scalar.activation(gathered[:, 0:split], h[:].indirect(offsets[:, 0:SCALAR_LIST_COLUMNS]), COPY)
 
-        prepare_w2(1, "h")
+        w2_late = staged("w2_late", P, "h")
+        cast(scalar_copy, w2_late, w2_raw[1], 0, 64)
+        cast(vector_copy, w2_late, w2_raw[1], 64, P)
+        quantize(w2_q, P, w2_late, 0, 64)
+        quantize(w2_q, P, w2_late, 64, P)
 
         words = gathered[:].bitcast(F32)
         for u in range(2):

@@ -79,8 +79,8 @@ def tile_picked_shuffle_mlp_gelu_perm_l_kernel(tc, xT, w1, w2, offs, out):
 
         offsets = keep.tile([P, H // LIST_ROWS], U16, name="offsets")
         first_raw = load("first_raw", w1[0:KP, :], ((nc.sync, 0, 2), (nc.scalar, 2, 4)))
-        x0_raw = load("x0_raw", xT[0:KP, :])
         wide_raw = load("wide_raw", w1[KP:K, 0:256])
+        x0_raw = load("x0_raw", xT[0:KP, :])
         x1_raw = load("x1_raw", xT[KP:K, :])
         third_raw = load("third_raw", w1[KP:K, 256:384])
         last_raw = load("last_raw", w1[KP:K, 384:512], tag="h")
@@ -103,20 +103,20 @@ def tile_picked_shuffle_mlp_gelu_perm_l_kernel(tc, xT, w1, w2, offs, out):
         w1_q = quantised("w1", 2 * H)
 
         first = staged("first", H)
-        cast(vector_copy, first, first_raw, 0, 320)
-        cast(scalar_copy, first, first_raw, 320, H)
+        cast(vector_copy, first, first_raw, 0, 288)
+        cast(scalar_copy, first, first_raw, 288, H)
         quantize(w1_q, 0, first, 0, H // 2)
         quantize(w1_q, 0, first, H // 2, H)
 
         x0, x1 = staged("x0", T), staged("x1", T)
-        cast(scalar_copy, x0, x0_raw, 0, T)
-        quantize(x_q, 0, x0, 0, T)
-
         wide = staged("wide", 2 * P)
         cast(vector_copy, wide, wide_raw, 0, 160)
         cast(scalar_copy, wide, wide_raw, 160, 2 * P)
-        cast(vector_copy, x1, x1_raw, 0, T)
-        quantize(w1_q, H, wide, 0, 2 * P)
+        cast(scalar_copy, x0, x0_raw, 0, T)
+        cast(scalar_copy, x1, x1_raw, 0, T)
+        quantize(w1_q, H, wide, 0, P)
+        quantize(w1_q, H, wide, P, 2 * P)
+        quantize(x_q, 0, x0, 0, T)
         quantize(x_q, T, x1, 0, T)
 
         def first_layer(g, index):

@@ -21,7 +21,7 @@ KP = P * PACK
 BANK = 512
 LIST_ROWS = 16
 ALIGN = 512
-GROUPS = ((0, 256), (256, 128), (384, 128))
+GROUPS = ((0, 128), (128, 128), (256, 128), (384, 128))
 SCALAR_LIST_COLUMNS = 16
 
 
@@ -97,14 +97,14 @@ def tile_picked_shuffle_mlp_gelu_perm_l_kernel(tc, xT, w1, w2, offs, out):
         make_identity(nc, identity[:])
 
         banks = [psum.tile([P, BANK], F32, name="bank%d" % b) for b in range(8)]
-        acc, turned, out_banks = banks[0:3], banks[3], banks[4:7]
+        acc, turned, out_banks = banks[0:4], banks[4], banks[5:8]
 
         x_q = quantised("x", 2 * T)
         w1_q = quantised("w1", 2 * H)
 
         first = staged("first", H)
-        cast(vector_copy, first, first_raw, 0, 288)
-        cast(scalar_copy, first, first_raw, 288, H)
+        cast(vector_copy, first, first_raw, 0, 352)
+        cast(scalar_copy, first, first_raw, 352, H)
         quantize(w1_q, 0, first, 0, H // 2)
         quantize(w1_q, 0, first, H // 2, H)
 
@@ -127,6 +127,7 @@ def tile_picked_shuffle_mlp_gelu_perm_l_kernel(tc, xT, w1, w2, offs, out):
         for index in range(len(GROUPS)):
             first_layer(0, index)
         first_layer(1, 0)
+        first_layer(1, 1)
 
         third, last = staged("third", P), staged("last", P)
         cast(scalar_copy, third, third_raw, 0, 96)
@@ -137,10 +138,10 @@ def tile_picked_shuffle_mlp_gelu_perm_l_kernel(tc, xT, w1, w2, offs, out):
         cast(scalar_copy, last, last_raw, 96, P)
         quantize(w1_q, H + 256, third, 0, 64)
         quantize(w1_q, H + 256, third, 64, P)
-        first_layer(1, 1)
+        first_layer(1, 2)
         for c0 in (64, 0, 32, 96):
             quantize(w1_q, H + 384, last, c0, c0 + 32)
-        first_layer(1, 2)
+        first_layer(1, 3)
 
         nc.tensor.transpose(banks[7][:, 0:P], identity[:], identity[:])
 

@@ -21,7 +21,7 @@ KP = P * PACK
 BANK = 512
 LIST_ROWS = 16
 ALIGN = 512
-GROUPS = ((0, 128), (128, 128), (256, 128), (384, 128))
+GROUPS = ((0, 256), (256, 128), (384, 128))
 SCALAR_LIST_COLUMNS = 16
 
 
@@ -97,16 +97,19 @@ def tile_picked_shuffle_mlp_gelu_perm_l_kernel(tc, xT, w1, w2, offs, out):
         make_identity(nc, identity[:])
 
         banks = [psum.tile([P, BANK], F32, name="bank%d" % b) for b in range(8)]
-        acc, turned, out_banks = banks[0:4], banks[4], banks[5:8]
+        acc, turned, out_banks = banks[0:3], banks[3], banks[4:7]
 
         x_q = quantised("x", 2 * T)
         w1_q = quantised("w1", 2 * H)
 
         first = staged("first", H)
-        cast(vector_copy, first, first_raw, 0, 352)
-        cast(scalar_copy, first, first_raw, 352, H)
+        cast(vector_copy, first, first_raw, 0, 384)
+        cast(scalar_copy, first, first_raw, 384, H)
         quantize(w1_q, 0, first, 0, H // 2)
-        quantize(w1_q, 0, first, H // 2, H)
+        quantize(w1_q, 0, first, 256, 384)
+        held_codes = keep.tile([P, P], U32, name="held_codes", align_bytes=ALIGN)
+        held_q = (held_codes, x_q[1][4:P, T : 2 * T])
+        quantize(held_q, -384, first, 384, H)
 
         x0, x1 = staged("x0", T), staged("x1", T)
         wide = staged("wide", 2 * P)
@@ -124,10 +127,10 @@ def tile_picked_shuffle_mlp_gelu_perm_l_kernel(tc, xT, w1, w2, offs, out):
             channels = slice(g * H + c0, g * H + c0 + width)
             product(acc[index][:, 0:width], x_q, slice(g * T, (g + 1) * T), w1_q, channels, g == 0, g == 1)
 
-        for index in range(len(GROUPS)):
-            first_layer(0, index)
+        first_layer(0, 0)
+        first_layer(0, 1)
         first_layer(1, 0)
-        first_layer(1, 1)
+        product(acc[2][:, 0:P], x_q, slice(0, T), held_q, slice(0, P), True, False)
 
         third, last = staged("third", P), staged("last", P)
         cast(scalar_copy, third, third_raw, 0, 96)
@@ -138,10 +141,10 @@ def tile_picked_shuffle_mlp_gelu_perm_l_kernel(tc, xT, w1, w2, offs, out):
         cast(scalar_copy, last, last_raw, 96, P)
         quantize(w1_q, H + 256, third, 0, 64)
         quantize(w1_q, H + 256, third, 64, P)
-        first_layer(1, 2)
+        first_layer(1, 1)
         for c0 in (64, 0, 32, 96):
             quantize(w1_q, H + 384, last, c0, c0 + 32)
-        first_layer(1, 3)
+        first_layer(1, 2)
 
         nc.tensor.transpose(banks[7][:, 0:P], identity[:], identity[:])
 

@@ -113,8 +113,8 @@ def tile_picked_shuffle_mlp_gelu_perm_l_kernel(tc, xT, w1, w2, offs, out):
 
         x0, x1 = staged("x0", T), staged("x1", T)
         wide = staged("wide", 2 * P)
-        cast(vector_copy, wide, wide_raw, 0, 160)
-        cast(scalar_copy, wide, wide_raw, 160, 2 * P)
+        cast(vector_copy, wide, wide_raw, 0, 192)
+        cast(scalar_copy, wide, wide_raw, 192, 2 * P)
         cast(scalar_copy, x0, x0_raw, 0, T)
         cast(scalar_copy, x1, x1_raw, 0, T)
         quantize(w1_q, H, wide, 0, P)

@@ -93,8 +93,10 @@ def tile_picked_shuffle_mlp_gelu_perm_l_kernel(tc, xT, w1, w2, offs, out):
         nc.vector.memset(preload[:], 0.0)
         nc.scalar.activation(preload_out[:], preload[:], GELU)
 
+        identity_made = keep.tile([P, P], F32, name="identity_made", align_bytes=ALIGN)
         identity = keep.tile([P, P], F32, name="identity", align_bytes=ALIGN)
-        make_identity(nc, identity[:])
+        make_identity(nc, identity_made[:])
+        vector_copy(identity[:], identity_made[:])
 
         banks = [psum.tile([P, BANK], F32, name="bank%d" % b) for b in range(8)]
         acc, turned, out_banks = banks[0:3], banks[3], banks[4:7]
@@ -146,7 +148,7 @@ def tile_picked_shuffle_mlp_gelu_perm_l_kernel(tc, xT, w1, w2, offs, out):
             quantize(w1_q, H + 384, last, c0, c0 + 32)
         first_layer(1, 2)
 
-        nc.tensor.transpose(banks[7][:, 0:P], identity[:], identity[:])
+        product(banks[7][:, 0:P], x_q, slice(T, 2 * T), w1_q, slice(H + 384, 2 * H), True, True)
 
         w2_q = quantised("w2", N)
 

@@ -115,8 +115,8 @@ def tile_picked_shuffle_mlp_gelu_perm_l_kernel(tc, xT, w1, w2, offs, out):
 
         x0, x1 = staged("x0", T), staged("x1", T)
         wide = staged("wide", 2 * P)
-        cast(vector_copy, wide, wide_raw, 0, 192)
-        cast(scalar_copy, wide, wide_raw, 192, 2 * P)
+        cast(vector_copy, wide, wide_raw, 0, 208)
+        cast(scalar_copy, wide, wide_raw, 208, 2 * P)
         cast(scalar_copy, x0, x0_raw, 0, T)
         cast(scalar_copy, x1, x1_raw, 0, T)
         quantize(w1_q, H, wide, 0, P)

@@ -85,8 +85,8 @@ def tile_picked_shuffle_mlp_gelu_perm_l_kernel(tc, xT, w1, w2, offs, out):
         third_raw = load("third_raw", w1[KP:K, 256:384])
         last_raw = load("last_raw", w1[KP:K, 384:512], tag="h")
         w2_raw = [load("w2_raw0", w2[:, 0:P], [(nc.sync, j, j + 1) for j in range(PACK)])]
-        w2_raw.append(load("w2_raw1", w2[:, P:N]))
         nc.sync.dma_start(offsets[:], offs)
+        w2_raw.append(load("w2_raw1", w2[:, P:N], tag="third_raw"))
 
         preload = keep.tile([P, 1], F32, name="preload")
         preload_out = keep.tile([P, 1], F32, name="preload_out")
@@ -167,7 +167,7 @@ def tile_picked_shuffle_mlp_gelu_perm_l_kernel(tc, xT, w1, w2, offs, out):
         )
         nc.scalar.activation(gathered[:, 0:split], h[:].indirect(offsets[:, 0:SCALAR_LIST_COLUMNS]), COPY)
 
-        w2_late = staged("w2_late", P, "h")
+        w2_late = staged("w2_late", P)
         cast(scalar_copy, w2_late, w2_raw[1], 0, 64)
         cast(vector_copy, w2_late, w2_raw[1], 64, P)
         quantize(w2_q, P, w2_late, 0, 64)

@@ -108,10 +108,11 @@ def tile_picked_shuffle_mlp_gelu_perm_l_kernel(tc, xT, w1, w2, offs, out):
         cast(vector_copy, first, first_raw, 0, 384)
         cast(scalar_copy, first, first_raw, 384, H)
         quantize(w1_q, 0, first, 0, H // 2)
-        quantize(w1_q, 0, first, 256, 384)
-        held_codes = keep.tile([P, P], U32, name="held_codes", align_bytes=ALIGN)
-        held_q = (held_codes, x_q[1][4:P, T : 2 * T])
-        quantize(held_q, -384, first, 384, H)
+        held_q = []
+        for index in (1, 2):
+            held_codes = keep.tile([P, P], U32, name="held_codes%d" % index, align_bytes=ALIGN)
+            held_q.append((held_codes, x_q[1][4 * index : P, T : 2 * T]))
+            quantize(held_q[-1], -GROUPS[index][0], first, GROUPS[index][0], GROUPS[index][0] + P)
 
         x0, x1 = staged("x0", T), staged("x1", T)
         wide = staged("wide", 2 * P)
@@ -130,9 +131,9 @@ def tile_picked_shuffle_mlp_gelu_perm_l_kernel(tc, xT, w1, w2, offs, out):
             product(acc[index][:, 0:width], x_q, slice(g * T, (g + 1) * T), w1_q, channels, g == 0, g == 1)
 
         first_layer(0, 0)
-        first_layer(0, 1)
         first_layer(1, 0)
-        product(acc[2][:, 0:P], x_q, slice(0, T), held_q, slice(0, P), True, False)
+        for index in (1, 2):
+            product(acc[index][:, 0:P], x_q, slice(0, T), held_q[index - 1], slice(0, P), True, False)
 
         third, last = staged("third", P), staged("last", P)
         cast(scalar_copy, third, third_raw, 0, 96)

@@ -139,13 +139,13 @@ def tile_picked_shuffle_mlp_gelu_perm_l_kernel(tc, xT, w1, w2, offs, out):
         cast(scalar_copy, third, third_raw, 0, 96)
         cast(vector_copy, third, third_raw, 96, P)
         cast(vector_copy, last, last_raw, 0, 32)
-        cast(scalar_copy, last, last_raw, 64, 96)
+        cast(scalar_copy, last, last_raw, 80, P)
         cast(vector_copy, last, last_raw, 32, 64)
-        cast(scalar_copy, last, last_raw, 96, P)
+        cast(vector_copy, last, last_raw, 64, 80)
         quantize(w1_q, H + 256, third, 0, 64)
         quantize(w1_q, H + 256, third, 64, P)
         first_layer(1, 1)
-        for c0 in (64, 0, 32, 96):
+        for c0 in (0, 32, 96, 64):
             quantize(w1_q, H + 384, last, c0, c0 + 32)
         first_layer(1, 2)
 
@@ -181,10 +181,11 @@ def tile_picked_shuffle_mlp_gelu_perm_l_kernel(tc, xT, w1, w2, offs, out):
         h_q = quantised("h", T)
         turned_words = turned[:, 0 : 2 * P].rearrange("p (u t) -> p t u", u=2)
         halves = (slice(0, T // 2), slice(T // 2, T))
-        for half, tokens in enumerate(halves):
-            grouped = staged("h_grouped%d" % half, T // 2)
+        for part, tokens in enumerate(slice(t, t + 32) for t in range(0, T, 32)):
+            width = tokens.stop - tokens.start
+            grouped = staged("h_grouped%d" % part, width)
             scalar_copy(grouped[:].bitcast(F32).rearrange("p (t u) -> p t u", u=2), turned_words[:, tokens])
-            quantize(h_q, tokens.start, grouped, 0, T // 2)
+            quantize(h_q, tokens.start, grouped, 0, width)
 
         y = [keep.tile([P, T], F32, name="y%d" % m, align_bytes=ALIGN) for m in range(N // P)]
         steps = (

@@ -149,13 +149,12 @@ def tile_picked_shuffle_mlp_gelu_perm_l_kernel(tc, xT, w1, w2, offs, out):
             quantize(w1_q, H + 384, last, c0, c0 + 32)
         first_layer(1, 2)
 
-        product(banks[7][:, 0:P], x_q, slice(T, 2 * T), w1_q, slice(H + 384, 2 * H), True, True)
-
         w2_q = quantised("w2", N)
 
         w2_early = staged("w2_early", P)
         cast(vector_copy, w2_early, w2_raw[0], 0, P)
         quantize(w2_q, 0, w2_early, 0, P)
+        nc.tensor.transpose(banks[7][:, P : 2 * P], w2_early[:].bitcast(F32)[:, 0:P], identity[:])
 
         h = keep.tile([P, H], BF16, name="h", tag="h", align_bytes=ALIGN)
         for index, (c0, width) in enumerate(GROUPS):
@@ -177,6 +176,8 @@ def tile_picked_shuffle_mlp_gelu_perm_l_kernel(tc, xT, w1, w2, offs, out):
         words = gathered[:].bitcast(F32)
         for u in range(2):
             nc.tensor.transpose(turned[:, u * P : (u + 1) * P], words[:, u : 2 * P : 2], identity[:])
+
+        product(banks[7][:, 0:64], w2_q, slice(0, P), w2_q, slice(P + 64, N), True, True)
 
         h_q = quantised("h", T)
         turned_words = turned[:, 0 : 2 * P].rearrange("p (u t) -> p t u", u=2)

@@ -180,12 +180,15 @@ def tile_picked_shuffle_mlp_gelu_perm_l_kernel(tc, xT, w1, w2, offs, out):
         product(banks[7][:, 0:64], w2_q, slice(0, P), w2_q, slice(P + 64, N), True, True)
 
         h_q = quantised("h", T)
-        turned_words = turned[:, 0 : 2 * P].rearrange("p (u t) -> p t u", u=2)
+        turned_pairs = turned[:, 0 : 2 * P].rearrange("p (u c i) -> p c u i", u=2, i=2)
         halves = (slice(0, T // 2), slice(T // 2, T))
         for part, tokens in enumerate(slice(t, t + 32) for t in range(0, T, 32)):
             width = tokens.stop - tokens.start
             grouped = staged("h_grouped%d" % part, width)
-            scalar_copy(grouped[:].bitcast(F32).rearrange("p (t u) -> p t u", u=2), turned_words[:, tokens])
+            scalar_copy(
+                grouped[:].bitcast(F32).rearrange("p (c i u) -> p c u i", i=2, u=2),
+                turned_pairs[:, tokens.start // 2 : tokens.stop // 2],
+            )
             quantize(h_q, tokens.start, grouped, 0, width)
 
         y = [keep.tile([P, T], F32, name="y%d" % m, align_bytes=ALIGN) for m in range(N // P)]

@@ -116,10 +116,11 @@ def tile_picked_shuffle_mlp_gelu_perm_l_kernel(tc, xT, w1, w2, offs, out):
 
         x0, x1 = staged("x0", T), staged("x1", T)
         wide = staged("wide", 2 * P)
-        cast(vector_copy, wide, wide_raw, 0, 208)
-        cast(scalar_copy, wide, wide_raw, 208, 2 * P)
+        cast(vector_copy, wide, wide_raw, 0, 160)
+        cast(scalar_copy, wide, wide_raw, 160, 2 * P)
         cast(scalar_copy, x0, x0_raw, 0, T)
-        cast(scalar_copy, x1, x1_raw, 0, T)
+        cast(scalar_copy, x1, x1_raw, 32, T)
+        cast(vector_copy, x1, x1_raw, 0, 32)
         quantize(w1_q, H, wide, 0, P)
         quantize(w1_q, H, wide, P, 2 * P)
         quantize(x_q, 0, x0, 0, T)
@@ -139,13 +140,13 @@ def tile_picked_shuffle_mlp_gelu_perm_l_kernel(tc, xT, w1, w2, offs, out):
         cast(scalar_copy, third, third_raw, 0, 96)
         cast(vector_copy, third, third_raw, 96, P)
         cast(vector_copy, last, last_raw, 0, 32)
-        cast(scalar_copy, last, last_raw, 80, P)
-        cast(vector_copy, last, last_raw, 32, 64)
-        cast(vector_copy, last, last_raw, 64, 80)
+        cast(scalar_copy, last, last_raw, 96, P)
+        cast(scalar_copy, last, last_raw, 72, 96)
+        cast(vector_copy, last, last_raw, 32, 72)
         quantize(w1_q, H + 256, third, 0, 64)
         quantize(w1_q, H + 256, third, 64, P)
         first_layer(1, 1)
-        for c0 in (0, 32, 96, 64):
+        for c0 in (0, 96, 32, 64):
             quantize(w1_q, H + 384, last, c0, c0 + 32)
         first_layer(1, 2)
 
@@ -154,7 +155,6 @@ def tile_picked_shuffle_mlp_gelu_perm_l_kernel(tc, xT, w1, w2, offs, out):
         w2_early = staged("w2_early", P)
         cast(vector_copy, w2_early, w2_raw[0], 0, P)
         quantize(w2_q, 0, w2_early, 0, P)
-        nc.tensor.transpose(banks[7][:, P : 2 * P], w2_early[:].bitcast(F32)[:, 0:P], identity[:])
 
         h = keep.tile([P, H], BF16, name="h", tag="h", align_bytes=ALIGN)
         for index, (c0, width) in enumerate(GROUPS):
@@ -176,8 +176,6 @@ def tile_picked_shuffle_mlp_gelu_perm_l_kernel(tc, xT, w1, w2, offs, out):
         words = gathered[:].bitcast(F32)
         for u in range(2):
             nc.tensor.transpose(turned[:, u * P : (u + 1) * P], words[:, u : 2 * P : 2], identity[:])
-
-        product(banks[7][:, 0:64], w2_q, slice(0, P), w2_q, slice(P + 64, N), True, True)
 
         h_q = quantised("h", T)
         turned_pairs = turned[:, 0 : 2 * P].rearrange("p (u c i) -> p c u i", u=2, i=2)

@@ -14,6 +14,8 @@ U8 = mybir.dt.uint8
 FP8X4 = mybir.dt.float8_e4m3fn_x4
 GELU = mybir.ActivationFunctionType.Gelu_apprx_tanh
 COPY = mybir.ActivationFunctionType.Copy
+MULT = mybir.AluOpType.mult
+ADD = mybir.AluOpType.add
 
 P = 128
 PACK = 4
@@ -33,6 +35,9 @@ def tile_picked_shuffle_mlp_gelu_perm_l_kernel(tc, xT, w1, w2, offs, out):
 
     def scalar_copy(dst, src):
         nc.scalar.copy(dst, src)
+
+    def gpsimd_copy(dst, src):
+        nc.gpsimd.tensor_scalar(out=dst, in0=src, scalar1=1.0, scalar2=0.0, op0=MULT, op1=ADD)
 
     def cast(copy, grouped, raw, c0, c1):
         copy(
@@ -152,8 +157,8 @@ def tile_picked_shuffle_mlp_gelu_perm_l_kernel(tc, xT, w1, w2, offs, out):
 
         w2_q = quantised("w2", N)
 
-        w2_early = staged("w2_early", P)
-        cast(vector_copy, w2_early, w2_raw[0], 0, P)
+        w2_early = staged("w2_early", P, tag="last")
+        cast(gpsimd_copy, w2_early, w2_raw[0], 0, P)
         quantize(w2_q, 0, w2_early, 0, P)
 
         h = keep.tile([P, H], BF16, name="h", tag="h", align_bytes=ALIGN)

@@ -84,12 +84,15 @@ def tile_picked_shuffle_mlp_gelu_perm_l_kernel(tc, xT, w1, w2, offs, out):
 
         offsets = keep.tile([P, H // LIST_ROWS], U16, name="offsets")
         first_raw = load("first_raw", w1[0:KP, :], ((nc.sync, 0, 2), (nc.scalar, 2, 4)))
+        x_raw = keep.tile([P, 2, PACK, T], F32, name="x_raw", align_bytes=ALIGN)
+        nc.sync.dma_start(out=x_raw[:], in_=xT.rearrange("(g p j) c -> p g j c", g=2, j=PACK))
         wide_raw = load("wide_raw", w1[KP:K, 0:256])
-        x0_raw = load("x0_raw", xT[0:KP, :])
-        x1_raw = load("x1_raw", xT[KP:K, :])
         third_raw = load("third_raw", w1[KP:K, 256:384])
         last_raw = load("last_raw", w1[KP:K, 384:512], tag="h")
-        w2_raw = [load("w2_raw0", w2[:, 0:P], [(nc.sync, j, j + 1) for j in range(PACK)])]
+        w2_raw = [load("w2_raw0", w2[:, 0:P], [(nc.sync, j, j + 1) for j in range(PACK - 1)])]
+        w2_dealt = w2[:, 0:P].rearrange("(p j) c -> p j c", j=PACK)
+        for p0 in (0, P // 2):
+            nc.sync.dma_start(out=w2_raw[0][p0 : p0 + P // 2, 3:4], in_=w2_dealt[p0 : p0 + P // 2, 3:4])
         nc.sync.dma_start(offsets[:], offs)
         w2_raw.append(load("w2_raw1", w2[:, P:N], tag="third_raw"))
 
@@ -106,40 +109,45 @@ def tile_picked_shuffle_mlp_gelu_perm_l_kernel(tc, xT, w1, w2, offs, out):
         banks = [psum.tile([P, BANK], F32, name="bank%d" % b) for b in range(8)]
         acc, turned, out_banks = banks[0:3], banks[3], banks[4:7]
 
-        x_q = quantised("x", 2 * T)
         w1_q = quantised("w1", 2 * H)
+        x0_codes = keep.tile([P, T], U32, name="x0_codes", align_bytes=ALIGN)
+        x_q = [(x0_codes, w1_q[1][4:P, H - 64 : H + 64]), quantised("x1", T)]
 
         first = staged("first", H)
-        cast(vector_copy, first, first_raw, 0, 384)
-        cast(scalar_copy, first, first_raw, 384, H)
+        cast(vector_copy, first, first_raw, 0, 320)
+        cast(scalar_copy, first, first_raw, 320, H)
         quantize(w1_q, 0, first, 0, H // 2)
         held_q = []
         for index in (1, 2):
             held_codes = keep.tile([P, P], U32, name="held_codes%d" % index, align_bytes=ALIGN)
-            held_q.append((held_codes, x_q[1][4 * index : P, T : 2 * T]))
+            held_q.append((held_codes, w1_q[1][8 * index - 4 : P, H + P : H + 2 * P]))
             quantize(held_q[-1], -GROUPS[index][0], first, GROUPS[index][0], GROUPS[index][0] + P)
 
         x0, x1 = staged("x0", T), staged("x1", T)
         wide = staged("wide", 2 * P)
-        cast(vector_copy, wide, wide_raw, 0, 160)
-        cast(scalar_copy, wide, wide_raw, 160, 2 * P)
-        cast(scalar_copy, x0, x0_raw, 0, T)
-        cast(scalar_copy, x1, x1_raw, 32, T)
-        cast(vector_copy, x1, x1_raw, 0, 32)
-        quantize(w1_q, H, wide, 0, P)
-        quantize(w1_q, H, wide, P, 2 * P)
-        quantize(x_q, 0, x0, 0, T)
-        quantize(x_q, T, x1, 0, T)
+        cast(scalar_copy, x0, x_raw[:, 0], 0, T)
+        cast(vector_copy, x1, x_raw[:, 1], 0, 64)
+        cast(scalar_copy, x1, x_raw[:, 1], 64, T)
+        quantize(x_q[0], 0, x0, 0, T)
+        quantize(x_q[1], 0, x1, 0, T)
+        cast(scalar_copy, wide, wide_raw, 0, 32)
+        cast(vector_copy, wide, wide_raw, 32, 64)
+        cast(vector_copy, wide, wide_raw, 64, P)
+        cast(vector_copy, wide, wide_raw, P, 176)
+        cast(scalar_copy, wide, wide_raw, 176, 2 * P)
+        for c0, c1 in ((0, 64), (64, P), (P, 2 * P)):
+            quantize(w1_q, H, wide, c0, c1)
 
         def first_layer(g, index):
             c0, width = GROUPS[index]
             channels = slice(g * H + c0, g * H + c0 + width)
-            product(acc[index][:, 0:width], x_q, slice(g * T, (g + 1) * T), w1_q, channels, g == 0, g == 1)
+            product(acc[index][:, 0:width], x_q[g], slice(0, T), w1_q, channels, g == 0, g == 1)
 
         first_layer(0, 0)
-        first_layer(1, 0)
+        for c0 in (0, P):
+            product(acc[0][:, c0 : c0 + P], x_q[1], slice(0, T), w1_q, slice(H + c0, H + c0 + P), False, c0 == P)
         for index in (1, 2):
-            product(acc[index][:, 0:P], x_q, slice(0, T), held_q[index - 1], slice(0, P), True, False)
+            product(acc[index][:, 0:P], x_q[0], slice(0, T), held_q[index - 1], slice(0, P), True, False)
 
         third, last = staged("third", P), staged("last", P)
         cast(scalar_copy, third, third_raw, 0, 96)

@@ -110,17 +110,17 @@ def tile_picked_shuffle_mlp_gelu_perm_l_kernel(tc, xT, w1, w2, offs, out):
         acc, turned, out_banks = banks[0:3], banks[3], banks[4:7]
 
         w1_q = quantised("w1", 2 * H)
-        x0_codes = keep.tile([P, T], U32, name="x0_codes", align_bytes=ALIGN)
-        x_q = [(x0_codes, w1_q[1][4:P, H - 64 : H + 64]), quantised("x1", T)]
+        x_q = [quantised("x0", T), quantised("x1", T)]
+        gated_q = (w1_q[0][:, 0 : 2 * P], w1_q[1][4:P, H - 192 : H + 64])
 
         first = staged("first", H)
         cast(vector_copy, first, first_raw, 0, 320)
         cast(scalar_copy, first, first_raw, 320, H)
-        quantize(w1_q, 0, first, 0, H // 2)
+        quantize(gated_q, 0, first, 0, H // 2)
         held_q = []
         for index in (1, 2):
             held_codes = keep.tile([P, P], U32, name="held_codes%d" % index, align_bytes=ALIGN)
-            held_q.append((held_codes, w1_q[1][8 * index - 4 : P, H + P : H + 2 * P]))
+            held_q.append((held_codes, x_q[1][1][4:P, :] if index == 1 else w1_q[1][4:P, H + P : H + 2 * P]))
             quantize(held_q[-1], -GROUPS[index][0], first, GROUPS[index][0], GROUPS[index][0] + P)
 
         x0, x1 = staged("x0", T), staged("x1", T)
@@ -143,11 +143,11 @@ def tile_picked_shuffle_mlp_gelu_perm_l_kernel(tc, xT, w1, w2, offs, out):
             channels = slice(g * H + c0, g * H + c0 + width)
             product(acc[index][:, 0:width], x_q[g], slice(0, T), w1_q, channels, g == 0, g == 1)
 
-        first_layer(0, 0)
+        product(acc[1][:, 0:P], x_q[0], slice(0, T), held_q[0], slice(0, P), True, False)
+        product(acc[0][:, 0 : 2 * P], x_q[0], slice(0, T), gated_q, slice(0, 2 * P), True, False)
         for c0 in (0, P):
             product(acc[0][:, c0 : c0 + P], x_q[1], slice(0, T), w1_q, slice(H + c0, H + c0 + P), False, c0 == P)
-        for index in (1, 2):
-            product(acc[index][:, 0:P], x_q[0], slice(0, T), held_q[index - 1], slice(0, P), True, False)
+        product(acc[2][:, 0:P], x_q[0], slice(0, T), held_q[1], slice(0, P), True, False)
 
         third, last = staged("third", P), staged("last", P)
         cast(scalar_copy, third, third_raw, 0, 96)

@@ -162,6 +162,7 @@ def tile_picked_shuffle_mlp_gelu_perm_l_kernel(tc, xT, w1, w2, offs, out):
         for c0 in (0, 96, 32, 64):
             quantize(w1_q, H + 384, last, c0, c0 + 32)
         first_layer(1, 2)
+        product(banks[7][:, 0:P], x_q[1], slice(0, T), w1_q, slice(H + 3 * P, 2 * H), True, True)
 
         w2_q = quantised("w2", N)
 

@@ -83,16 +83,17 @@ def tile_picked_shuffle_mlp_gelu_perm_l_kernel(tc, xT, w1, w2, offs, out):
             return codes, scales
 
         offsets = keep.tile([P, H // LIST_ROWS], U16, name="offsets")
-        first_raw = load("first_raw", w1[0:KP, :], ((nc.sync, 0, 2), (nc.scalar, 2, 4)))
+        first_raw = load("first_raw", w1[0:KP, :], ((nc.sync, 0, PACK),))
         x_raw = keep.tile([P, 2, PACK, T], F32, name="x_raw", align_bytes=ALIGN)
         nc.sync.dma_start(out=x_raw[:], in_=xT.rearrange("(g p j) c -> p g j c", g=2, j=PACK))
         wide_raw = load("wide_raw", w1[KP:K, 0:256])
         third_raw = load("third_raw", w1[KP:K, 256:384])
         last_raw = load("last_raw", w1[KP:K, 384:512], tag="h")
-        w2_raw = [load("w2_raw0", w2[:, 0:P], [(nc.sync, j, j + 1) for j in range(PACK - 1)])]
+        w2_raw = [load("w2_raw0", w2[:, 0:P], [(nc.sync, j, j + 1) for j in range(2)])]
         w2_dealt = w2[:, 0:P].rearrange("(p j) c -> p j c", j=PACK)
-        for p0 in (0, P // 2):
-            nc.sync.dma_start(out=w2_raw[0][p0 : p0 + P // 2, 3:4], in_=w2_dealt[p0 : p0 + P // 2, 3:4])
+        for j in (2, 3):
+            for c0 in (0, 64):
+                nc.sync.dma_start(out=w2_raw[0][:, j, c0 : c0 + 64], in_=w2_dealt[:, j, c0 : c0 + 64])
         nc.sync.dma_start(offsets[:], offs)
         w2_raw.append(load("w2_raw1", w2[:, P:N], tag="third_raw"))
 
@@ -205,9 +206,9 @@ def tile_picked_shuffle_mlp_gelu_perm_l_kernel(tc, xT, w1, w2, offs, out):
 
         y = [keep.tile([P, T], F32, name="y%d" % m, align_bytes=ALIGN) for m in range(N // P)]
         steps = (
-            (0, halves[0], vector_copy, nc.sync),
-            (1, slice(0, T), scalar_copy, nc.sync),
-            (0, halves[1], vector_copy, nc.scalar),
+            (0, halves[0], scalar_copy, nc.scalar),
+            (1, slice(0, T), vector_copy, nc.sync),
+            (0, halves[1], scalar_copy, nc.scalar),
         )
         for bank, (m, tokens, copy, queue) in zip(out_banks, steps):
             width = tokens.stop - tokens.start

@@ -65,6 +65,7 @@ def tile_picked_shuffle_mlp_gelu_perm_l_kernel(tc, xT, w1, w2, offs, out):
 
     with ExitStack() as ctx:
         keep = ctx.enter_context(tc.tile_pool(name="keep", bufs=1))
+        shared = ctx.enter_context(tc.tile_pool(name="shared", bufs=1))
         psum = ctx.enter_context(tc.psum_pool(name="psum", bufs=1))
 
         def load(name, rows, parts=((nc.sync, 0, PACK),), tag=None):
@@ -83,54 +84,57 @@ def tile_picked_shuffle_mlp_gelu_perm_l_kernel(tc, xT, w1, w2, offs, out):
             return codes, scales
 
         offsets = keep.tile([P, H // LIST_ROWS], U16, name="offsets")
-        first_raw = load("first_raw", w1[0:KP, :], ((nc.sync, 0, PACK),))
-        x_raw = keep.tile([P, 2, PACK, T], F32, name="x_raw", align_bytes=ALIGN)
-        nc.sync.dma_start(out=x_raw[:], in_=xT.rearrange("(g p j) c -> p g j c", g=2, j=PACK))
-        wide_raw = load("wide_raw", w1[KP:K, 0:256])
-        third_raw = load("third_raw", w1[KP:K, 256:384])
-        last_raw = load("last_raw", w1[KP:K, 384:512], tag="h")
-        w2_raw = [load("w2_raw0", w2[:, 0:P], [(nc.sync, j, j + 1) for j in range(2)])]
-        w2_dealt = w2[:, 0:P].rearrange("(p j) c -> p j c", j=PACK)
-        for j in (2, 3):
-            for c0 in (0, 64):
-                nc.sync.dma_start(out=w2_raw[0][:, j, c0 : c0 + 64], in_=w2_dealt[:, j, c0 : c0 + 64])
-        nc.sync.dma_start(offsets[:], offs)
-        w2_raw.append(load("w2_raw1", w2[:, P:N], tag="third_raw"))
+        def load_at(name, rows, parts, offset):
+            raw = shared.tile([P, PACK, rows.shape[1]], F32, name=name, offset=offset, align_bytes=ALIGN)
+            dealt = rows.rearrange("(p j) c -> p j c", j=PACK)
+            for queue, j0, j1 in parts:
+                queue.dma_start(out=raw[:, j0:j1], in_=dealt[:, j0:j1])
+            return raw
 
+        both = ((nc.sync, 0, 2), (nc.scalar, 2, PACK))
+        piece = PACK * P * 4
+        first_raw = load_at("first_raw", w1[0:KP, :], both, 0)
+        x_raw = [load("x_raw0", xT[0:KP, :]), load("x_raw1", xT[KP:K, :], ((nc.scalar, 0, PACK),))]
+        wide_raw = load("wide_raw", w1[KP:K, 0:256], both)
+        third_raw = load_at("third_raw", w1[KP:K, 256:384], both, 4 * piece)
         preload = keep.tile([P, 1], F32, name="preload")
         preload_out = keep.tile([P, 1], F32, name="preload_out")
-        nc.vector.memset(preload[:], 0.0)
+        nc.gpsimd.memset(preload[:], 0.0)
         nc.scalar.activation(preload_out[:], preload[:], GELU)
+
+        last_raw = load_at("last_raw", w1[KP:K, 384:512], both, 5 * piece)
+        nc.sync.dma_start(offsets[:], offs)
 
         identity_made = keep.tile([P, P], F32, name="identity_made", align_bytes=ALIGN)
         identity = keep.tile([P, P], F32, name="identity", align_bytes=ALIGN)
         make_identity(nc, identity_made[:])
         vector_copy(identity[:], identity_made[:])
 
+
         banks = [psum.tile([P, BANK], F32, name="bank%d" % b) for b in range(8)]
         acc, turned, out_banks = banks[0:3], banks[3], banks[4:7]
 
         w1_q = quantised("w1", 2 * H)
         x_q = [quantised("x0", T), quantised("x1", T)]
-        gated_q = (w1_q[0][:, 0 : 2 * P], w1_q[1][4:P, H - 192 : H + 64])
 
         first = staged("first", H)
-        cast(vector_copy, first, first_raw, 0, 320)
+        cast(vector_copy, first, first_raw, 0, 160)
+        cast(vector_copy, first, first_raw, 160, 320)
         cast(scalar_copy, first, first_raw, 320, H)
-        quantize(gated_q, 0, first, 0, H // 2)
-        held_q = []
-        for index in (1, 2):
-            held_codes = keep.tile([P, P], U32, name="held_codes%d" % index, align_bytes=ALIGN)
-            held_q.append((held_codes, x_q[1][1][4:P, :] if index == 1 else w1_q[1][4:P, H + P : H + 2 * P]))
-            quantize(held_q[-1], -GROUPS[index][0], first, GROUPS[index][0], GROUPS[index][0] + P)
+
+        w2_raw = [load_at("w2_raw0", w2[:, 0:P], ((nc.scalar, 0, PACK),), 0)]
 
         x0, x1 = staged("x0", T), staged("x1", T)
         wide = staged("wide", 2 * P)
-        cast(scalar_copy, x0, x_raw[:, 0], 0, T)
-        cast(vector_copy, x1, x_raw[:, 1], 0, 64)
-        cast(scalar_copy, x1, x_raw[:, 1], 64, T)
-        quantize(x_q[0], 0, x0, 0, T)
+        quantize(w1_q, 0, first, 0, P)
+        cast(vector_copy, x1, x_raw[1], 0, 96)
+        cast(scalar_copy, x1, x_raw[1], 96, T)
+        cast(scalar_copy, x0, x_raw[0], 0, T)
+        for c0 in (P, 3 * P, 2 * P):
+            quantize(w1_q, 0, first, c0, c0 + P)
         quantize(x_q[1], 0, x1, 0, T)
+        quantize(x_q[0], 0, x0, 0, T)
+        w2_raw.append(load("w2_raw1", w2[:, P:N], tag="x_raw0"))
         cast(scalar_copy, wide, wide_raw, 0, 32)
         cast(vector_copy, wide, wide_raw, 32, 64)
         cast(vector_copy, wide, wide_raw, 64, P)
@@ -144,11 +148,9 @@ def tile_picked_shuffle_mlp_gelu_perm_l_kernel(tc, xT, w1, w2, offs, out):
             channels = slice(g * H + c0, g * H + c0 + width)
             product(acc[index][:, 0:width], x_q[g], slice(0, T), w1_q, channels, g == 0, g == 1)
 
-        product(acc[1][:, 0:P], x_q[0], slice(0, T), held_q[0], slice(0, P), True, False)
-        product(acc[0][:, 0 : 2 * P], x_q[0], slice(0, T), gated_q, slice(0, 2 * P), True, False)
-        for c0 in (0, P):
-            product(acc[0][:, c0 : c0 + P], x_q[1], slice(0, T), w1_q, slice(H + c0, H + c0 + P), False, c0 == P)
-        product(acc[2][:, 0:P], x_q[0], slice(0, T), held_q[1], slice(0, P), True, False)
+        for index in range(len(GROUPS)):
+            first_layer(0, index)
+        first_layer(1, 0)
 
         third, last = staged("third", P), staged("last", P)
         cast(scalar_copy, third, third_raw, 0, 96)
@@ -163,7 +165,6 @@ def tile_picked_shuffle_mlp_gelu_perm_l_kernel(tc, xT, w1, w2, offs, out):
         for c0 in (0, 96, 32, 64):
             quantize(w1_q, H + 384, last, c0, c0 + 32)
         first_layer(1, 2)
-        product(banks[7][:, 0:P], x_q[1], slice(0, T), w1_q, slice(H + 3 * P, 2 * H), True, True)
 
         w2_q = quantised("w2", N)
 
@@ -171,7 +172,7 @@ def tile_picked_shuffle_mlp_gelu_perm_l_kernel(tc, xT, w1, w2, offs, out):
         cast(gpsimd_copy, w2_early, w2_raw[0], 0, P)
         quantize(w2_q, 0, w2_early, 0, P)
 
-        h = keep.tile([P, H], BF16, name="h", tag="h", align_bytes=ALIGN)
+        h = shared.tile([P, H], BF16, name="h", offset=5 * piece, align_bytes=ALIGN)
         for index, (c0, width) in enumerate(GROUPS):
             nc.scalar.activation(h[:, c0 : c0 + width], acc[index][:, 0:width], GELU)
 
@@ -182,7 +183,7 @@ def tile_picked_shuffle_mlp_gelu_perm_l_kernel(tc, xT, w1, w2, offs, out):
         )
         nc.scalar.activation(gathered[:, 0:split], h[:].indirect(offsets[:, 0:SCALAR_LIST_COLUMNS]), COPY)
 
-        w2_late = staged("w2_late", P)
+        w2_late = shared.tile([P, P * PACK], BF16, name="w2_late", offset=5 * piece, align_bytes=ALIGN)
         cast(scalar_copy, w2_late, w2_raw[1], 0, 64)
         cast(vector_copy, w2_late, w2_raw[1], 64, P)
         quantize(w2_q, P, w2_late, 0, 64)

@@ -65,7 +65,6 @@ def tile_picked_shuffle_mlp_gelu_perm_l_kernel(tc, xT, w1, w2, offs, out):
 
     with ExitStack() as ctx:
         keep = ctx.enter_context(tc.tile_pool(name="keep", bufs=1))
-        shared = ctx.enter_context(tc.tile_pool(name="shared", bufs=1))
         psum = ctx.enter_context(tc.psum_pool(name="psum", bufs=1))
 
         def load(name, rows, parts=((nc.sync, 0, PACK),), tag=None):
@@ -84,26 +83,24 @@ def tile_picked_shuffle_mlp_gelu_perm_l_kernel(tc, xT, w1, w2, offs, out):
             return codes, scales
 
         offsets = keep.tile([P, H // LIST_ROWS], U16, name="offsets")
-        def load_at(name, rows, parts, offset):
-            raw = shared.tile([P, PACK, rows.shape[1]], F32, name=name, offset=offset, align_bytes=ALIGN)
-            dealt = rows.rearrange("(p j) c -> p j c", j=PACK)
-            for queue, j0, j1 in parts:
-                queue.dma_start(out=raw[:, j0:j1], in_=dealt[:, j0:j1])
-            return raw
+        first_raw = load("first_raw", w1[0:KP, :], ((nc.sync, 0, PACK),))
+        x_raw = keep.tile([P, 2, PACK, T], F32, name="x_raw", align_bytes=ALIGN)
+        nc.sync.dma_start(out=x_raw[:], in_=xT.rearrange("(g p j) c -> p g j c", g=2, j=PACK))
+        wide_raw = load("wide_raw", w1[KP:K, 0:256])
+        third_raw = load("third_raw", w1[KP:K, 256:384])
+        last_raw = load("last_raw", w1[KP:K, 384:512], tag="h")
+        w2_raw = [load("w2_raw0", w2[:, 0:P], [(nc.sync, j, j + 1) for j in range(2)])]
+        w2_dealt = w2[:, 0:P].rearrange("(p j) c -> p j c", j=PACK)
+        for j in (2, 3):
+            for c0 in (0, 64):
+                nc.sync.dma_start(out=w2_raw[0][:, j, c0 : c0 + 64], in_=w2_dealt[:, j, c0 : c0 + 64])
+        nc.sync.dma_start(offsets[:], offs)
+        w2_raw.append(load("w2_raw1", w2[:, P:N], tag="third_raw"))
 
-        both = ((nc.sync, 0, 2), (nc.scalar, 2, PACK))
-        piece = PACK * P * 4
-        first_raw = load_at("first_raw", w1[0:KP, :], both, 0)
-        x_raw = [load("x_raw0", xT[0:KP, :]), load("x_raw1", xT[KP:K, :], ((nc.scalar, 0, PACK),))]
-        wide_raw = load("wide_raw", w1[KP:K, 0:256], both)
-        third_raw = load_at("third_raw", w1[KP:K, 256:384], both, 4 * piece)
         preload = keep.tile([P, 1], F32, name="preload")
         preload_out = keep.tile([P, 1], F32, name="preload_out")
-        nc.gpsimd.memset(preload[:], 0.0)
+        nc.vector.memset(preload[:], 0.0)
         nc.scalar.activation(preload_out[:], preload[:], GELU)
-
-        last_raw = load_at("last_raw", w1[KP:K, 384:512], both, 5 * piece)
-        nc.sync.dma_start(offsets[:], offs)
 
         identity_made = keep.tile([P, P], F32, name="identity_made", align_bytes=ALIGN)
         identity = keep.tile([P, P], F32, name="identity", align_bytes=ALIGN)
@@ -122,19 +119,17 @@ def tile_picked_shuffle_mlp_gelu_perm_l_kernel(tc, xT, w1, w2, offs, out):
         cast(vector_copy, first, first_raw, 160, 320)
         cast(scalar_copy, first, first_raw, 320, H)
 
-        w2_raw = [load_at("w2_raw0", w2[:, 0:P], ((nc.scalar, 0, PACK),), 0)]
 
         x0, x1 = staged("x0", T), staged("x1", T)
         wide = staged("wide", 2 * P)
         quantize(w1_q, 0, first, 0, P)
-        cast(vector_copy, x1, x_raw[1], 0, 96)
-        cast(scalar_copy, x1, x_raw[1], 96, T)
-        cast(scalar_copy, x0, x_raw[0], 0, T)
+        cast(vector_copy, x1, x_raw[:, 1], 0, 64)
+        cast(scalar_copy, x0, x_raw[:, 0], 0, T)
+        cast(scalar_copy, x1, x_raw[:, 1], 64, T)
         for c0 in (P, 3 * P, 2 * P):
             quantize(w1_q, 0, first, c0, c0 + P)
-        quantize(x_q[1], 0, x1, 0, T)
         quantize(x_q[0], 0, x0, 0, T)
-        w2_raw.append(load("w2_raw1", w2[:, P:N], tag="x_raw0"))
+        quantize(x_q[1], 0, x1, 0, T)
         cast(scalar_copy, wide, wide_raw, 0, 32)
         cast(vector_copy, wide, wide_raw, 32, 64)
         cast(vector_copy, wide, wide_raw, 64, P)
@@ -150,7 +145,8 @@ def tile_picked_shuffle_mlp_gelu_perm_l_kernel(tc, xT, w1, w2, offs, out):
 
         for index in range(len(GROUPS)):
             first_layer(0, index)
-        first_layer(1, 0)
+        for c0 in (0, P):
+            product(acc[0][:, c0 : c0 + P], x_q[1], slice(0, T), w1_q, slice(H + c0, H + c0 + P), False, c0 == P)
 
         third, last = staged("third", P), staged("last", P)
         cast(scalar_copy, third, third_raw, 0, 96)
@@ -172,7 +168,7 @@ def tile_picked_shuffle_mlp_gelu_perm_l_kernel(tc, xT, w1, w2, offs, out):
         cast(gpsimd_copy, w2_early, w2_raw[0], 0, P)
         quantize(w2_q, 0, w2_early, 0, P)
 
-        h = shared.tile([P, H], BF16, name="h", offset=5 * piece, align_bytes=ALIGN)
+        h = keep.tile([P, H], BF16, name="h", tag="h", align_bytes=ALIGN)
         for index, (c0, width) in enumerate(GROUPS):
             nc.scalar.activation(h[:, c0 : c0 + width], acc[index][:, 0:width], GELU)
 
@@ -183,7 +179,7 @@ def tile_picked_shuffle_mlp_gelu_perm_l_kernel(tc, xT, w1, w2, offs, out):
         )
         nc.scalar.activation(gathered[:, 0:split], h[:].indirect(offsets[:, 0:SCALAR_LIST_COLUMNS]), COPY)
 
-        w2_late = shared.tile([P, P * PACK], BF16, name="w2_late", offset=5 * piece, align_bytes=ALIGN)
+        w2_late = staged("w2_late", P)
         cast(scalar_copy, w2_late, w2_raw[1], 0, 64)
         cast(vector_copy, w2_late, w2_raw[1], 64, P)
         quantize(w2_q, P, w2_late, 0, 64)

from contextlib import ExitStack

import concourse.mybir as mybir
from concourse.masks import make_identity

K, T, H, N = 1024, 128, 512, 256
FLOPS = 2 * K * T * H + 2 * H * T * N

F32 = mybir.dt.float32
BF16 = mybir.dt.bfloat16
U32 = mybir.dt.uint32
U16 = mybir.dt.uint16
U8 = mybir.dt.uint8
FP8X4 = mybir.dt.float8_e4m3fn_x4
GELU = mybir.ActivationFunctionType.Gelu_apprx_tanh
COPY = mybir.ActivationFunctionType.Copy
MULT = mybir.AluOpType.mult
ADD = mybir.AluOpType.add

P = 128
PACK = 4
KP = P * PACK
BANK = 512
LIST_ROWS = 16
ALIGN = 512
GROUPS = ((0, 256), (256, 128), (384, 128))
SCALAR_LIST_COLUMNS = 16


def tile_picked_shuffle_mlp_gelu_perm_l_kernel(tc, xT, w1, w2, offs, out):
    nc = tc.nc

    def vector_copy(dst, src):
        nc.vector.tensor_copy(out=dst, in_=src)

    def scalar_copy(dst, src):
        nc.scalar.copy(dst, src)

    def gpsimd_copy(dst, src):
        nc.gpsimd.tensor_scalar(out=dst, in0=src, scalar1=1.0, scalar2=0.0, op0=MULT, op1=ADD)

    def cast(copy, grouped, raw, c0, c1):
        copy(
            grouped[:, PACK * c0 : PACK * c1].rearrange("p (c i j) -> p c j i", i=2, j=PACK),
            raw[:, :, c0:c1].rearrange("p j (c i) -> p c j i", i=2),
        )

    def quantize(operand, first, grouped, c0, c1):
        codes, scales = operand
        columns = slice(first + c0, first + c1)
        nc.vector.quantize_mx(
            out=codes[:, columns].bitcast(FP8X4), scales=scales[:, columns], in_=grouped[:, PACK * c0 : PACK * c1]
        )

    def product(acc, stationary, stationary_columns, moving, moving_columns, start, stop):
        nc.tensor.matmul_mx(
            out=acc,
            lhsT=stationary[0][:, stationary_columns].bitcast(FP8X4),
            lhsT_scale=stationary[1][:, stationary_columns],
            rhs=moving[0][:, moving_columns].bitcast(FP8X4),
            rhs_scale=moving[1][:, moving_columns],
            start=start,
            stop=stop,
        )

    with ExitStack() as ctx:
        keep = ctx.enter_context(tc.tile_pool(name="keep", bufs=1))
        psum = ctx.enter_context(tc.psum_pool(name="psum", bufs=1))

        def load(name, rows, parts=((nc.sync, 0, PACK),), tag=None):
            raw = keep.tile([P, PACK, rows.shape[1]], F32, name=name, tag=tag or name, align_bytes=ALIGN)
            dealt = rows.rearrange("(p j) c -> p j c", j=PACK)
            for queue, j0, j1 in parts:
                queue.dma_start(out=raw[:, j0:j1], in_=dealt[:, j0:j1])
            return raw

        def staged(name, columns, tag=None):
            return keep.tile([P, columns * PACK], BF16, name=name, tag=tag or name, align_bytes=ALIGN)

        def quantised(name, columns):
            codes = keep.tile([P, columns], U32, name=name + "_codes", align_bytes=ALIGN)
            scales = keep.tile([P, columns], U8, name=name + "_scales", align_bytes=ALIGN)
            return codes, scales

        offsets = keep.tile([P, H // LIST_ROWS], U16, name="offsets")
        first_raw = load("first_raw", w1[0:KP, :], ((nc.sync, 0, PACK),))
        x_raw = keep.tile([P, 2, PACK, T], F32, name="x_raw", align_bytes=ALIGN)
        nc.sync.dma_start(out=x_raw[:], in_=xT.rearrange("(g p j) c -> p g j c", g=2, j=PACK))
        wide_raw = load("wide_raw", w1[KP:K, 0:256])
        third_raw = load("third_raw", w1[KP:K, 256:384])
        last_raw = load("last_raw", w1[KP:K, 384:512], tag="h")
        w2_raw = [load("w2_raw0", w2[:, 0:P], [(nc.sync, j, j + 1) for j in range(2)])]
        w2_dealt = w2[:, 0:P].rearrange("(p j) c -> p j c", j=PACK)
        for j in (2, 3):
            for c0 in (0, 64):
                nc.sync.dma_start(out=w2_raw[0][:, j, c0 : c0 + 64], in_=w2_dealt[:, j, c0 : c0 + 64])
        nc.sync.dma_start(offsets[:], offs)
        w2_raw.append(load("w2_raw1", w2[:, P:N], tag="third_raw"))

        preload = keep.tile([P, 1], F32, name="preload")
        preload_out = keep.tile([P, 1], F32, name="preload_out")
        nc.vector.memset(preload[:], 0.0)
        nc.scalar.activation(preload_out[:], preload[:], GELU)

        identity_made = keep.tile([P, P], F32, name="identity_made", align_bytes=ALIGN)
        identity = keep.tile([P, P], F32, name="identity", align_bytes=ALIGN)
        make_identity(nc, identity_made[:])
        vector_copy(identity[:], identity_made[:])


        banks = [psum.tile([P, BANK], F32, name="bank%d" % b) for b in range(8)]
        acc, turned, out_banks = banks[0:3], banks[3], banks[4:7]

        w1_q = quantised("w1", 2 * H)
        x_q = [quantised("x0", T), quantised("x1", T)]

        first = staged("first", H)
        cast(vector_copy, first, first_raw, 0, 160)
        cast(vector_copy, first, first_raw, 160, 320)
        cast(scalar_copy, first, first_raw, 320, H)


        x0, x1 = staged("x0", T), staged("x1", T)
        wide = staged("wide", 2 * P)
        quantize(w1_q, 0, first, 0, P)
        cast(vector_copy, x1, x_raw[:, 1], 0, 64)
        cast(scalar_copy, x0, x_raw[:, 0], 0, T)
        cast(scalar_copy, x1, x_raw[:, 1], 64, T)
        for c0 in (P, 3 * P, 2 * P):
            quantize(w1_q, 0, first, c0, c0 + P)
        quantize(x_q[0], 0, x0, 0, T)
        quantize(x_q[1], 0, x1, 0, T)
        cast(scalar_copy, wide, wide_raw, 0, 32)
        cast(vector_copy, wide, wide_raw, 32, 64)
        cast(vector_copy, wide, wide_raw, 64, P)
        cast(vector_copy, wide, wide_raw, P, 176)
        cast(scalar_copy, wide, wide_raw, 176, 2 * P)
        for c0, c1 in ((0, 64), (64, P), (P, 2 * P)):
            quantize(w1_q, H, wide, c0, c1)

        def first_layer(g, index):
            c0, width = GROUPS[index]
            channels = slice(g * H + c0, g * H + c0 + width)
            product(acc[index][:, 0:width], x_q[g], slice(0, T), w1_q, channels, g == 0, g == 1)

        for index in range(len(GROUPS)):
            first_layer(0, index)
        for c0 in (0, P):
            product(acc[0][:, c0 : c0 + P], x_q[1], slice(0, T), w1_q, slice(H + c0, H + c0 + P), False, c0 == P)

        third, last = staged("third", P), staged("last", P)
        cast(scalar_copy, third, third_raw, 0, 96)
        cast(vector_copy, third, third_raw, 96, P)
        cast(vector_copy, last, last_raw, 0, 32)
        cast(scalar_copy, last, last_raw, 96, P)
        cast(scalar_copy, last, last_raw, 72, 96)
        cast(vector_copy, last, last_raw, 32, 72)
        quantize(w1_q, H + 256, third, 0, 64)
        quantize(w1_q, H + 256, third, 64, P)
        first_layer(1, 1)
        for c0 in (0, 96, 32, 64):
            quantize(w1_q, H + 384, last, c0, c0 + 32)
        first_layer(1, 2)

        w2_q = quantised("w2", N)

        w2_early = staged("w2_early", P, tag="last")
        cast(gpsimd_copy, w2_early, w2_raw[0], 0, P)
        quantize(w2_q, 0, w2_early, 0, P)

        h = keep.tile([P, H], BF16, name="h", tag="h", align_bytes=ALIGN)
        for index, (c0, width) in enumerate(GROUPS):
            nc.scalar.activation(h[:, c0 : c0 + width], acc[index][:, 0:width], GELU)

        gathered = keep.tile([P, H], BF16, name="gathered", align_bytes=ALIGN)
        split = LIST_ROWS * SCALAR_LIST_COLUMNS
        nc.vector.tensor_copy(
            out=gathered[:, split:H], in_=h[:].indirect(offsets[:, SCALAR_LIST_COLUMNS : H // LIST_ROWS])
        )
        nc.scalar.activation(gathered[:, 0:split], h[:].indirect(offsets[:, 0:SCALAR_LIST_COLUMNS]), COPY)

        w2_late = staged("w2_late", P)
        cast(scalar_copy, w2_late, w2_raw[1], 0, 64)
        cast(vector_copy, w2_late, w2_raw[1], 64, P)
        quantize(w2_q, P, w2_late, 0, 64)
        quantize(w2_q, P, w2_late, 64, P)

        words = gathered[:].bitcast(F32)
        for u in range(2):
            nc.tensor.transpose(turned[:, u * P : (u + 1) * P], words[:, u : 2 * P : 2], identity[:])

        h_q = quantised("h", T)
        turned_pairs = turned[:, 0 : 2 * P].rearrange("p (u c i) -> p c u i", u=2, i=2)
        halves = (slice(0, T // 2), slice(T // 2, T))
        for part, tokens in enumerate(slice(t, t + 32) for t in range(0, T, 32)):
            width = tokens.stop - tokens.start
            grouped = staged("h_grouped%d" % part, width)
            scalar_copy(
                grouped[:].bitcast(F32).rearrange("p (c i u) -> p c u i", i=2, u=2),
                turned_pairs[:, tokens.start // 2 : tokens.stop // 2],
            )
            quantize(h_q, tokens.start, grouped, 0, width)

        y = [keep.tile([P, T], F32, name="y%d" % m, align_bytes=ALIGN) for m in range(N // P)]
        steps = (
            (0, halves[0], scalar_copy, nc.scalar),
            (1, slice(0, T), vector_copy, nc.sync),
            (0, halves[1], scalar_copy, nc.scalar),
        )
        for bank, (m, tokens, copy, queue) in zip(out_banks, steps):
            width = tokens.stop - tokens.start
            product(bank[:, 0:width], w2_q, slice(P * m, P * (m + 1)), h_q, tokens, True, True)
            copy(y[m][:, tokens], bank[:, 0:width])
            queue.dma_start(out=out[P * m : P * (m + 1), tokens], in_=y[m][:, tokens])
